import numpy as np, ml_dtypes
CORES = [24,25,26,27,28,29,30,31]
N = 8
import mx_ref
BF = ml_dtypes.bfloat16
def entries(a):
    return np.ascontiguousarray(a.T).reshape(-1)
def table(e):
    return np.ascontiguousarray(np.reshape(e, (-1, 16)).T).astype(np.int32)
def gcols(t, e):
    v = np.concatenate([t.reshape(8, 16, -1, 4), np.zeros((8, 16, 1, 4), BF)], axis=2)
    return np.ascontiguousarray(np.stack([v[g][:, e[g]] for g in range(8)])).reshape(128, -1)
def tile(rs):
    return np.stack(rs, axis=2).reshape(128, -1).astype(BF)
def pick(q, e):
    c = np.concatenate([q[0].reshape(128, -1, 4), np.zeros((128, 1, 4), np.uint8)], axis=1); s = np.concatenate([q[1], np.ones((16, 1), np.uint8)], axis=1)
    return (np.ascontiguousarray(c[:, e].reshape(128, -1)), np.ascontiguousarray(s[:, e]))
def join(*qs):
    return (np.concatenate([q[0] for q in qs], axis=1), np.concatenate([q[1] for q in qs], axis=1))
def put(q, e, v):
    c, s = q[0].reshape(128, -1, 4).copy(), q[1].copy(); c[:, e] = v[0].reshape(128, -1, 4); s[:, e] = v[1]
    return (c.reshape(128, -1), s)
def pk(c, s):
    return (np.ascontiguousarray(c), mx_ref.live(s))
def emit(q):
    return q[0], q[1]
def packed(v, rng):
    q = [mx_ref.quantize(np.ascontiguousarray(v[r])) for r in range(N)]
    return np.stack([a for a, b in q]), np.stack([mx_ref.plane(b, rng) for a, b in q])
def values_of_codes():
    e, c = np.zeros((128, 128, 4), np.float32), np.zeros((128, 2, 4), np.uint8)
    e[np.arange(128), np.arange(128), 0] = 1
    c[:127, :, 0] = np.arange(256).reshape(2, 128).T[:127]
    return mx_ref.matmul(mx_ref.quantize(e.reshape(128, 512).astype(BF)), (c.reshape(128, 8), np.full((16, 2), 127, np.uint8))).T.reshape(-1).astype(np.float64)
CODE_VALUE, SCALE_VALUE = values_of_codes(), 2.0 ** (np.arange(256) - 127.0)
def decode(q):
    return (CODE_VALUE[q[0]].reshape(16, 8, -1, 4) * SCALE_VALUE[q[1]][:, None, :, None] + 0.0).reshape(128, -1).astype(np.float32)
def f(rng, *shape):
    return mx_ref.flush((rng.standard_normal(shape, dtype=np.float32) * np.exp2(rng.integers(-2, 3, shape[:-1] + (1,)))).astype(BF))
def wide(rng, *shape, cols=0):
    v = rng.standard_normal(shape, dtype=np.float32) * np.exp2(rng.integers(-12, 13, shape)).astype(np.float32)
    if cols: v *= np.repeat(np.exp2(rng.integers(-cols, cols + 1, shape[:-2] + (1, shape[-1] // 4))) * (rng.random(shape[:-2] + (1, shape[-1] // 4)) > 0.0625), 4, axis=-1).astype(np.float32)
    return mx_ref.flush(v.astype(BF))
C, K = 320, 128
PARTNER = [1, 2, 4]
LOCAL = np.arange(C) % 32
ROOT = np.arange(C) - LOCAL
PLACE = np.arange(32)
def big(v):
    v = v.astype(np.float32)
    v[np.abs(v) < np.float32(2.0 ** -16)] = 0
    return v.astype(BF)
def numbers_of(rng):
    return {"x": big(f(rng, N, 128, 4 * C)), "u": np.array(f(rng, N, 128, 512)), "v": np.array(f(rng, N, 128, 512))}
def parents(rng):
    return {k: np.stack([table(ROOT + rng.integers(0, np.maximum(LOCAL, 1), C)) for r in range(N)]) for k in ("p0", "p1")}
def weights(rng, still=[]):
    w = np.array(big(f(rng, N, 128, 2048))).reshape(N, 128, 4, 128, 4)
    for i in still:
        w[:, i] = 0
        w[:, :, :, i] = 0
    c, p = packed(w.reshape(N, 128, 2048), rng)
    return {"wc": c, "ws": p}
def setup_inputs(rng):
    return {**numbers_of(rng), **parents(rng), **weights(rng)}
def setup_inputs_ties(rng):
    d = numbers_of(rng)
    x = d["x"].reshape(N, 128, C, 4)
    x[:, ::64] = 0
    x[:, ::64, :, 0] = rng.integers(0, 3, (N, 2, C)).astype(np.float32).astype(BF)
    u = d["u"].reshape(N, 128, 128, 4)
    u[:, :, ::64] = 0
    o = rng.permutation(N)
    for r in range(N):
        for h in (0, 64): u[r, h, h, 0] = 0.0 if r == o[0] else -1.0 if r == o[1] else 1.0
    return {"x": x.reshape(N, 128, 4 * C), "u": u.reshape(N, 128, 512), "v": d["v"], **parents(rng), **weights(rng, [0, 64])}
def setup_inputs_near(rng):
    d = numbers_of(rng)
    x = d["x"].astype(np.float32).reshape(N, 128, C, 4)
    u = d["u"].reshape(N, 128, 128, 4)
    u[:, :, ::64] = 0
    o = rng.permutation(N) % 4
    for r in range(N):
        k = 2.0 ** -30 if o[r] > 0 else 1.0
        for h in (0, 64):
            x[r, h:h + 16] = 0
            sign = np.repeat(rng.permutation(C // 32) % 2 * 2.0 - 1.0, 32)
            far = 32 * np.arange(C // 32) + rng.integers(0, 32, C // 32)
            s = rng.integers(0, 16, C)
            if o[r] < 3:
                x[r, h + 8] = ((s[:, None] >> np.arange(4)) & 1) * np.exp2(np.arange(4) - 23.0)
                u[r, h + 8, h] = k
            if o[r] < 2:
                x[r, h, :, 0] = sign
                x[r, h + 11, :, 0] = 2.0 ** -10
                u[r, h, h, 0] = k
                u[r, h + 11, h, 0] = k
            if o[r] == 2:
                x[r, h, far, 0] = sign[far] * 2.0 ** 29
                u[r, h, h, 0] = 1.0
            if o[r] == 3:
                odd = np.arange(C) // 32 % 2
                j = rng.integers(0, 3, C)
                x[r, h + 10, :, 0] = (1 - odd) * np.array([1.0, 0.0, 1.125])[j] * 2.0 ** -29
                x[r, h + 12, :, 0] = (1 - odd) * (j == 1) * 2.0 ** -29
                u[r, h + 10, h, 0] = 1.125 * k
                u[r, h + 12, h, 0] = 1.25 * k
                x[r, h, :, 0] = odd * 1.96875
                x[r, h + 1, :, 0] = odd * rng.integers(3, 5, C) * np.exp2(np.arange(C) // 64 % 4 - 16.0)
                u[r, h + 1, h, 0] = k
    still = [h + i for h in (0, 64) for i in range(16)]
    return {"x": x.reshape(N, 128, 4 * C).astype(BF), "u": u.reshape(N, 128, 512), "v": d["v"], **parents(rng), **weights(rng, still)}
def setup_inputs_huge(rng):
    d = numbers_of(rng)
    o = rng.permutation(N) % 2
    x = (0.5 + 0.12 * rng.random((N, 128, C, 4))) * 2.0 ** 30
    for r in range(N):
        if o[r] == 0: c = np.repeat(rng.permutation(C // 32) % 2 * 2.0 - 1.0, 32)
        else: c = rng.permutation(C) % 2 * 2.0 - 1.0
        x[r] *= c[None, :, None]
    u = d["u"].reshape(N, 128, 128, 4)
    a = 2.0 ** 30 * (1.0 - 0.1 * rng.random((N, 128, 2, 4))) * rng.choice([-1.0, 1.0], (N, 1, 2, 1))
    u[:, :, ::64] = a.astype(np.float32).astype(BF)
    w = np.zeros((N, 128, 4, 128, 4), np.float32)
    i = np.arange(128)
    for b in range(4): w[:, i, b, i, b] = -2
    c, p = packed(w.reshape(N, 128, 2048).astype(BF), rng)
    return {"x": x.astype(np.float32).reshape(N, 128, 4 * C).astype(BF), "u": u.reshape(N, 128, 512), "v": d["v"], **parents(rng), "wc": c, "ws": p}
def setup_inputs_late(rng):
    d = numbers_of(rng)
    x = d["x"].astype(np.float32).reshape(N, 8, 16, C, 4)
    odd = 1.0 + (2.0 * rng.integers(0, 64, (N, 8, 8, C, 4)) + 1.0) * 2.0 ** -7
    x[:, :, 8:] = odd * np.exp2(rng.integers(-14, -7, (N, 8, 8, C, 4))) * rng.choice([-1.0, 1.0], (N, 8, 8, C, 4))
    x[:, :, 8, :, 0] = 1.96875 * rng.choice([-1.0, 1.0], (N, 8, C))
    x[:, ::4, 0] = 0
    u = d["u"].reshape(N, 128, 128, 4)
    u[:, :, ::64] = 0
    for h in (0, 64): u[:, h, h, 0] = 1.0
    before = np.maximum(LOCAL - 1, 0)
    a, b = [], []
    for r in range(N):
        k = np.repeat(rng.permutation(C // 32) % 4, 32)
        a.append(table(ROOT + np.where(k == 1, 0, np.where(k == 3, before // 2, before))))
        b.append(table(ROOT + np.where((k == 1) | (k == 2), 0, before)))
    return {"x": x.reshape(N, 128, 4 * C).astype(BF), "u": u.reshape(N, 128, 512), "v": d["v"], "p0": np.stack(a), "p1": np.stack(b), **weights(rng)}
def setup_inputs_spread(rng):
    d = setup_inputs(rng)
    d["x"] = big(wide(rng, N, 128, 4 * C, cols=6))
    return d
def check_inputs(d):
    b = []
    for k in ("x", "u", "v"):
        a = np.abs(d[k].astype(np.float32))
        if not (np.isfinite(a).all() and ((a == 0) | (a >= 2.0 ** -30) & (a <= 2.0 ** 30)).all()): b.append("a value of " + k)
    none, least, most = [emit(mx_ref.quantize(np.full((128, 16), k, np.float32).astype(BF)))[1][0, 0] for k in (0.0, 2.0 ** -30, 2.0 ** 30)]
    for r in range(N):
        for k in ("p0", "p1"):
            e = entries(d[k][r])
            if not ((e >= ROOT) & (e < ROOT + np.maximum(LOCAL, 1))).all(): b.append("an entry of " + k)
        if ((d["wc"][r] == 0x7F) | (d["wc"][r] == 0xFF)).any(): b.append("wc: a code that is no number")
        s = mx_ref.live(d["ws"][r])
        if ((s != none) & ((s < least) | (s > most))).any(): b.append("ws: a scale out of range")
    return b
def split(s, a, b):
    a, b = np.stack([a, a], axis=1), np.stack([b, b], axis=1)
    up = np.where(np.take_along_axis(s, a, axis=2) >= np.take_along_axis(s, b, axis=2), a, b).reshape(-1, 32) % 32
    n = len(up)
    above = np.zeros((n, 32, 32), bool)
    for j in range(32):
        if j > 0: above[:, :, j] = above[np.arange(n), :, up[:, j]]
        above[:, j, j] = True
    left, top = np.ones((n, 32), bool), np.zeros((n, 32), np.int64)
    c, w = [], []
    for l in range(4):
        one = (top[:, :, None] == top[:, None]) & left[:, :, None] & left[:, None]
        size = np.sum(above & one, axis=2)
        half = 2 * size >= np.sum(one, axis=2)
        best = np.max(np.where(one & half[:, None], PLACE, -1), axis=2)
        c.append(np.where(left, best, PLACE))
        w.append(size)
        left = left & (best != PLACE)
        cut = ~np.take_along_axis(left, up, axis=1)
        cut[:, 0] = True
        top = np.max(np.where(above & cut[:, :, None], PLACE[:, None], 0), axis=1)
    c, w = [np.stack(k, axis=1).reshape(N, 2, -1, 4, 32).transpose(0, 1, 3, 2, 4).reshape(N, 8, C) for k in (c, w)]
    return c + ROOT, np.argsort(-w, axis=2, kind="stable")
def reference(x, u, v, p0, p1, wc, ws):
    qu = [mx_ref.quantize(u[r]) for r in range(N)]
    lay = [pk(wc[r], ws[r]) for r in range(N)]
    a, b = np.stack([entries(p0[r]) for r in range(N)]), np.stack([entries(p1[r]) for r in range(N)])
    now = [x[r] for r in range(N)]
    for m in PARTNER:
        q = [mx_ref.quantize(now[r]) for r in range(N)]
        own = [decode(q[r]) for r in range(N)]
        s = np.stack([mx_ref.matmul(qu[r], q[r])[::64] for r in range(N)]) + np.float32(0.0)
        c, o = split(s, a, b)
        mosaic = [gcols(own[r].astype(BF), c[r]) for r in range(N)]
        sent = [mx_ref.quantize(gcols(mosaic[r], o[r][:, :K])) for r in range(N)]
        for r in range(N):
            e = np.argsort(o[r], axis=1)
            e = np.where(e < K, e, K + np.arange(C))
            mate = gcols(np.concatenate([decode(sent[r ^ m]).astype(BF), mosaic[r]], axis=1), e).astype(np.float32)
            z = mx_ref.quantize(((mosaic[r].astype(np.float32) + mate) * np.float32(0.5)).astype(BF))
            now[r] = tile([mx_ref.matmul(pick(lay[r], np.arange(128 * k, 128 * k + 128)), z) * np.float32(0.03125) + own[r][:, k::4] for k in range(4)])
    y, cl = np.zeros((N, 128, C), np.float32), np.zeros((N, 8, C), np.float32)
    oc, osc = np.zeros((N, 128, 4 * C), np.uint8), np.zeros((N, 16, C), np.uint8)
    for r in range(N):
        q = mx_ref.quantize(now[r])
        y[r] = mx_ref.matmul(mx_ref.quantize(v[r]), q)
        cl[r] = c[r]
        oc[r], osc[r] = emit(q)
    return {"y": y, "cl": cl, "oc": oc, "osc": osc}

@@ -1,0 +1,461 @@
+from concourse.mybir import dt, AluOpType, ActivationFunctionType
+A = AluOpType
+F = ActivationFunctionType
+BF, F32, F16, U16, I32, X4, U8 = "bfloat16", "float32", "float16", "uint16", "int32", "float8_e4m3fn_x4", "uint8"
+PARTNER = [1, 2, 4]
+_S = {
+    "xt": (1280, BF), "ut": (512, BF), "vt": (512, BF), "ct": (2048, BF), "tt": (1280, BF), "zt": (1280, BF),
+    "qx": (320, X4), "sx": (320, U8), "qu": (128, X4), "su": (128, U8), "qu2": (128, X4), "su2": (128, U8),
+    "qv": (128, X4), "sv": (128, U8), "qw": (512, X4), "sw": (512, U8), "qc": (512, X4), "sc": (512, U8),
+    "qz": (320, X4), "sz": (320, U8),
+    "idn": (128, F32), "zw": (1792, BF), "gw": (1280, BF), "he": (512, BF), "yo": (320, F32),
+    "pt": (48, I32), "ci": (8, I32), "cf": (40, F32), "tab": (80, F32), "iw": (320, F32), "ni": (176, I32),
+    "offu": (8, U16), "offp": (36, U16), "offd": (12, U16), "offa": (10, U16), "offm": (20, U16), "offc": (20, U16),
+    "offq": (4, U16), "offw": (2, U16), "offs": (20, U16), "offz": (20, U16),
+    "ss": (320, F32), "sb": (176, F32), "d0": (352, BF), "d1": (352, BF), "x0": (384, BF), "xa": (192, BF), "xb": (192, BF),
+    "xc": (176, BF), "t1": (192, BF), "t2": (160, BF), "r0": (176, F32), "r1": (176, F32), "n0": (176, F32),
+    "ap": (160, BF), "art": (160, BF), "ar": (160, BF), "r32": (160, BF), "seg": (160, BF), "ones": (320, BF), "dn": (160, BF),
+    "cnt": (160, BF), "yy": (160, BF), "yt": (160, BF), "keep": (160, BF), "nu": (160, BF), "rr": (160, BF),
+    "dy": (160, BF), "dyt": (640, BF), "kk": (160, BF), "z0": (640, BF), "rho": (640, BF),
+    "y2": (640, BF), "y2t": (640, BF), "k3": (640, BF), "xs": (640, BF),
+    "bt": (48, F32), "sig": (20, F32), "sm": (160, F32), "smb": (96, BF),
+    "swn": (40, F32), "cw": (48, F32), "mm": (320, BF), "rs": (320, BF), "sg": (320, BF), "acc": (8, F32),
+    "i2": (320, BF), "ng": (320, BF), "ngt": (320, BF), "pp": (320, F16), "ppt": (320, F16), "ps": (320, F16),
+    "m2": (320, BF), "rc": (320, BF), "rcf": (320, F32), "kq": (48, F32), "tq": (48, F32), "wi": (48, F32), "wz": (48, F32),
+    "w1": (128, F32), "w2": (64, F32), "w3": (64, F32), "cq": (48, F32), "zq": (96, F32),
+    "lw": (640, BF), "lt": (256, BF), "ls": (8, F32),
+}
+for _t in range(3):
+    _S["qt%d" % _t] = (320, X4)
+    _S["st%d" % _t] = (320, U8)
+    _S["ql%d" % _t] = (320, X4)
+    _S["sl%d" % _t] = (320, U8)
+    _S["lo%d" % _t] = (8, U16)
+    _S["li%d" % _t] = (8, U16)
+SCRATCH = {k: ("sbuf", [128, n], d) for k, (n, d) in _S.items()}
+SCRATCH["pa"] = ("psum", [128, 2048], F32)
+SCRATCH["pb"] = ("psum", [128, 2048], F32)
+SEMAPHORES = ["v", "a", "pe", "gp"] + ["m%d" % i for i in range(32)] + ["%s%d" % (n, t) for n in ("rq", "rs", "rl", "oq", "os", "ol") for t in range(3)]
+BIG = 2.0 ** 40
+CY, WAKE, FAR = 0.001, 0.07, 2.2
+ZV, XV = (3, 7), (3, 7)
+
+
+def rank_program(g, core, T, topo):
+    rank = T.rank_of(core)
+    if rank is None:
+        return
+    Q = {"v": g.vector, "a": g.scalar, "pe": g.tensor, "gp": g, "sy": g.sync}
+    nodes, hist, pool = [], {}, [0]
+
+    def R(name, a=None, b=None, s=1, p=(0, 128)):
+        if a is None:
+            a, b = 0, T[name].shape[1]
+        ap = T[name][p[0]:p[1], a:b:s] if s > 1 else T[name][p[0]:p[1], a:b]
+        n = (b - a + s - 1) // s
+        if name in ("pa", "pb"):
+            return (ap, [(name, 0, 128, a // 512 * 512, a // 512 * 512 + 512, 1)], n, False, False)
+        return (ap, [(name, p[0], p[1], a, b, s)], n, _S[name][1] in (BF, F16, U16), False)
+
+    def ind(w, o, cast=None):
+        ap = w[0] if cast is None else w[0].bitcast(cast)
+        return (ap.indirect(o[0]), w[1] + o[1], 16 * o[2], False, True)
+
+    def meet(x, y):
+        if x[2] <= y[1] or y[2] <= x[1] or x[4] <= y[3] or y[4] <= x[3]:
+            return False
+        return not (x[5] == y[5] and x[5] > 1 and (x[3] - y[3]) % x[5])
+
+    def node(q, reads, writes, emit, cost, lat=0.0, ev=None, free=False, after=()):
+        me, deps, soft = len(nodes), set(after), set()
+        for regs, wr in ((reads, False), (writes, True)):
+            for x in regs:
+                psum = x[0] in ("pa", "pb")
+                for (y, w2, k) in hist.get(x[0], []):
+                    if meet(x, y) and (wr or w2 or (psum and nodes[k]["q"] != q)):
+                        (soft if free and psum and nodes[k]["q"] == q else deps).add(k)
+        for x in writes:
+            hist[x[0]] = [z for z in hist.get(x[0], []) if not (x[5] == 1 and x[1] <= z[0][1] and z[0][2] <= x[2] and x[3] <= z[0][3] and z[0][4] <= x[4])]
+            hist[x[0]].append((x, True, me))
+        for x in reads:
+            hist.setdefault(x[0], []).append((x, False, me))
+        nodes.append({"q": q, "deps": deps, "all": deps | soft, "emit": emit, "cost": cost, "lat": lat, "ev": ev})
+        return me
+
+    def op(q, fn, outs, cost, *args, free=False, **kw):
+        reads, writes = [], []
+        for i, x in enumerate(args):
+            if isinstance(x, tuple):
+                if i < outs:
+                    writes.extend(x[1][:1])
+                    reads.extend(x[1][1:])
+                else:
+                    reads.extend(x[1])
+        for k in kw:
+            if isinstance(kw[k], tuple):
+                (writes if k == "accum_out" else reads).extend(kw[k][1])
+        a2 = [x[0] if isinstance(x, tuple) else x for x in args]
+        k2 = {k: (x[0] if isinstance(x, tuple) else x) for k, x in kw.items()}
+        node(q, reads, writes, lambda: fn(*a2, **k2).then_inc(T.sem[q], 1), cost, free=free)
+
+    V, S = g.vector, g.scalar
+
+    def cc(o, *ins):
+        if ins[0][4]:
+            return 0.06 + 1.6 * CY * ins[0][2]
+        if o[4]:
+            return 0.06 + 3.8 * CY * o[2]
+        return CY * max(64, o[2] * (0.5 if o[3] and all(i[3] for i in ins) else 1))
+
+    def cp(o, i): op("v", V.tensor_copy, 1, cc(o, i), o, i)
+    def tt(o, a, b, f): op("v", V.tensor_tensor, 1, CY * max(64, 2 * o[2]), o, a, b, f)
+    def tr(o, i): op("v", V.transpose, 1, cc(o, i), o, i)
+    def ms(o, c): op("v", V.memset, 1, cc(o, o), o, c)
+    def sc(o, a, b, i, f0, f1): op("v", V.tensor_tensor_scan, 1, cc(o, a, b), o, a, b, i, f0, f1)
+    def qz(c, s, i): op("v", V.quantize_mx, 2, 0.015 + 0.0011 * c[2], c, s, i)
+    def act(o, i, f, **kw): op("a", S.activation, 1, cc(o, i) if i[4] else CY * max(64, o[2]), o, i, f, **kw)
+    def lin(o, i, m, c): act(o, i, F.Identity, scale=m, bias=c)
+    def iota(o, pat, base, cm): op("gp", g.iota, 1, 0.13 + 2 * CY * o[2], o, pat, base, cm, allow_small_or_imprecise_dtypes=True)
+    def mm(o, w, ws, x, xs, start=True, stop=True): op("pe", g.tensor.matmul_mx, 1, 0.0006 * (o[2] + 16), o, w, ws, x, xs, start, stop, free=not start)
+
+    def ts(o, i, s1, f0, s2=None, f1=None):
+        if f1 is None:
+            op("v", V.tensor_scalar, 1, cc(o, i), o, i, s1, None, f0)
+        else:
+            op("v", V.tensor_scalar, 1, cc(o, i), o, i, s1, s2, f0, f1)
+
+    def dma(q, o, i, lat=2.0):
+        ev = ("m%d" % pool[0], 16)
+        pool[0] += 1
+        node(q, i[1], o[1], lambda: Q[q].dma_start(o[0], i[0]).then_inc(T.sem[ev[0]], 16), 0.1, lat, ev)
+
+    def send(dst, o, i, rs, ls, lat, codes=False):
+        rid, pid, _ = topo.addr(dst)
+        a, b = (o[0].bitcast(dt.uint8), i[0].bitcast(dt.uint8)) if codes else (o[0], i[0])
+        k = node("gp", i[1], [], lambda: g.remote_dma(a, b, T.sem[rs], T.sem[ls], pid, rid, topo.mask(core, dst)), 0.5, lat, (ls, len(topo.engines(core, dst))))
+        node("far", [], o[1], None, 0.0, 0.0, (rs, len(topo.engines(dst, core))), after=(k,))
+
+    def lay_out():
+        n = len(nodes)
+        tail, outs, left = [0.0] * n, [[] for _ in nodes], [len(x["all"]) for x in nodes]
+        for k in range(n - 1, -1, -1):
+            tail[k] += nodes[k]["cost"] + nodes[k]["lat"]
+            for d in nodes[k]["all"]:
+                tail[d] = max(tail[d], tail[k] + WAKE)
+                outs[d].append(k)
+        free, count, known, final = {}, {}, {q: {} for q in Q}, {}
+        ready, start = [k for k in range(n) if not left[k]], [0.0] * n
+        while ready:
+            k = min(ready, key=lambda i: (max(start[i], free.get(nodes[i]["q"], 0.0)), -tail[i], i))
+            q = nodes[k]["q"]
+            t0 = max(start[k], free.get(q, 0.0))
+            for i in ready:
+                if nodes[i]["q"] == q and tail[i] > tail[k] and start[i] < t0 + 0.6 * nodes[k]["cost"]:
+                    k = i
+            x = nodes[k]
+            ready.remove(k)
+            t1 = max(start[k], free.get(q, 0.0)) + x["cost"]
+            if q != "far":
+                free[q] = t1
+                need = {}
+                for d in x["deps"]:
+                    e = nodes[d]["ev"]
+                    need[e[0]] = max(need.get(e[0], 0), e[1])
+                for s in sorted(need):
+                    if known[q].get(s, 0) < need[s]:
+                        Q[q].wait_ge(T.sem[s], need[s])
+                        known[q][s] = need[s]
+                if x["ev"] is None:
+                    count[q] = count.get(q, 0) + 1
+                    x["ev"] = (q, count[q])
+                x["emit"]()
+            final[x["ev"][0]] = max(final.get(x["ev"][0], 0), x["ev"][1])
+            for i in outs[k]:
+                start[i] = max(start[i], t1 + x["lat"] + WAKE)
+                left[i] -= 1
+                if not left[i]:
+                    ready.append(i)
+        for s in sorted(final):
+            g.sync.wait_ge(T.sem[s], final[s])
+
+    def H(t): return (t, [])
+    def u8(x): return (x[0].bitcast(dt.uint8),) + x[1:]
+    def u32(x): return (x[0].bitcast(dt.uint32),) + x[1:]
+    def C(k): return R("cf", k, k + 1)
+    def quad(k): return (32 * k, 32 * k + 32)
+    (J, R16, SB, EB, E16, E33, NS, ROOT, NBIG, PBIG, J32, LW, PH, VV, VB, S20, N20, LE5, LO5, S10, NR,
+     T0, T1, T2, T3, T4, T5, T6, T7, T8, T9, TA, TB) = range(33)
+
+    dma("sy", R("xt", 0, 640), H(T.x[:, 0:640]), 3.0)
+    dma("a", R("xt", 640, 1280), H(T.x[:, 640:1280]), 3.0)
+    dma("sy", R("ut"), H(T.u[:]), 2.5)
+    ms(R("pt"), 0)
+    dma("a", R("pt", 1, 21, p=(0, 16)), H(T.p0[:]))
+    dma("sy", R("pt", 0, 20, p=(16, 32)), H(T.p0[:]))
+    dma("a", R("pt", 25, 45, p=(0, 16)), H(T.p1[:]))
+    dma("sy", R("pt", 24, 44, p=(16, 32)), H(T.p1[:]))
+    dma("sy", u8(R("qw")), H(T.wc[:]))
+    dma("sy", R("sw"), H(T.ws[:]))
+    dma("sy", R("vt"), H(T.v[:]))
+    iota(R("ci", 4, 5), [[0, 1]], 0, 1)
+    iota(R("idn"), [[1, 128]], 0, -1)
+    iota(R("iw"), [[1, 320]], 0, 0)
+    iota(R("tab", 0, 10), [[16, 10]], 0, 0)
+    iota(R("r32"), [[0, 5], [1, 32]], 0, 0)
+    iota(R("tab", 10, 30), [[0, 2], [1, 5], [0, 2]], 0, 0)
+    iota(R("tab", 30, 50), [[0, 2], [1, 5], [5, 2]], 0, 0)
+    iota(R("tab", 50, 70), [[0, 4], [32, 5]], -161, 0)
+    iota(R("tab", 70, 74), [[0, 2], [5, 2]], 0, 0)
+    for k, m in enumerate((31, 15, 32, 16)):
+        ts(R("ci", k, k + 1), R("ci", 4, 5), m, A.bitwise_and)
+    for b in range(4):
+        ms(R("ct", 512 * b, 512 * b + 512), 0.0)
+        ts(R("ct", 513 * b, 512 * b + 512, 4), R("idn"), 0.0, A.is_equal, 32.0, A.mult)
+        qz(R("qc", 128 * b, 128 * b + 128), R("sc", 128 * b, 128 * b + 128), R("ct", 512 * b, 512 * b + 512))
+    cp(R("cf", 0, 4), R("ci", 0, 4))
+    ms(R("offu", 0, 4), 0)
+    ms(R("offu", 4, 8), 64)
+    ms(R("x0", 352, 384), 0.0)
+    ms(R("xa", 176, 192), 0.0)
+    ms(R("xb", 176, 192), 0.0)
+    ms(R("d0", 0, 352, 2), 0.0)
+    ms(R("ones"), 1.0)
+    ms(R("dn"), -1.0 / 32)
+    lin(C(E16), C(EB), -1.0, 16.0)
+    lin(C(NS), C(SB), -5.0, 0.0)
+    ts(C(ROOT), C(J), 0.0, A.is_equal)
+    ts(C(NR), C(J), 0.0, A.not_equal)
+    lin(C(NBIG), C(NR), -BIG, 0.0)
+    lin(C(PBIG), C(NR), BIG, 0.0)
+    lin(C(J32), C(J), -1.0, 32.0)
+    ts(R("ni"), R("iw", 0, 176), C(E16), A.add)
+    lin(C(E33), C(E16), 2.0, 1.0)
+    ts(R("ni"), R("ni"), 31, A.bitwise_and)
+    ts(R("offa"), R("tab", 0, 10), C(R16), A.add, C(E16), A.add)
+    ts(R("n0"), R("ni"), C(J), A.not_equal, C(NR), A.mult)
+    ts(R("seg"), R("r32"), 0.0, A.not_equal)
+    qz(R("qu"), R("su"), R("ut"))
+    cp(u32(R("qu2")), ind(R("qu"), R("offu"), dt.uint32))
+    act(R("su2"), ind(R("su"), R("offu")), F.Copy)
+    for k in range(2):
+        qz(R("qx", 160 * k, 160 * k + 160), R("sx", 160 * k, 160 * k + 160), R("xt", 640 * k, 640 * k + 640))
+    for k in range(4):
+        cp(R("offp", 0, 35, p=quad(k)), R("pt", 10 * (k % 2), 10 * (k % 2) + 35, p=quad(0)))
+    O0, O1 = R("offp", 0, 11), R("offp", 24, 35)
+    ts(R("r0"), ind(R("iw"), O0), C(NS), A.add, 0.0, A.max)
+    act(R("r1"), ind(R("iw"), O1), F.Relu, bias=C(NS))
+    tt(R("r0"), R("r0"), R("r1"), A.subtract)
+    act(R("d0", 1, 352, 2), R("r0"), F.Copy, scale=C(ROOT))
+    act(R("r1"), R("r1"), F.Copy, scale=C(ROOT))
+    tt(R("d1", 1, 352, 2), R("r1"), R("n0"), A.add)
+    for t in range(5):
+        ms(R("bt", t, t + 1), 33.0 * 64.0 ** t)
+        ms(R("bt", 8 + t, 9 + t), 32.0 * 64.0 ** t)
+        ms(R("bt", 24 + t, 44, 5), 64.0 ** -t)
+    lin(R("bt", 16, 21), R("bt", 8, 13), 1.0 / (32.0 * BIG), 0.0)
+    lin(C(LW), C(J), 1.0 / 32, 1.0 / 32)
+    lin(C(PH), C(EB), 1.0, 7.5)
+    ts(R("tab", 50, 70), R("tab", 50, 70), C(NS), A.subtract, 1.0 / 32, A.mult)
+    ts(C(T0), C(J), 17.0, A.is_ge, 17.0, A.mult)
+    ts(C(T1), C(J), 22.0, A.is_ge, 5.0, A.mult)
+    lin(C(S20), C(SB), 20.0 / 32, 0.0)
+    lin(C(LE5), C(SB), 5.0 / 32, 0.0)
+    lin(C(S10), C(SB), 10.0 / 32, 0.0)
+    lin(C(N20), C(SB), -20.0 / 32, 20.0)
+    lin(C(T9), C(SB), 1.0 / 32, 0.0)
+    ts(C(T2), C(T0), C(T1), A.add, 1.0, A.add)
+    ts(C(T3), C(T2), C(T9), A.mult, C(J), A.subtract)
+    lin(C(VV), C(T3), -1.0, 1.0)
+    lin(C(VB), C(T3), 1.0, -1.5)
+    ts(C(T4), C(R16), 1.0, A.is_ge, 10.0, A.mult)
+    ts(C(T5), C(R16), 6.0, A.is_ge, -5.0, A.mult)
+    ts(R("offc", 0, 10), R("tab", 30, 40), C(S10), A.add, C(S20), A.add)
+    ts(R("offc", 10, 20), R("tab", 40, 50), C(S10), A.add, C(N20), A.add)
+    ts(C(T6), C(T4), C(T5), A.add, 5.0, A.add)
+    lin(C(LO5), C(T6), C(T9), 0.0)
+    ts(R("offm", 0, 10, 2), R("tab", 10, 20, 2), C(LE5), A.add, C(S20), A.add)
+    ts(R("offm", 10, 20, 2), R("tab", 20, 30, 2), C(LE5), A.add, C(N20), A.add)
+    ts(R("offm", 1, 10, 2), R("tab", 11, 20, 2), C(LO5), A.add, C(S20), A.add)
+    ts(R("offm", 11, 20, 2), R("tab", 21, 30, 2), C(LO5), A.add, C(N20), A.add)
+    ts(R("offw", 0, 1), C(EB), 3.0, A.mult, C(R16), A.add)
+    ts(R("offw", 1, 2), C(E16), C(R16), A.add, 16.0, A.add)
+    ts(C(T7), C(R16), 5.0, A.is_ge)
+    lin(C(T8), C(T7), -5.0, C(R16))
+    ts(C(TA), C(T7), C(T9), A.not_equal, 20.0, A.mult)
+    ts(C(TB), C(TA), C(T8), A.add, C(S10), A.add)
+    ts(R("offq"), R("tab", 70, 74), C(TB), A.add)
+    ms(R("lw", 0, 256), 0.0)
+    ms(R("kq"), 0.0)
+    ms(R("cw", 40, 48), 0.0)
+    qz(R("qv"), R("sv"), R("vt"))
+
+    def wrap(src, out, add, o):
+        tr(R("w1", 64 * o, 64 * o + 32), R(src, 0, 32))
+        tr(R("w1", 64 * o + 32, 64 * o + 64), R(src, 16, 48))
+        cp(R("w2", 32 * o, 32 * o + 32), ind(R("w1", 64 * o, 64 * o + 64), R("offw")))
+        tr(R("w3", 32 * o, 32 * o + 32), R("w2", 32 * o, 32 * o + 32))
+        ts(R(out, 0, 20, 2), R("w3", 32 * o, 32 * o + 10), add, A.add)
+        ts(R(out, 1, 20, 2), R("w3", 32 * o + 16, 32 * o + 26), add, A.add)
+
+    def swap(out):
+        for k in range(4):
+            (cp if k % 2 else lambda o, i: act(o, i, F.Copy))(R(out, 20, 40, p=quad(k ^ 1)), R(out, 0, 20, p=quad(k)))
+
+    def E(b): return R("qc", 128 * b, 128 * b + 128), R("sc", 128 * b, 128 * b + 128)
+    def ends(n, a=0, k=5): return R(n, a + 31, a + 32 * k, 32)
+    def run(n, k, w=1): return R(n, 160 * w * k, 160 * w * (k + 1))
+    def bank(k, b, n=160): return R("pa" if k else "pb", 512 * b, 512 * b + n)
+
+    for rnd in range(3):
+        mate = T.cores[rank ^ PARTNER[rnd]]
+        QT, ST, QL, SL, LO, LI = [R("%s%d" % (n, rnd)) for n in ("qt", "st", "ql", "sl", "lo", "li")]
+        for k in range(2):
+            mm(bank(0, k), R("qu2"), R("su2"), run("qx", k), run("sx", k))
+        cp(run("ss", 0), bank(0, 0))
+        act(run("ss", 1), bank(0, 1), F.Copy)
+        act(R("sb"), ind(R("ss"), O1), F.Copy)
+        tt(R("d1", 0, 352, 2), ind(R("ss"), O0), R("sb"), A.is_ge)
+        sc(R("x0", 0, 352), R("d0"), R("d1"), 0.0, A.mult, A.add)
+        for b in range(4):
+            mm(bank(1, b, 320), *E(b), R("qx"), R("sx"))
+            mm(bank(0, b), *E(b), run("qx", 0), run("sx", 0), True, False)
+        for b in range(4):
+            act(R("tt", b, 1280, 4), bank(1, b, 320), F.Copy, scale=2.0 ** -5)
+        qz(QT, ST, R("tt"))
+        send(mate, QL, QT, "rq%d" % rnd, "oq%d" % rnd, FAR + 9.0, True)
+        send(mate, SL, ST, "rs%d" % rnd, "os%d" % rnd, FAR + 9.0)
+        for b in range(4):
+            act(R("zw", 448 * b + 128, 448 * b + 448), bank(1, b, 320), F.Copy, scale=2.0 ** -5)
+        for b in range(4):
+            mm(bank(1, b, 320), *E(b), QL, SL)
+            act(R("gw", 320 * b, 320 * b + 320), bank(1, b, 320), F.Copy, scale=2.0 ** -6)
+            mm(bank(1, b), *E(b), run("qx", 1), run("sx", 1), True, False)
+        for k in range(5):
+            if k == 0:
+                tr(R("t1"), R("x0", 1, 384, 2))
+                tr(R("t2"), R("x0", 33, 353, 2))
+                act(R("xc"), R("x0", 1, 352, 2), F.Copy)
+                ts(R("offd", 0, 12, 2), R("t1", 0, 192, 32), 2.0, A.mult, C(E33), A.add)
+                ts(R("offd", 1, 11, 2), R("t2", 0, 160, 32), 2.0, A.mult, C(E33), A.add)
+                win = R("x0", 0, 352)
+            else:
+                n = "xa" if k % 2 else "xb"
+                tr(R("t1"), R(n))
+                tr(R("t2"), R(n, 16, 176))
+                act(R("xc"), R(n, 0, 176), F.Copy)
+                ts(R("offd", 0, 12, 2), R("t1", 0, 192, 32), C(E16), A.add)
+                ts(R("offd", 1, 11, 2), R("t2", 0, 160, 32), C(E16), A.add)
+                win = R(n, 0, 176)
+            tt(R("xb" if k % 2 else "xa", 0, 176), ind(win, R("offd", 0, 11)), R("xc"), A.min)
+        ts(R("ap"), ind(R("xa", 0, 176), R("offa")), C(NBIG), A.mult)
+        act(R("art"), ind(R("xa", 0, 176), R("offa")), F.Identity, scale=C(PBIG), bias=C(J32))
+        sc(R("cnt"), R("seg"), R("ap"), 0.0, A.mult, A.add)
+        tr(R("ar"), R("art"))
+        for l in range(4):
+            SG = R("sig", 5 * l, 5 * l + 5)
+            S2, HF, HB, LV, W = [R("sm", 40 * l + 8 * k, 40 * l + 8 * k + 5) for k in range(5)]
+            PRE, RE, BASE = [R("smb", 24 * l + 8 * k, 24 * l + 8 * k + 5) for k in range(3)]
+            if l == 0:
+                ts(RE, ends("cnt"), -16.0 * BIG, A.is_ge, 40.0, A.mult)
+                tt(S2, ends("cnt"), R("bt", 16, 21), A.mult)
+                ts(HF, ends("cnt"), -16.0 * BIG, A.is_ge)
+                tt(SG, S2, R("bt", 8, 13), A.add)
+            else:
+                o = 24 * l - 8
+                for t in range(5):
+                    ts(R("yy", 32 * t, 32 * t + 32), R("ap", 32 * t, 32 * t + 32), R("kk", 32 * t + 31, 32 * t + 32), A.add, R("smb", o + t, o + t + 1), A.add)
+                tt(SG, ends("kk"), R("smb", o, o + 5), A.add)
+                tr(R("yt"), R("yy"))
+                act(S2, SG, F.Copy, scale=2.03125)
+                ts(R("keep"), R("yt"), 0.0, A.not_equal)
+                sc(R("nu"), R("keep"), R("yt"), 0.0, A.mult, A.max)
+                sc(R("rr"), R("keep"), R("ones", 0, 160), 1.0, A.mult, A.add)
+                tt(HF, S2, ends("nu"), A.is_gt)
+                tt(RE, HF, ends("rr"), A.mult)
+            tt(PRE, R("bt", 0, 5), SG, A.subtract)
+            for t in range(5):
+                ts(R("dy", 32 * t, 32 * t + 32), R("ar", 32 * t, 32 * t + 32), R("smb", 24 * l + 8 + t, 24 * l + 9 + t), A.is_lt, R("smb", 24 * l + t, 24 * l + t + 1), A.mult)
+            tr(run("dyt", l), R("dy"))
+            if l < 3:
+                tt(HB, HF, R("bt", 0, 5), A.mult)
+                tt(BASE, SG, HB, A.subtract)
+                sc(R("kk"), R("seg"), run("dyt", l), 0.0, A.mult, A.max)
+            act(run("z0", l), run("dyt", l), F.Sign, bias=-0.5)
+            sc(run("rho", l), R("dn"), run("z0", l), -1.0, A.add, A.max)
+            if l:
+                act(LV, SG, F.Identity, scale=-BIG, bias=C(LW))
+                tt(W, ends("rho", 160 * l), LV, A.max)
+            for t in range(5):
+                o = 160 * l + 32 * t
+                act(R("y2", o, o + 32), R("ap", 32 * t, 32 * t + 32), F.Identity, bias=R("sm", 40 * l + 32 + t, 40 * l + 33 + t) if l else R("rho", o + 31, o + 32))
+            tr(run("y2t", l), run("y2", l))
+            act(run("k3", l), run("y2t", l), F.Sign, scale=-1.0, bias=1.0 / 64)
+            sc(run("xs", l), run("k3", l), run("y2t", l), 0.0, A.mult, A.max)
+        tt(R("swn", 0, 20), R("sig"), R("bt", 24, 44), A.mult)
+        swap("swn")
+        act(R("mm"), ind(R("swn"), R("offm")), F.Copy)
+        tr(R("rs"), R("mm"))
+        act(R("sg"), R("rs"), F.Sign, bias=C(VB), accum_out=R("acc", 0, 1))
+        ts(R("i2"), R("rs"), C(VV), A.is_equal, 2.0, A.mult)
+        sc(R("pp"), R("ones"), R("i2"), R("acc", 0, 1), A.mult, A.add)
+        act(R("ng"), R("i2"), F.Copy, scale=-512.0)
+        tr(R("ppt"), R("pp"))
+        tr(R("ngt"), R("ng"))
+        sc(R("ps"), R("ngt"), R("ppt"), 0.0, A.add, A.max)
+        ts(R("kq", 0, 10), ends("ps", 0, 10), 0.5, A.mult, 151.5, A.add)
+        ts(R("kq", 32, 42), ends("ps", 0, 10), 0.5, A.mult, 151.5, A.add)
+        for h in range(2):
+            ts(R("kq", 16, 26, p=quad(2 * h)), R("ps", 16, 320, 32, p=quad(2 * h + 1)), 0.5, A.mult, 151.5, A.add)
+            ts(R("kq", 16, 26, p=quad(2 * h + 1)), R("ps", 21, 320, 32, p=quad(2 * h + 1)), 0.5, A.mult, 151.5, A.add)
+        ts(R("tq"), R("kq"), 1.5 * 2.0 ** 27, A.add, 1.5 * 2.0 ** 27, A.subtract)
+        tt(R("wi"), R("kq"), R("tq"), A.add)
+        wrap("wi", "offs", C(PH), 0)
+        tt(R("cw", 0, 20), ends("xs", 0, 20), R("tab", 50, 70), A.add)
+        swap("cw")
+        act(R("m2"), ind(R("cw"), R("offc")), F.Copy)
+        tr(R("rc"), R("m2"))
+        cp(ind(R("lw"), R("offs")), R("rc"))
+        tr(R("lt"), R("lw", 0, 256))
+        tt(R("ls"), R("lt", 0, 256, 32), R("lt", 16, 256, 32), A.add)
+        ts(LO, R("ls"), 32.0, A.mult, 160.0, A.add)
+        send(mate, LI, LO, "rl%d" % rnd, "ol%d" % rnd, FAR)
+        for b in range(4):
+            act(R("he", 128 * b, 128 * b + 128), ind(R("zw", 448 * b + 128, 448 * b + 448), LO), F.Copy, scale=0.5)
+        ts(R("cq"), ind(R("cw"), R("offq", 0, 3)), 32.0, A.mult, 280.5, A.add)
+        ts(R("zq", 0, 48), R("kq"), 120.0, A.is_gt)
+        tt(R("cq"), R("cq"), R("kq"), A.subtract)
+        tt(R("zq", 48, 96), R("cq"), R("zq", 0, 48), A.mult)
+        tt(R("wz"), R("zq", 48, 96), R("kq"), A.add)
+        wrap("wz", "offz", 7.5, 1)
+        if rnd == 2:
+            lin(R("rcf"), R("rc"), 32.0, 160.0)
+            for k in range(8):
+                dma("sy", H(T.cl[k:k + 1, :]), R("rcf", p=(16 * k, 16 * k + 1)))
+        for b in range(4):
+            tt(R("zw", 448 * b, 448 * b + 128), ind(R("gw", 320 * b, 320 * b + 320), LI), R("he", 128 * b, 128 * b + 128), A.add)
+        for k in range(2):
+            for b in range(4):
+                o, i = R("zt", 640 * k + b, 640 * k + 640, 4), ind(R("zw", 448 * b, 448 * b + 448), R("offz", 10 * k, 10 * k + 10))
+                if 4 * k + b in ZV:
+                    cp(o, i)
+                else:
+                    act(o, i, F.Copy)
+            qz(run("qz", k), run("sz", k), run("zt", k, 4))
+            for b in range(4):
+                mm(bank(k, b), R("qw", 128 * b, 128 * b + 128), R("sw", 128 * b, 128 * b + 128), run("qz", k), run("sz", k), False, True)
+                if 4 * k + b in XV:
+                    ts(R("xt", 640 * k + b, 640 * k + 640, 4), bank(k, b), 2.0 ** -5, A.mult)
+                else:
+                    act(R("xt", 640 * k + b, 640 * k + 640, 4), bank(k, b), F.Copy, scale=2.0 ** -5)
+            qz(run("qx", k), run("sx", k), run("xt", k, 4))
+
+    for k in range(2):
+        mm(bank(0, k), R("qv"), R("sv"), run("qx", k), run("sx", k))
+        dma("sy", H(T.oc[:, 640 * k:640 * k + 640]), u8(run("qx", k)))
+    for k in range(4):
+        dma("gp" if k == 3 else "sy", H(T.osc[4 * k:4 * k + 4, :]), R("sx", p=(32 * k, 32 * k + 4)))
+    act(run("yo", 0), bank(0, 0), F.Copy)
+    cp(run("yo", 1), bank(0, 1))
+    dma("a", H(T.y[:, 0:160]), run("yo", 0))
+    dma("sy", H(T.y[:, 160:320]), run("yo", 1))
+    lay_out()

@@ -11,34 +11,37 @@ _S = {
     "idn": (128, F32), "zw": (1792, BF), "gw": (1280, BF), "he": (512, BF), "yo": (320, F32),
     "pt": (48, I32), "ci": (8, I32), "cf": (40, F32), "tab": (80, F32), "iw": (320, F32), "ni": (176, I32),
     "offu": (8, U16), "offp": (36, U16), "offd": (12, U16), "offa": (10, U16), "offm": (20, U16), "offc": (20, U16),
-    "offq": (4, U16), "offw": (2, U16), "offs": (20, U16), "offz": (20, U16),
+    "offq": (4, U16), "offw": (2, U16), "offs": (20, U16), "offz": (20, U16), "offl": (2, U16),
     "ss": (320, F32), "sb": (176, F32), "d0": (352, BF), "d1": (352, BF), "x0": (384, BF), "xa": (192, BF), "xb": (192, BF),
     "xc": (176, BF), "t1": (192, BF), "t2": (160, BF), "r0": (176, F32), "r1": (176, F32), "n0": (176, F32),
     "ap": (160, BF), "art": (160, BF), "ar": (160, BF), "r32": (160, BF), "seg": (160, BF), "ones": (320, BF), "dn": (160, BF),
-    "cnt": (160, BF), "yy": (160, BF), "yt": (160, BF), "keep": (160, BF), "nu": (160, BF), "rr": (160, BF),
+    "cnt": (160, BF), "yy": (160, BF), "yt": (160, BF), "keep": (160, BF),
+    "nr": (320, BF), "md": (320, BF), "re": (320, BF), "dg": (160, BF), "ar1": (160, BF),
     "dy": (160, BF), "dyt": (640, BF), "kk": (160, BF), "z0": (640, BF), "rho": (640, BF),
     "y2": (640, BF), "y2t": (640, BF), "k3": (640, BF), "xs": (640, BF),
     "bt": (48, F32), "sig": (20, F32), "sm": (160, F32), "smb": (96, BF),
     "swn": (40, F32), "cw": (48, F32), "mm": (320, BF), "rs": (320, BF), "sg": (320, BF), "acc": (8, F32),
     "i2": (320, BF), "ng": (320, BF), "ngt": (320, BF), "pp": (320, F16), "ppt": (320, F16), "ps": (320, F16),
-    "m2": (320, BF), "rc": (320, BF), "rcf": (320, F32), "kq": (48, F32), "tq": (48, F32), "wi": (48, F32), "wz": (48, F32),
+    "m2": (320, BF), "rc": (320, BF), "rcf": (320, F32), "kq": (48, F32), "wz": (48, F32),
     "w1": (128, F32), "w2": (64, F32), "w3": (64, F32), "cq": (48, F32), "zq": (96, F32),
-    "lw": (640, BF), "lt": (256, BF), "ls": (8, F32),
+    "lw": (336, BF), "lt": (256, BF),
 }
 for _t in range(3):
     _S["qt%d" % _t] = (320, X4)
     _S["st%d" % _t] = (320, U8)
     _S["ql%d" % _t] = (320, X4)
     _S["sl%d" % _t] = (320, U8)
-    _S["lo%d" % _t] = (8, U16)
+    _S["lo%d" % _t] = (16, U16)
     _S["li%d" % _t] = (8, U16)
 SCRATCH = {k: ("sbuf", [128, n], d) for k, (n, d) in _S.items()}
 SCRATCH["pa"] = ("psum", [128, 2048], F32)
 SCRATCH["pb"] = ("psum", [128, 2048], F32)
 SEMAPHORES = ["v", "a", "pe", "gp"] + ["m%d" % i for i in range(32)] + ["%s%d" % (n, t) for n in ("rq", "rs", "rl", "oq", "os", "ol") for t in range(3)]
-BIG = 2.0 ** 40
-CY, WAKE, FAR = 0.001, 0.07, 2.2
-ZV, XV = (3, 7), (3, 7)
+BIG = 2.0 ** 50
+B0 = 2048.0
+CY, WAKE, FAR = 0.00083, 0.16, 2.2
+STEPS = (1, 3, 3)
+ZV, XV = (3, 6, 7), (1, 3, 5, 7)
 
 
 def rank_program(g, core, T, topo):
@@ -183,8 +186,8 @@ def rank_program(g, core, T, topo):
     def u32(x): return (x[0].bitcast(dt.uint32),) + x[1:]
     def C(k): return R("cf", k, k + 1)
     def quad(k): return (32 * k, 32 * k + 32)
-    (J, R16, SB, EB, E16, E33, NS, ROOT, NBIG, PBIG, J32, LW, PH, VV, VB, S20, N20, LE5, LO5, S10, NR,
-     T0, T1, T2, T3, T4, T5, T6, T7, T8, T9, TA, TB) = range(33)
+    (J, R16, SB, EB, P1, P6, E16, E33, NS, ROOT, PBIG, J32, PH, VV, VB, S20, N20, LE5, LO5, S10, NR,
+     T0, T1, T2, T3, T4, T5, T6, T7, T8, T9, TA, TB, TC) = range(34)
 
     dma("sy", R("xt", 0, 640), H(T.x[:, 0:640]), 3.0)
     dma("a", R("xt", 640, 1280), H(T.x[:, 640:1280]), 3.0)
@@ -197,7 +200,7 @@ def rank_program(g, core, T, topo):
     dma("sy", u8(R("qw")), H(T.wc[:]))
     dma("sy", R("sw"), H(T.ws[:]))
     dma("sy", R("vt"), H(T.v[:]))
-    iota(R("ci", 4, 5), [[0, 1]], 0, 1)
+    iota(R("ci", 7, 8), [[0, 1]], 0, 1)
     iota(R("idn"), [[1, 128]], 0, -1)
     iota(R("iw"), [[1, 320]], 0, 0)
     iota(R("tab", 0, 10), [[16, 10]], 0, 0)
@@ -206,13 +209,13 @@ def rank_program(g, core, T, topo):
     iota(R("tab", 30, 50), [[0, 2], [1, 5], [5, 2]], 0, 0)
     iota(R("tab", 50, 70), [[0, 4], [32, 5]], -161, 0)
     iota(R("tab", 70, 74), [[0, 2], [5, 2]], 0, 0)
-    for k, m in enumerate((31, 15, 32, 16)):
-        ts(R("ci", k, k + 1), R("ci", 4, 5), m, A.bitwise_and)
+    for k, m in enumerate((31, 15, 32, 16, 1, 6)):
+        ts(R("ci", k, k + 1), R("ci", 7, 8), m, A.bitwise_and)
     for b in range(4):
         ms(R("ct", 512 * b, 512 * b + 512), 0.0)
         ts(R("ct", 513 * b, 512 * b + 512, 4), R("idn"), 0.0, A.is_equal, 32.0, A.mult)
         qz(R("qc", 128 * b, 128 * b + 128), R("sc", 128 * b, 128 * b + 128), R("ct", 512 * b, 512 * b + 512))
-    cp(R("cf", 0, 4), R("ci", 0, 4))
+    cp(R("cf", 0, 6), R("ci", 0, 6))
     ms(R("offu", 0, 4), 0)
     ms(R("offu", 4, 8), 64)
     ms(R("x0", 352, 384), 0.0)
@@ -225,7 +228,6 @@ def rank_program(g, core, T, topo):
     lin(C(NS), C(SB), -5.0, 0.0)
     ts(C(ROOT), C(J), 0.0, A.is_equal)
     ts(C(NR), C(J), 0.0, A.not_equal)
-    lin(C(NBIG), C(NR), -BIG, 0.0)
     lin(C(PBIG), C(NR), BIG, 0.0)
     lin(C(J32), C(J), -1.0, 32.0)
     ts(R("ni"), R("iw", 0, 176), C(E16), A.add)
@@ -249,11 +251,12 @@ def rank_program(g, core, T, topo):
     act(R("r1"), R("r1"), F.Copy, scale=C(ROOT))
     tt(R("d1", 1, 352, 2), R("r1"), R("n0"), A.add)
     for t in range(5):
-        ms(R("bt", t, t + 1), 33.0 * 64.0 ** t)
-        ms(R("bt", 8 + t, 9 + t), 32.0 * 64.0 ** t)
-        ms(R("bt", 24 + t, 44, 5), 64.0 ** -t)
-    lin(R("bt", 16, 21), R("bt", 8, 13), 1.0 / (32.0 * BIG), 0.0)
-    lin(C(LW), C(J), 1.0 / 32, 1.0 / 32)
+        ms(R("bt", t, t + 1), 33.0 * B0 * 64.0 ** t)
+        ms(R("bt", 24 + t, 44, 5), 64.0 ** -t / B0)
+    ts(R("dg"), R("r32"), C(J), A.not_equal, BIG, A.mult)
+    ms(R("md"), BIG)
+    lin(C(TC), C(P1), 128.0, C(EB))
+    ts(R("offl", 0, 1), C(P6), 16.0, A.mult, C(TC), A.add)
     lin(C(PH), C(EB), 1.0, 7.5)
     ts(R("tab", 50, 70), R("tab", 50, 70), C(NS), A.subtract, 1.0 / 32, A.mult)
     ts(C(T0), C(J), 17.0, A.is_ge, 17.0, A.mult)
@@ -284,7 +287,7 @@ def rank_program(g, core, T, topo):
     ts(C(TA), C(T7), C(T9), A.not_equal, 20.0, A.mult)
     ts(C(TB), C(TA), C(T8), A.add, C(S10), A.add)
     ts(R("offq"), R("tab", 70, 74), C(TB), A.add)
-    ms(R("lw", 0, 256), 0.0)
+    ms(R("lw", 0, 144), 0.0)
     ms(R("kq"), 0.0)
     ms(R("cw", 40, 48), 0.0)
     qz(R("qv"), R("sv"), R("vt"))
@@ -297,9 +300,10 @@ def rank_program(g, core, T, topo):
         ts(R(out, 0, 20, 2), R("w3", 32 * o, 32 * o + 10), add, A.add)
         ts(R(out, 1, 20, 2), R("w3", 32 * o + 16, 32 * o + 26), add, A.add)
 
-    def swap(out):
+    def swap(out, a, b, f):
+        tt(R(out, 0, 20), R(*a), R(*b), f)
         for k in range(4):
-            (cp if k % 2 else lambda o, i: act(o, i, F.Copy))(R(out, 20, 40, p=quad(k ^ 1)), R(out, 0, 20, p=quad(k)))
+            tt(R(out, 20, 40, p=quad(k ^ 1)), R(*a, p=quad(k)), R(*b, p=quad(k)), f)
 
     def E(b): return R("qc", 128 * b, 128 * b + 128), R("sc", 128 * b, 128 * b + 128)
     def ends(n, a=0, k=5): return R(n, a + 31, a + 32 * k, 32)
@@ -330,69 +334,68 @@ def rank_program(g, core, T, topo):
             mm(bank(1, b, 320), *E(b), QL, SL)
             act(R("gw", 320 * b, 320 * b + 320), bank(1, b, 320), F.Copy, scale=2.0 ** -6)
             mm(bank(1, b), *E(b), run("qx", 1), run("sx", 1), True, False)
-        for k in range(5):
-            if k == 0:
+        cur = "x0"
+        for steps in STEPS:
+            if cur == "x0":
                 tr(R("t1"), R("x0", 1, 384, 2))
                 tr(R("t2"), R("x0", 33, 353, 2))
                 act(R("xc"), R("x0", 1, 352, 2), F.Copy)
                 ts(R("offd", 0, 12, 2), R("t1", 0, 192, 32), 2.0, A.mult, C(E33), A.add)
                 ts(R("offd", 1, 11, 2), R("t2", 0, 160, 32), 2.0, A.mult, C(E33), A.add)
-                win = R("x0", 0, 352)
             else:
-                n = "xa" if k % 2 else "xb"
-                tr(R("t1"), R(n))
-                tr(R("t2"), R(n, 16, 176))
-                act(R("xc"), R(n, 0, 176), F.Copy)
+                tr(R("t1"), R(cur))
+                tr(R("t2"), R(cur, 16, 176))
+                act(R("xc"), R(cur, 0, 176), F.Copy)
                 ts(R("offd", 0, 12, 2), R("t1", 0, 192, 32), C(E16), A.add)
                 ts(R("offd", 1, 11, 2), R("t2", 0, 160, 32), C(E16), A.add)
-                win = R(n, 0, 176)
-            tt(R("xb" if k % 2 else "xa", 0, 176), ind(win, R("offd", 0, 11)), R("xc"), A.min)
-        ts(R("ap"), ind(R("xa", 0, 176), R("offa")), C(NBIG), A.mult)
-        act(R("art"), ind(R("xa", 0, 176), R("offa")), F.Identity, scale=C(PBIG), bias=C(J32))
+            for _ in range(steps):
+                nxt = "xb" if cur == "xa" else "xa"
+                tt(R(nxt, 0, 176), ind(R(cur, 0, 352 if cur == "x0" else 176), R("offd", 0, 11)), R("xc"), A.min)
+                cur = nxt
+        ts(R("ap"), ind(R(cur, 0, 176), R("offa")), C(PBIG), A.mult)
+        act(R("art"), ind(R(cur, 0, 176), R("offa")), F.Identity, scale=C(PBIG), bias=C(J32))
         sc(R("cnt"), R("seg"), R("ap"), 0.0, A.mult, A.add)
         tr(R("ar"), R("art"))
+        tt(R("ar1"), R("ar"), R("dg"), A.min)
         for l in range(4):
             SG = R("sig", 5 * l, 5 * l + 5)
-            S2, HF, HB, LV, W = [R("sm", 40 * l + 8 * k, 40 * l + 8 * k + 5) for k in range(5)]
-            PRE, RE, BASE = [R("smb", 24 * l + 8 * k, 24 * l + 8 * k + 5) for k in range(3)]
+            HF, HB = [R("sm", 40 * l + 8 * k, 40 * l + 8 * k + 5) for k in range(2)]
+            PRE, BASE = [R("smb", 24 * l + 8 * k, 24 * l + 8 * k + 5) for k in (0, 2)]
+            RE = R("re", 63, 320, 64)
             if l == 0:
-                ts(RE, ends("cnt"), -16.0 * BIG, A.is_ge, 40.0, A.mult)
-                tt(S2, ends("cnt"), R("bt", 16, 21), A.mult)
-                ts(HF, ends("cnt"), -16.0 * BIG, A.is_ge)
-                tt(SG, S2, R("bt", 8, 13), A.add)
+                ts(RE, ends("cnt"), 16.0 * BIG, A.is_le, 40.0, A.mult)
+                for t in range(5):
+                    lin(R("smb", t, t + 1), R("cnt", 32 * t + 31, 32 * t + 32), B0 * 64.0 ** t / BIG, B0 * 64.0 ** t)
+                tt(SG, R("bt", 0, 5), PRE, A.subtract)
             else:
                 o = 24 * l - 8
                 for t in range(5):
-                    ts(R("yy", 32 * t, 32 * t + 32), R("ap", 32 * t, 32 * t + 32), R("kk", 32 * t + 31, 32 * t + 32), A.add, R("smb", o + t, o + t + 1), A.add)
+                    ts(R("yy", 32 * t, 32 * t + 32), R("ap", 32 * t, 32 * t + 32), R("kk", 32 * t + 31, 32 * t + 32), A.subtract, R("smb", o + t, o + t + 1), A.subtract)
                 tt(SG, ends("kk"), R("smb", o, o + 5), A.add)
                 tr(R("yt"), R("yy"))
-                act(S2, SG, F.Copy, scale=2.03125)
+                lin(R("md", 63, 320, 64), SG, 2.03125, 40.0)
                 ts(R("keep"), R("yt"), 0.0, A.not_equal)
-                sc(R("nu"), R("keep"), R("yt"), 0.0, A.mult, A.max)
-                sc(R("rr"), R("keep"), R("ones", 0, 160), 1.0, A.mult, A.add)
-                tt(HF, S2, ends("nu"), A.is_gt)
-                tt(RE, HF, ends("rr"), A.mult)
-            tt(PRE, R("bt", 0, 5), SG, A.subtract)
+                sc(R("nr", 0, 320, 2), R("keep"), R("yt"), 0.0, A.mult, A.min)
+                sc(R("nr", 1, 320, 2), R("keep"), R("ones", 0, 160), 1.0, A.mult, A.add)
+                sc(R("re"), R("md"), R("nr"), 0.0, A.add, A.min)
+                tt(PRE, R("bt", 0, 5), SG, A.subtract)
             for t in range(5):
-                ts(R("dy", 32 * t, 32 * t + 32), R("ar", 32 * t, 32 * t + 32), R("smb", 24 * l + 8 + t, 24 * l + 9 + t), A.is_lt, R("smb", 24 * l + t, 24 * l + t + 1), A.mult)
+                ts(R("dy", 32 * t, 32 * t + 32), R("ar1" if l else "ar", 32 * t, 32 * t + 32), R("re", 64 * t + 63, 64 * t + 64), A.is_lt, R("smb", 24 * l + t, 24 * l + t + 1), A.mult)
             tr(run("dyt", l), R("dy"))
             if l < 3:
+                ts(HF, RE, 0.0, A.is_gt)
                 tt(HB, HF, R("bt", 0, 5), A.mult)
                 tt(BASE, SG, HB, A.subtract)
                 sc(R("kk"), R("seg"), run("dyt", l), 0.0, A.mult, A.max)
             act(run("z0", l), run("dyt", l), F.Sign, bias=-0.5)
             sc(run("rho", l), R("dn"), run("z0", l), -1.0, A.add, A.max)
-            if l:
-                act(LV, SG, F.Identity, scale=-BIG, bias=C(LW))
-                tt(W, ends("rho", 160 * l), LV, A.max)
             for t in range(5):
                 o = 160 * l + 32 * t
-                act(R("y2", o, o + 32), R("ap", 32 * t, 32 * t + 32), F.Identity, bias=R("sm", 40 * l + 32 + t, 40 * l + 33 + t) if l else R("rho", o + 31, o + 32))
+                act(R("y2", o, o + 32), R("ap", 32 * t, 32 * t + 32), F.Identity, scale=-1.0, bias=R("rho", o + 31, o + 32))
             tr(run("y2t", l), run("y2", l))
             act(run("k3", l), run("y2t", l), F.Sign, scale=-1.0, bias=1.0 / 64)
             sc(run("xs", l), run("k3", l), run("y2t", l), 0.0, A.mult, A.max)
-        tt(R("swn", 0, 20), R("sig"), R("bt", 24, 44), A.mult)
-        swap("swn")
+        swap("swn", ("sig", 0, 20), ("bt", 24, 44), A.mult)
         act(R("mm"), ind(R("swn"), R("offm")), F.Copy)
         tr(R("rs"), R("mm"))
         act(R("sg"), R("rs"), F.Sign, bias=C(VB), accum_out=R("acc", 0, 1))
@@ -407,17 +410,15 @@ def rank_program(g, core, T, topo):
         for h in range(2):
             ts(R("kq", 16, 26, p=quad(2 * h)), R("ps", 16, 320, 32, p=quad(2 * h + 1)), 0.5, A.mult, 151.5, A.add)
             ts(R("kq", 16, 26, p=quad(2 * h + 1)), R("ps", 21, 320, 32, p=quad(2 * h + 1)), 0.5, A.mult, 151.5, A.add)
-        ts(R("tq"), R("kq"), 1.5 * 2.0 ** 27, A.add, 1.5 * 2.0 ** 27, A.subtract)
-        tt(R("wi"), R("kq"), R("tq"), A.add)
-        wrap("wi", "offs", C(PH), 0)
-        tt(R("cw", 0, 20), ends("xs", 0, 20), R("tab", 50, 70), A.add)
-        swap("cw")
+        wrap("kq", "offs", C(PH), 0)
+        swap("cw", ("xs", 31, 640, 32), ("tab", 50, 70), A.add)
         act(R("m2"), ind(R("cw"), R("offc")), F.Copy)
         tr(R("rc"), R("m2"))
         cp(ind(R("lw"), R("offs")), R("rc"))
-        tr(R("lt"), R("lw", 0, 256))
-        tt(R("ls"), R("lt", 0, 256, 32), R("lt", 16, 256, 32), A.add)
-        ts(LO, R("ls"), 32.0, A.mult, 160.0, A.add)
+        tr(R("lt", 0, 128), R("lw", 0, 128))
+        tr(R("lt", 128, 256), R("lw", 16, 144))
+        ts(LO, ind(R("lt"), R("offl", 0, 1)), 32.0, A.mult, 160.0, A.add)
+        LO = R("lo%d" % rnd, 0, 8)
         send(mate, LI, LO, "rl%d" % rnd, "ol%d" % rnd, FAR)
         for b in range(4):
             act(R("he", 128 * b, 128 * b + 128), ind(R("zw", 448 * b + 128, 448 * b + 448), LO), F.Copy, scale=0.5)

@@ -1,29 +1,27 @@
+import math
 from concourse.mybir import dt, AluOpType, ActivationFunctionType
 A = AluOpType
 F = ActivationFunctionType
 BF, F32, F16, U16, I32, X4, U8 = "bfloat16", "float32", "float16", "uint16", "int32", "float8_e4m3fn_x4", "uint8"
 PARTNER = [1, 2, 4]
 _S = {
-    "xt": (1280, BF), "ut": (512, BF), "vt": (512, BF), "ct": (2048, BF), "tt": (1280, BF), "zt": (1280, BF),
+    "xt": (1280, BF), "ut": (512, BF), "vt": (512, BF), "ct": (516, BF), "tt": (1280, BF), "zt": (1280, BF),
     "qx": (320, X4), "sx": (320, U8), "qu": (128, X4), "su": (128, U8), "qu2": (128, X4), "su2": (128, U8),
     "qv": (128, X4), "sv": (128, U8), "qw": (512, X4), "sw": (512, U8), "qc": (512, X4), "sc": (512, U8),
     "qz": (320, X4), "sz": (320, U8),
-    "idn": (128, F32), "zw": (1792, BF), "gw": (1280, BF), "he": (512, BF), "yo": (320, F32),
-    "pt": (48, I32), "ci": (8, I32), "cf": (40, F32), "tab": (80, F32), "iw": (320, F32), "ni": (176, I32),
-    "offu": (8, U16), "offp": (36, U16), "offd": (12, U16), "offa": (10, U16), "offm": (20, U16), "offc": (20, U16),
-    "offq": (4, U16), "offw": (2, U16), "offs": (20, U16), "offz": (20, U16), "offl": (2, U16),
-    "ss": (320, F32), "sb": (176, F32), "d0": (352, BF), "d1": (352, BF), "x0": (384, BF), "xa": (192, BF), "xb": (192, BF),
-    "xc": (176, BF), "t1": (192, BF), "t2": (160, BF), "r0": (176, F32), "r1": (176, F32), "n0": (176, F32),
-    "ap": (160, BF), "art": (160, BF), "ar": (160, BF), "r32": (160, BF), "seg": (160, BF), "ones": (320, BF), "dn": (160, BF),
-    "cnt": (160, BF), "yy": (160, BF), "yt": (160, BF), "keep": (160, BF),
-    "nr": (320, BF), "md": (320, BF), "re": (320, BF), "dg": (160, BF), "ar1": (160, BF),
-    "dy": (160, BF), "dyt": (640, BF), "kk": (160, BF), "z0": (640, BF), "rho": (640, BF),
-    "y2": (640, BF), "y2t": (640, BF), "k3": (640, BF), "xs": (640, BF),
-    "bt": (48, F32), "sig": (20, F32), "sm": (160, F32), "smb": (96, BF),
-    "swn": (40, F32), "cw": (48, F32), "mm": (320, BF), "rs": (320, BF), "sg": (320, BF), "acc": (8, F32),
-    "i2": (320, BF), "ng": (320, BF), "ngt": (320, BF), "pp": (320, F16), "ppt": (320, F16), "ps": (320, F16),
-    "m2": (320, BF), "rc": (320, BF), "rcf": (320, F32), "kq": (48, F32), "wz": (48, F32),
-    "w1": (128, F32), "w2": (64, F32), "w3": (64, F32), "cq": (48, F32), "zq": (96, F32),
+    "zw": (1792, BF), "gw": (1280, BF), "he": (512, BF), "yo": (320, F32),
+    "pt": (48, I32), "ci": (8, I32), "cf": (64, F32), "tab": (48, F32), "iw": (320, F32), "ni": (176, I32),
+    "offk": (16, U16), "offp": (36, U16), "offd": (52, U16), "offa": (10, U16), "offs": (32, U16), "offz": (32, U16),
+    "ss": (320, F32), "sb": (176, F32), "d0": (352, BF), "d1": (352, BF), "x0": (384, BF), "xj": (6 * 192, BF),
+    "tw": (3 * 352, BF), "xu": (160, BF), "xc": (176, BF), "nb": (176, BF), "r0": (176, F32), "r1": (176, F32), "n0": (176, F32),
+    "ap": (160, BF), "apt": (160, BF), "ar0": (160, BF), "arx": (160, BF), "ar": (160, BF), "thr": (160, F16), "pj": (176, BF),
+    "dm": (160, BF), "dc": (160, BF), "r32": (160, BF), "seg": (160, BF), "dn": (160, BF), "de": (160, BF),
+    "cnt": (160, BF), "yy": (160, BF), "lf": (160, BF), "n0s": (320, BF), "n1s": (320, BF), "gg": (320, BF), "dd": (160, BF),
+    "dy": (160, BF), "u0": (320, BF), "u1": (4 * 320, BF), "up": (4 * 384, BF), "sm": (64, BF),
+    "z0": (480, BF), "rho": (480, BF), "y2": (640, BF), "y2t": (640, BF), "k3": (640, BF), "xs": (640, BF),
+    "sl": (320, BF), "km": (672, BF), "mm": (320, BF), "rs": (320, BF), "sg": (320, BF),
+    "e1": (320, F16), "e2": (336, F16), "pp": (352, F16), "pq": (672, F16), "ps": (672, F16), "kq": (72, F32),
+    "m2": (320, BF), "rc": (352, BF), "rt": (672, BF), "rcf": (320, F32), "wz": (160, F32),
     "lw": (336, BF), "lt": (256, BF),
 }
 for _t in range(3):
@@ -37,9 +35,10 @@ SCRATCH = {k: ("sbuf", [128, n], d) for k, (n, d) in _S.items()}
 SCRATCH["pa"] = ("psum", [128, 2048], F32)
 SCRATCH["pb"] = ("psum", [128, 2048], F32)
 SEMAPHORES = ["v", "a", "pe", "gp"] + ["m%d" % i for i in range(32)] + ["%s%d" % (n, t) for n in ("rq", "rs", "rl", "oq", "os", "ol") for t in range(3)]
-BIG = 2.0 ** 50
-B0 = 2048.0
-CY, WAKE, FAR = 0.00083, 0.16, 2.2
+U = [2.0 ** -6, 2.0 ** -6, 2.0 ** -12, 2.0 ** -18, 2.0 ** -24]
+SLOT = (0, 0, 17, 26)
+CY, WAKE, FAR = 0.001, 0.1, 2.0
+PASSES = 6
 STEPS = (1, 3, 3)
 ZV, XV = (3, 6, 7), (1, 3, 5, 7)
 
@@ -67,7 +66,7 @@ def rank_program(g, core, T, topo):
     def meet(x, y):
         if x[2] <= y[1] or y[2] <= x[1] or x[4] <= y[3] or y[4] <= x[3]:
             return False
-        return not (x[5] == y[5] and x[5] > 1 and (x[3] - y[3]) % x[5])
+        return (x[3] - y[3]) % math.gcd(x[5], y[5]) == 0
 
     def node(q, reads, writes, emit, cost, lat=0.0, ev=None, free=False, after=()):
         me, deps, soft = len(nodes), set(after), set()
@@ -78,7 +77,7 @@ def rank_program(g, core, T, topo):
                     if meet(x, y) and (wr or w2 or (psum and nodes[k]["q"] != q)):
                         (soft if free and psum and nodes[k]["q"] == q else deps).add(k)
         for x in writes:
-            hist[x[0]] = [z for z in hist.get(x[0], []) if not (x[5] == 1 and x[1] <= z[0][1] and z[0][2] <= x[2] and x[3] <= z[0][3] and z[0][4] <= x[4])]
+            hist[x[0]] = [z for z in hist.get(x[0], []) if not ((x[5] == 1 or x[3:] == z[0][3:]) and x[1] <= z[0][1] and z[0][2] <= x[2] and x[3] <= z[0][3] and z[0][4] <= x[4])]
             hist[x[0]].append((x, True, me))
         for x in reads:
             hist.setdefault(x[0], []).append((x, False, me))
@@ -105,20 +104,20 @@ def rank_program(g, core, T, topo):
 
     def cc(o, *ins):
         if ins[0][4]:
-            return 0.06 + 1.6 * CY * ins[0][2]
+            return 0.055 + 0.0013 * ins[0][2]
         if o[4]:
-            return 0.06 + 3.8 * CY * o[2]
+            return 0.05 + 0.0032 * o[2]
         return CY * max(64, o[2] * (0.5 if o[3] and all(i[3] for i in ins) else 1))
 
     def cp(o, i): op("v", V.tensor_copy, 1, cc(o, i), o, i)
-    def tt(o, a, b, f): op("v", V.tensor_tensor, 1, CY * max(64, 2 * o[2]), o, a, b, f)
+    def tt(o, a, b, f): op("v", V.tensor_tensor, 1, cc(o, a) if a[4] else CY * max(64, 2 * o[2]), o, a, b, f)
     def tr(o, i): op("v", V.transpose, 1, cc(o, i), o, i)
     def ms(o, c): op("v", V.memset, 1, cc(o, o), o, c)
     def sc(o, a, b, i, f0, f1): op("v", V.tensor_tensor_scan, 1, cc(o, a, b), o, a, b, i, f0, f1)
-    def qz(c, s, i): op("v", V.quantize_mx, 2, 0.015 + 0.0011 * c[2], c, s, i)
+    def qz(c, s, i): op("v", V.quantize_mx, 2, 0.015 + 0.00105 * c[2], c, s, i)
     def act(o, i, f, **kw): op("a", S.activation, 1, cc(o, i) if i[4] else CY * max(64, o[2]), o, i, f, **kw)
     def lin(o, i, m, c): act(o, i, F.Identity, scale=m, bias=c)
-    def iota(o, pat, base, cm): op("gp", g.iota, 1, 0.13 + 2 * CY * o[2], o, pat, base, cm, allow_small_or_imprecise_dtypes=True)
+    def iota(o, pat, base, cm): op("gp", g.iota, 1, 0.15 + 2 * CY * o[2], o, pat, base, cm, allow_small_or_imprecise_dtypes=True)
     def mm(o, w, ws, x, xs, start=True, stop=True): op("pe", g.tensor.matmul_mx, 1, 0.0006 * (o[2] + 16), o, w, ws, x, xs, start, stop, free=not start)
 
     def ts(o, i, s1, f0, s2=None, f1=None):
@@ -140,26 +139,41 @@ def rank_program(g, core, T, topo):
 
     def lay_out():
         n = len(nodes)
-        tail, outs, left = [0.0] * n, [[] for _ in nodes], [len(x["all"]) for x in nodes]
+        ins = [[(d, nodes[d]["lat"] + (WAKE if d in x["deps"] else 0.001)) for d in x["all"]] for x in nodes]
+        outs = [[] for _ in nodes]
+        for k in range(n):
+            for d, w in ins[k]:
+                outs[d].append((k, w))
+
+        def place(order, before, back):
+            end, used = [0.0] * n, {q: [] for q in Q}
+            for k in order:
+                x = nodes[k]
+                t = max([x["lat"] if back else 0.0] + [end[d] + w for d, w in before[k]])
+                if x["q"] != "far":
+                    u, i = used[x["q"]], 0
+                    while i < len(u) and u[i][0] < t + x["cost"]:
+                        t = max(t, u[i][1])
+                        i += 1
+                    u.insert(i, (t, t + x["cost"]))
+                end[k] = t + x["cost"]
+            return end
+
+        late = [0.0] * n
         for k in range(n - 1, -1, -1):
-            tail[k] += nodes[k]["cost"] + nodes[k]["lat"]
-            for d in nodes[k]["all"]:
-                tail[d] = max(tail[d], tail[k] + WAKE)
-                outs[d].append(k)
-        free, count, known, final = {}, {}, {q: {} for q in Q}, {}
-        ready, start = [k for k in range(n) if not left[k]], [0.0] * n
-        while ready:
-            k = min(ready, key=lambda i: (max(start[i], free.get(nodes[i]["q"], 0.0)), -tail[i], i))
-            q = nodes[k]["q"]
-            t0 = max(start[k], free.get(q, 0.0))
-            for i in ready:
-                if nodes[i]["q"] == q and tail[i] > tail[k] and start[i] < t0 + 0.6 * nodes[k]["cost"]:
-                    k = i
+            late[k] = nodes[k]["cost"] + max([nodes[k]["lat"]] + [late[i] + w for i, w in outs[k]])
+        best = None
+        for _ in range(PASSES):
+            end = place(sorted(range(n), key=lambda i: (-late[i], i)), ins, False)
+            span = max(end[k] + nodes[k]["lat"] for k in range(n))
+            if best is None or span < best[0]:
+                best = (span, end)
+            late = place(sorted(range(n), key=lambda i: (-end[i], -i)), outs, True)
+        count, known, final = {}, {q: {} for q in Q}, {}
+        for k in sorted(range(n), key=lambda i: (best[1][i] - nodes[i]["cost"], i)):
             x = nodes[k]
-            ready.remove(k)
-            t1 = max(start[k], free.get(q, 0.0)) + x["cost"]
+            q = x["q"]
             if q != "far":
-                free[q] = t1
                 need = {}
                 for d in x["deps"]:
                     e = nodes[d]["ev"]
@@ -173,11 +187,6 @@ def rank_program(g, core, T, topo):
                     x["ev"] = (q, count[q])
                 x["emit"]()
             final[x["ev"][0]] = max(final.get(x["ev"][0], 0), x["ev"][1])
-            for i in outs[k]:
-                start[i] = max(start[i], t1 + x["lat"] + WAKE)
-                left[i] -= 1
-                if not left[i]:
-                    ready.append(i)
         for s in sorted(final):
             g.sync.wait_ge(T.sem[s], final[s])
 
@@ -186,8 +195,9 @@ def rank_program(g, core, T, topo):
     def u32(x): return (x[0].bitcast(dt.uint32),) + x[1:]
     def C(k): return R("cf", k, k + 1)
     def quad(k): return (32 * k, 32 * k + 32)
-    (J, R16, SB, EB, P1, P6, E16, E33, NS, ROOT, PBIG, J32, PH, VV, VB, S20, N20, LE5, LO5, S10, NR,
-     T0, T1, T2, T3, T4, T5, T6, T7, T8, T9, TA, TB, TC) = range(34)
+    (J, R16, SB, EB, P1, P6, P14, E16, E33, NS, ROOT, NR, NRU, RHO, KC, IDX, OD, IB, VV, VB, PH, SC, ACC, T5,
+     T0, T1, T2, T3, T4, T6, T7, T8, T9, TA, TB, TC) = range(36)
+    OU, OL, OF, OK1, OK2 = [R("offk", a, b) for a, b in ((0, 8), (8, 9), (10, 11), (12, 14), (14, 16))]
 
     dma("sy", R("xt", 0, 640), H(T.x[:, 0:640]), 3.0)
     dma("a", R("xt", 640, 1280), H(T.x[:, 640:1280]), 3.0)
@@ -201,44 +211,38 @@ def rank_program(g, core, T, topo):
     dma("sy", R("sw"), H(T.ws[:]))
     dma("sy", R("vt"), H(T.v[:]))
     iota(R("ci", 7, 8), [[0, 1]], 0, 1)
-    iota(R("idn"), [[1, 128]], 0, -1)
+    iota(R("ct"), [[1, 516]], -3, -4)
     iota(R("iw"), [[1, 320]], 0, 0)
     iota(R("tab", 0, 10), [[16, 10]], 0, 0)
     iota(R("r32"), [[0, 5], [1, 32]], 0, 0)
-    iota(R("tab", 10, 30), [[0, 2], [1, 5], [0, 2]], 0, 0)
-    iota(R("tab", 30, 50), [[0, 2], [1, 5], [5, 2]], 0, 0)
-    iota(R("tab", 50, 70), [[0, 4], [32, 5]], -161, 0)
-    iota(R("tab", 70, 74), [[0, 2], [5, 2]], 0, 0)
-    for k, m in enumerate((31, 15, 32, 16, 1, 6)):
+    iota(R("tab", 16, 21), [[32, 5]], -161, 0)
+    for k, m in enumerate((31, 15, 32, 16, 1, 6, 14)):
         ts(R("ci", k, k + 1), R("ci", 7, 8), m, A.bitwise_and)
+    ts(R("ct"), R("ct"), 0.0, A.is_equal, 32.0, A.mult)
     for b in range(4):
-        ms(R("ct", 512 * b, 512 * b + 512), 0.0)
-        ts(R("ct", 513 * b, 512 * b + 512, 4), R("idn"), 0.0, A.is_equal, 32.0, A.mult)
-        qz(R("qc", 128 * b, 128 * b + 128), R("sc", 128 * b, 128 * b + 128), R("ct", 512 * b, 512 * b + 512))
-    cp(R("cf", 0, 6), R("ci", 0, 6))
-    ms(R("offu", 0, 4), 0)
-    ms(R("offu", 4, 8), 64)
+        qz(R("qc", 128 * b, 128 * b + 128), R("sc", 128 * b, 128 * b + 128), R("ct", 3 - b, 515 - b))
+    cp(R("cf", 0, 7), R("ci", 0, 7))
+    ms(R("offk", 0, 4), 0)
+    ms(R("offk", 4, 8), 64)
     ms(R("x0", 352, 384), 0.0)
-    ms(R("xa", 176, 192), 0.0)
-    ms(R("xb", 176, 192), 0.0)
+    for k in (0, 3):
+        ms(R("xj", 192 * k + 176, 192 * k + 192), 0.0)
     ms(R("d0", 0, 352, 2), 0.0)
-    ms(R("ones"), 1.0)
-    ms(R("dn"), -1.0 / 32)
     lin(C(E16), C(EB), -1.0, 16.0)
     lin(C(NS), C(SB), -5.0, 0.0)
     ts(C(ROOT), C(J), 0.0, A.is_equal)
     ts(C(NR), C(J), 0.0, A.not_equal)
-    lin(C(PBIG), C(NR), BIG, 0.0)
-    lin(C(J32), C(J), -1.0, 32.0)
+    lin(C(NRU), C(NR), U[1], 0.0)
     ts(R("ni"), R("iw", 0, 176), C(E16), A.add)
     lin(C(E33), C(E16), 2.0, 1.0)
     ts(R("ni"), R("ni"), 31, A.bitwise_and)
     ts(R("offa"), R("tab", 0, 10), C(R16), A.add, C(E16), A.add)
-    ts(R("n0"), R("ni"), C(J), A.not_equal, C(NR), A.mult)
-    ts(R("seg"), R("r32"), 0.0, A.not_equal)
+    ts(R("n0"), R("ni"), C(J), A.not_equal, C(NRU), A.mult)
+    lin(C(T5 + 20), C(ROOT), 255.0, 0.0)
+    lin(R("nb"), R("n0"), 1.0, C(T5 + 20))
     qz(R("qu"), R("su"), R("ut"))
-    cp(u32(R("qu2")), ind(R("qu"), R("offu"), dt.uint32))
-    act(R("su2"), ind(R("su"), R("offu")), F.Copy)
+    cp(u32(R("qu2")), ind(R("qu"), OU, dt.uint32))
+    act(R("su2"), ind(R("su"), OU), F.Copy)
     for k in range(2):
         qz(R("qx", 160 * k, 160 * k + 160), R("sx", 160 * k, 160 * k + 160), R("xt", 640 * k, 640 * k + 640))
     for k in range(4):
@@ -250,65 +254,79 @@ def rank_program(g, core, T, topo):
     act(R("d0", 1, 352, 2), R("r0"), F.Copy, scale=C(ROOT))
     act(R("r1"), R("r1"), F.Copy, scale=C(ROOT))
     tt(R("d1", 1, 352, 2), R("r1"), R("n0"), A.add)
-    for t in range(5):
-        ms(R("bt", t, t + 1), 33.0 * B0 * 64.0 ** t)
-        ms(R("bt", 24 + t, 44, 5), 64.0 ** -t / B0)
-    ts(R("dg"), R("r32"), C(J), A.not_equal, BIG, A.mult)
-    ms(R("md"), BIG)
+    lin(C(OD), C(EB), 1.0 / 16, 0.0)
+    lin(C(IB), C(SB), 1.0 / 32, 0.0)
+    lin(C(RHO), C(ROOT), 63.0 / 64, 0.0)
+    lin(C(KC), C(NR), U[3], 0.0)
+    lin(C(IDX), C(J), U[4], U[4])
+    for l in (1, 2, 3):
+        lin(C(TC + l), C(ROOT), 2.0, U[l] / 2)
+    ts(C(T0), C(R16), 1.0, A.add, C(OD), A.subtract)
+    ts(C(T1), C(P1), C(OD), A.is_equal)
+    lin(C(T0), C(T0), 16.0, 0.0)
+    ts(C(T1), C(T1), 176.0, A.mult, C(T0), A.add)
+    ts(OF, C(T1), 351.0, A.min)
     lin(C(TC), C(P1), 128.0, C(EB))
-    ts(R("offl", 0, 1), C(P6), 16.0, A.mult, C(TC), A.add)
-    lin(C(PH), C(EB), 1.0, 7.5)
-    ts(R("tab", 50, 70), R("tab", 50, 70), C(NS), A.subtract, 1.0 / 32, A.mult)
-    ts(C(T0), C(J), 17.0, A.is_ge, 17.0, A.mult)
-    ts(C(T1), C(J), 22.0, A.is_ge, 5.0, A.mult)
-    lin(C(S20), C(SB), 20.0 / 32, 0.0)
-    lin(C(LE5), C(SB), 5.0 / 32, 0.0)
-    lin(C(S10), C(SB), 10.0 / 32, 0.0)
-    lin(C(N20), C(SB), -20.0 / 32, 20.0)
-    lin(C(T9), C(SB), 1.0 / 32, 0.0)
-    ts(C(T2), C(T0), C(T1), A.add, 1.0, A.add)
-    ts(C(T3), C(T2), C(T9), A.mult, C(J), A.subtract)
-    lin(C(VV), C(T3), -1.0, 1.0)
-    lin(C(VB), C(T3), 1.0, -1.5)
-    ts(C(T4), C(R16), 1.0, A.is_ge, 10.0, A.mult)
-    ts(C(T5), C(R16), 6.0, A.is_ge, -5.0, A.mult)
-    ts(R("offc", 0, 10), R("tab", 30, 40), C(S10), A.add, C(S20), A.add)
-    ts(R("offc", 10, 20), R("tab", 40, 50), C(S10), A.add, C(N20), A.add)
-    ts(C(T6), C(T4), C(T5), A.add, 5.0, A.add)
-    lin(C(LO5), C(T6), C(T9), 0.0)
-    ts(R("offm", 0, 10, 2), R("tab", 10, 20, 2), C(LE5), A.add, C(S20), A.add)
-    ts(R("offm", 10, 20, 2), R("tab", 20, 30, 2), C(LE5), A.add, C(N20), A.add)
-    ts(R("offm", 1, 10, 2), R("tab", 11, 20, 2), C(LO5), A.add, C(S20), A.add)
-    ts(R("offm", 11, 20, 2), R("tab", 21, 30, 2), C(LO5), A.add, C(N20), A.add)
-    ts(R("offw", 0, 1), C(EB), 3.0, A.mult, C(R16), A.add)
-    ts(R("offw", 1, 2), C(E16), C(R16), A.add, 16.0, A.add)
-    ts(C(T7), C(R16), 5.0, A.is_ge)
-    lin(C(T8), C(T7), -5.0, C(R16))
-    ts(C(TA), C(T7), C(T9), A.not_equal, 20.0, A.mult)
-    ts(C(TB), C(TA), C(T8), A.add, C(S10), A.add)
-    ts(R("offq"), R("tab", 70, 74), C(TB), A.add)
-    ms(R("lw", 0, 144), 0.0)
+    ts(OL, C(P6), 16.0, A.mult, C(TC), A.add)
+    ms(R("seg"), 1.0)
+    ms(R("seg", 0, 160, 32), U[1])
+    ms(R("dn"), -1.0 / 32)
+    ms(R("de"), -1.0 / 64)
+    ts(R("yy"), R("r32"), C(J), A.is_equal, -1.0, A.mult)
+    lin(R("yo", 0, 160), R("r32"), -1.0 / 64, 3.0 + 31.5 / 64)
+    tt(R("thr"), R("yy"), R("yo", 0, 160), A.add)
+    iota(R("n0s"), [[0, 320]], 0, 0)
+    iota(R("n1s"), [[0, 320]], 1, 0)
+    ms(R("u0"), -0.25)
+    ms(R("u0", 0, 320, 64), -4.0)
+    iota(R("u1"), [[0, 1280]], -1, 0)
+    for l in range(4):
+        ms(R("up", 384 * l + 320, 384 * l + 384), -1.0)
+    ms(R("pj", 0, 16), 2.0)
+    iota(R("sl"), [[0, 320]], 0, 0)
+    iota(R("km"), [[0, 672]], 1, 0)
+    ms(R("km", 0, 672, 32), 0.0)
+    for k in (1, 3):
+        for x in SLOT[2:]:
+            ms(R("km", x, 672, 32, p=quad(k)), 0.0)
+    ts(C(T2), C(J), SLOT[2], A.is_ge, SLOT[2], A.mult)
+    ts(C(T3), C(J), SLOT[3], A.is_ge, SLOT[3] - SLOT[2], A.mult)
+    ts(C(T4), C(T2), C(T3), A.add, 1.0, A.add)
+    ts(C(T5), C(T4), C(IB), A.mult, C(J), A.subtract)
+    lin(C(VV), C(T5), -1.0, 1.0)
+    lin(C(VB), C(T5), 1.0, -1.5)
+    ms(R("e2", 0, 16), 0.0)
+    ms(R("pp", 0, 16), 0.0)
+    ms(R("pp", 336, 352), 0.0)
+    ms(R("rc", 0, 16), 0.0)
+    ms(R("rc", 336, 352), 0.0)
+    iota(R("m2"), [[0, 320]], 0, 0)
     ms(R("kq"), 0.0)
-    ms(R("cw", 40, 48), 0.0)
+    ms(R("lw", 0, 144), 0.0)
+    lin(C(PH), C(EB), 1.0, -353.0)
+    ts(C(T6), C(OD), C(IB), A.mult)
+    lin(C(SC), C(T6), 1.0 / U[4] - 32.0, 32.0)
+    ts(C(T7), C(P1), C(OD), A.not_equal)
+    lin(C(T8), C(OD), -1.0, 11.0)
+    lin(C(T9), C(P14), 0.5, 0.0)
+    ts(C(TA), C(T7), C(T8), A.mult, C(T9), A.add)
+    lin(C(T7), C(OD), 42.0, C(TA))
+    lin(C(T8), C(T6), -63.0, C(T7))
+    for k in range(2):
+        ts(R("offk", 12 + k, 13 + k), C(IB), 21.0, A.mult, C(T8), A.add) if k == 0 else ts(R("offk", 13, 14), R("offk", 12, 13), 8.0, A.add)
+    lin(C(TB), C(TA), 32.0, C(EB))
+    cp(R("offk", 14, 15), C(TB))
+    ts(R("offk", 15, 16), C(TB), 256.0, A.add, 671.0, A.min)
+    ts(R("tab", 24, 29), R("tab", 16, 21), C(NS), A.subtract, 1.0 / 32, A.mult)
+    ts(R("tab", 32, 37), R("tab", 16, 21), C(NS), A.subtract, U[4], A.mult)
     qz(R("qv"), R("sv"), R("vt"))
 
-    def wrap(src, out, add, o):
-        tr(R("w1", 64 * o, 64 * o + 32), R(src, 0, 32))
-        tr(R("w1", 64 * o + 32, 64 * o + 64), R(src, 16, 48))
-        cp(R("w2", 32 * o, 32 * o + 32), ind(R("w1", 64 * o, 64 * o + 64), R("offw")))
-        tr(R("w3", 32 * o, 32 * o + 32), R("w2", 32 * o, 32 * o + 32))
-        ts(R(out, 0, 20, 2), R("w3", 32 * o, 32 * o + 10), add, A.add)
-        ts(R(out, 1, 20, 2), R("w3", 32 * o + 16, 32 * o + 26), add, A.add)
-
-    def swap(out, a, b, f):
-        tt(R(out, 0, 20), R(*a), R(*b), f)
-        for k in range(4):
-            tt(R(out, 20, 40, p=quad(k ^ 1)), R(*a, p=quad(k)), R(*b, p=quad(k)), f)
-
     def E(b): return R("qc", 128 * b, 128 * b + 128), R("sc", 128 * b, 128 * b + 128)
-    def ends(n, a=0, k=5): return R(n, a + 31, a + 32 * k, 32)
+    def ends(n, a=0, k=5, p=(0, 128)): return R(n, a + 31, a + 32 * k, 32, p=p)
+    def last(n, a=0, p=(0, 128)): return R(n, a + 63, a + 320, 64, p=p)
     def run(n, k, w=1): return R(n, 160 * w * k, 160 * w * (k + 1))
     def bank(k, b, n=160): return R("pa" if k else "pb", 512 * b, 512 * b + n)
+    def col(n, k): return R(n, k, k + 1)
 
     for rnd in range(3):
         mate = T.cores[rank ^ PARTNER[rnd]]
@@ -334,102 +352,140 @@ def rank_program(g, core, T, topo):
             mm(bank(1, b, 320), *E(b), QL, SL)
             act(R("gw", 320 * b, 320 * b + 320), bank(1, b, 320), F.Copy, scale=2.0 ** -6)
             mm(bank(1, b), *E(b), run("qx", 1), run("sx", 1), True, False)
-        cur = "x0"
-        for steps in STEPS:
-            if cur == "x0":
-                tr(R("t1"), R("x0", 1, 384, 2))
-                tr(R("t2"), R("x0", 33, 353, 2))
-                act(R("xc"), R("x0", 1, 352, 2), F.Copy)
-                ts(R("offd", 0, 12, 2), R("t1", 0, 192, 32), 2.0, A.mult, C(E33), A.add)
-                ts(R("offd", 1, 11, 2), R("t2", 0, 160, 32), 2.0, A.mult, C(E33), A.add)
+        k = 0
+        for ph, steps in enumerate(STEPS):
+            o, f = 352 * ph, 12 * ph
+            if ph == 0:
+                tr(R("tw", 0, 192), R("x0", 1, 384, 2))
+                tr(R("tw", 192, 352), R("x0", 33, 353, 2))
+                base, win, m, e = R("nb"), R("x0", 0, 352), 2.0, C(E33)
             else:
-                tr(R("t1"), R(cur))
-                tr(R("t2"), R(cur, 16, 176))
-                act(R("xc"), R(cur, 0, 176), F.Copy)
-                ts(R("offd", 0, 12, 2), R("t1", 0, 192, 32), C(E16), A.add)
-                ts(R("offd", 1, 11, 2), R("t2", 0, 160, 32), C(E16), A.add)
+                a = 192 * (k - 1)
+                tr(R("tw", o, o + 192), R("xj", a, a + 192))
+                tr(R("tw", o + 192, o + 352), R("xj", a + 16, a + 176))
+                base, win, m, e = R("xc"), R("xj", a, a + 176), 1.0, C(E16)
+                act(base, win, F.Copy)
+            ts(R("offd", f, f + 12, 2), R("tw", o, o + 192, 32), m, A.mult, e, A.add)
+            ts(R("offd", f + 1, f + 11, 2), R("tw", o + 192, o + 352, 32), m, A.mult, e, A.add)
+            if ph == len(STEPS) - 1:
+                steps -= 1
+                ts(R("offd", 36, 52), ind(R("tw", o, o + 352), OF), e, A.add)
+                act(R("xu"), ind(win, R("offa")), F.Copy, scale=C(NR))
             for _ in range(steps):
-                nxt = "xb" if cur == "xa" else "xa"
-                tt(R(nxt, 0, 176), ind(R(cur, 0, 352 if cur == "x0" else 176), R("offd", 0, 11)), R("xc"), A.min)
-                cur = nxt
-        ts(R("ap"), ind(R(cur, 0, 176), R("offa")), C(PBIG), A.mult)
-        act(R("art"), ind(R(cur, 0, 176), R("offa")), F.Identity, scale=C(PBIG), bias=C(J32))
-        sc(R("cnt"), R("seg"), R("ap"), 0.0, A.mult, A.add)
-        tr(R("ar"), R("art"))
-        tt(R("ar1"), R("ar"), R("dg"), A.min)
+                tt(R("xj", 192 * k, 192 * k + 176), ind(win, R("offd", f, f + 11)), base, A.min)
+                win = R("xj", 192 * k, 192 * k + 176)
+                k += 1
+        tt(R("ap"), ind(win, R("offd", 36, 46)), R("xu"), A.min)
+        sc(R("cnt"), R("seg"), R("ap"), U[1], A.min, A.add)
+        tr(R("apt"), R("ap"))
+        ts(R("ar0"), R("apt"), -64.0, A.mult, 17.5 * U[1], A.add)
+        lin(R("arx"), R("apt"), -128.0, 4.0)
+        sc(R("ar"), R("arx"), R("thr"), 0.0, A.max, A.subtract)
+        lin(R("pj", 16, 176), R("ap"), 64.0, 2.0)
+        sc(R("dm"), R("pj", 16, 176), R("pj", 15, 175), 0.0, A.max, A.subtract)
+        act(R("dc"), R("dm"), F.Copy, scale=U[3])
+        ms(R("dc", 0, 160, 32), -4.0)
+        ms(R("dm", 0, 160, 32), -4.0)
+        lin(R("dm", 1, 160, 32), R("ap", 1, 160, 32), 64.0, 0.0)
         for l in range(4):
-            SG = R("sig", 5 * l, 5 * l + 5)
-            HF, HB = [R("sm", 40 * l + 8 * k, 40 * l + 8 * k + 5) for k in range(2)]
-            PRE, BASE = [R("smb", 24 * l + 8 * k, 24 * l + 8 * k + 5) for k in (0, 2)]
-            RE = R("re", 63, 320, 64)
+            U1 = 320 * l
             if l == 0:
-                ts(RE, ends("cnt"), 16.0 * BIG, A.is_le, 40.0, A.mult)
+                NV = R("sm", 0, 5)
+                lin(NV, ends("cnt"), 1.0, -33.0 * U[1])
+                ts(R("sm", 8, 13), ends("cnt"), 17.5 * U[1], A.is_le, 33.0 * U[1], A.mult)
+                tt(last("u0"), R("sm", 8, 13), NV, A.add)
                 for t in range(5):
-                    lin(R("smb", t, t + 1), R("cnt", 32 * t + 31, 32 * t + 32), B0 * 64.0 ** t / BIG, B0 * 64.0 ** t)
-                tt(SG, R("bt", 0, 5), PRE, A.subtract)
+                    ts(R("dy", 32 * t, 32 * t + 32), R("ar0", 32 * t, 32 * t + 32), col("cnt", 32 * t + 31), A.is_gt, col("cnt", 32 * t + 31), A.mult)
             else:
-                o = 24 * l - 8
+                o = 384 * (l - 1)
+                NV = last("up", o)
+                sc(R("yy"), R("dm"), R("up", o + 63, o + 383, 2), 0.0, A.add, A.max)
+                lin(last("n0s"), NV, -2.0, C(TC + l))
+                if l < 3:
+                    lin(last("n1s"), NV, 1.0 / 64, U[l] / 2)
+                    lin(R("sm", 16, 21), NV, 1.0 / 64, 0.0)
+                else:
+                    lin(last("n1s"), NV, 0.0, C(IDX))
+                ts(R("lf"), R("yy"), 0.0, A.is_equal, C(RHO), A.max)
+                tr(R("n0s", 0, 320, 2), R("lf"))
+                tr(R("n1s", 0, 320, 2), R("yy"))
+                sc(R("gg"), R("n0s"), R("n1s"), 0.0, A.add, A.min)
+                sc(R("dd"), R("de"), R("n0s", 0, 320, 2), 0.0, A.add, A.max)
                 for t in range(5):
-                    ts(R("yy", 32 * t, 32 * t + 32), R("ap", 32 * t, 32 * t + 32), R("kk", 32 * t + 31, 32 * t + 32), A.subtract, R("smb", o + t, o + t + 1), A.subtract)
-                tt(SG, ends("kk"), R("smb", o, o + 5), A.add)
-                tr(R("yt"), R("yy"))
-                lin(R("md", 63, 320, 64), SG, 2.03125, 40.0)
-                ts(R("keep"), R("yt"), 0.0, A.not_equal)
-                sc(R("nr", 0, 320, 2), R("keep"), R("yt"), 0.0, A.mult, A.min)
-                sc(R("nr", 1, 320, 2), R("keep"), R("ones", 0, 160), 1.0, A.mult, A.add)
-                sc(R("re"), R("md"), R("nr"), 0.0, A.add, A.min)
-                tt(PRE, R("bt", 0, 5), SG, A.subtract)
-            for t in range(5):
-                ts(R("dy", 32 * t, 32 * t + 32), R("ar1" if l else "ar", 32 * t, 32 * t + 32), R("re", 64 * t + 63, 64 * t + 64), A.is_lt, R("smb", 24 * l + t, 24 * l + t + 1), A.mult)
-            tr(run("dyt", l), R("dy"))
+                    ts(R("dy", 32 * t, 32 * t + 32), R("ar", 32 * t, 32 * t + 32), col("dd", 32 * t + 31), A.is_gt, col("gg", 64 * t + 63), A.mult)
+                if l < 3:
+                    tt(last("u0"), last("gg"), R("sm", 16, 21), A.max)
+                else:
+                    lin(last("u0"), NV, 0.0, C(KC))
+            DT = R("u1", U1, U1 + 320, 2)
+            tr(DT, R("dy"))
+            sc(R("up", 384 * l, 384 * l + 320), R("u0"), R("u1", U1, U1 + 320), 0.0, A.subtract, A.max)
+            for k in range(4):
+                d, b = 2 * (k // 2) + min(l, 1), 160 * (k % 2) + SLOT[l]
+                src = NV[1][0]
+                i, o = R(src[0], src[3], src[4], src[5], p=quad(k)), R("sl", b, b + 160 - SLOT[l], 32, p=quad(d))
+                if k % 2 and l == 3:
+                    ts(o, i, -1.0 / U[l], A.mult)
+                else:
+                    act(o, i, F.Copy, scale=-1.0 / U[l])
             if l < 3:
-                ts(HF, RE, 0.0, A.is_gt)
-                tt(HB, HF, R("bt", 0, 5), A.mult)
-                tt(BASE, SG, HB, A.subtract)
-                sc(R("kk"), R("seg"), run("dyt", l), 0.0, A.mult, A.max)
-            act(run("z0", l), run("dyt", l), F.Sign, bias=-0.5)
-            sc(run("rho", l), R("dn"), run("z0", l), -1.0, A.add, A.max)
-            for t in range(5):
-                o = 160 * l + 32 * t
-                act(R("y2", o, o + 32), R("ap", 32 * t, 32 * t + 32), F.Identity, scale=-1.0, bias=R("rho", o + 31, o + 32))
-            tr(run("y2t", l), run("y2", l))
-            act(run("k3", l), run("y2t", l), F.Sign, scale=-1.0, bias=1.0 / 64)
-            sc(run("xs", l), run("k3", l), run("y2t", l), 0.0, A.mult, A.max)
-        swap("swn", ("sig", 0, 20), ("bt", 24, 44), A.mult)
-        act(R("mm"), ind(R("swn"), R("offm")), F.Copy)
+                act(run("z0", l), DT, F.Sign, bias=-U[4] / 4)
+                sc(run("rho", l), R("dn"), run("z0", l), -1.0, A.add, A.max)
+                for t in range(5):
+                    o = 160 * l + 32 * t
+                    act(R("y2", o, o + 32), R("ap", 32 * t, 32 * t + 32), F.Identity, scale=-128.0, bias=col("rho", o + 31))
+                tr(run("y2t", l), run("y2", l))
+                act(run("k3", l), run("y2t", l), F.Sign, scale=-1.0, bias=1.0 / 64)
+                sc(run("xs", l), run("k3", l), run("y2t", l), 0.0, A.mult, A.max)
+            else:
+                sc(run("y2", l), R("dc"), R("up", 384 * l + 63, 384 * l + 383, 2), 0.0, A.add, A.max)
+                tr(run("y2t", l), run("y2", l))
+                ts(run("k3", l), run("y2t", l), 0.0, A.is_ge)
+                sc(run("xs", l), run("k3", l), run("y2t", l), 0.0, A.mult, A.min)
+            if l < 3:
+                tt(R("sm", 24 + 8 * l, 29 + 8 * l), ends("xs", 160 * l), R("tab", 24, 29), A.add)
+            for k in range(4):
+                d, b = 2 * (k // 2) + l // 2, 160 * (k % 2) + 16 * (l % 2)
+                o = R("m2", b, 160 * (k % 2) + 160, 32, p=quad(d))
+                if l < 3:
+                    act(o, R("sm", 24 + 8 * l, 29 + 8 * l, p=quad(k)), F.Copy)
+                else:
+                    tt(o, R("tab", 32, 37, p=quad(k)), ends("xs", 160 * l, p=quad(k)), A.subtract)
+        sc(R("mm"), R("km", 0, 320), R("sl"), 0.0, A.mult, A.add)
         tr(R("rs"), R("mm"))
-        act(R("sg"), R("rs"), F.Sign, bias=C(VB), accum_out=R("acc", 0, 1))
-        ts(R("i2"), R("rs"), C(VV), A.is_equal, 2.0, A.mult)
-        sc(R("pp"), R("ones"), R("i2"), R("acc", 0, 1), A.mult, A.add)
-        act(R("ng"), R("i2"), F.Copy, scale=-512.0)
-        tr(R("ppt"), R("pp"))
-        tr(R("ngt"), R("ng"))
-        sc(R("ps"), R("ngt"), R("ppt"), 0.0, A.add, A.max)
-        ts(R("kq", 0, 10), ends("ps", 0, 10), 0.5, A.mult, 151.5, A.add)
-        ts(R("kq", 32, 42), ends("ps", 0, 10), 0.5, A.mult, 151.5, A.add)
-        for h in range(2):
-            ts(R("kq", 16, 26, p=quad(2 * h)), R("ps", 16, 320, 32, p=quad(2 * h + 1)), 0.5, A.mult, 151.5, A.add)
-            ts(R("kq", 16, 26, p=quad(2 * h + 1)), R("ps", 21, 320, 32, p=quad(2 * h + 1)), 0.5, A.mult, 151.5, A.add)
-        wrap("kq", "offs", C(PH), 0)
-        swap("cw", ("xs", 31, 640, 32), ("tab", 50, 70), A.add)
-        act(R("m2"), ind(R("cw"), R("offc")), F.Copy)
-        tr(R("rc"), R("m2"))
-        cp(ind(R("lw"), R("offs")), R("rc"))
+        act(R("sg"), R("rs"), F.Sign, bias=C(VB), accum_out=C(ACC))
+        ts(R("e1"), R("rs"), C(VV), A.is_equal, 1026.0, A.mult)
+        ts(R("e2", 16, 336), R("rs"), C(VV), A.is_equal, 1024.0, A.mult)
+        sc(R("pp", 16, 336), R("e1"), R("e2", 15, 335), C(ACC), A.add, A.subtract)
+        tr(R("pq", 0, 320), R("pp", 16, 336))
+        tr(R("pq", 320, 672), R("pp"))
+        sc(R("ps", 0, 320), R("km", 0, 320), R("pq", 0, 320), 0.0, A.mult, A.max)
+        sc(R("ps", 320, 672), R("km", 320, 672), R("pq", 320, 672), 0.0, A.mult, A.max)
+        cp(R("kq", 0, 21), R("ps", 31, 672, 32))
+        act(R("kq", 21, 42), R("ps", SLOT[3] - 1, 672, 32), F.Copy)
+        cp(R("kq", 42, 63, p=quad(0)), R("ps", SLOT[2] - 1, 672, 32, p=quad(1)))
+        act(R("kq", 42, 63, p=quad(2)), R("ps", SLOT[2] - 1, 672, 32, p=quad(3)), F.Copy)
+        ts(R("offs"), ind(R("kq"), OK1), 0.5, A.mult, C(PH), A.add)
+        RC = R("rc", 16, 336)
+        tr(RC, R("m2"))
+        cp(ind(R("lw"), R("offs", 0, 20)), RC)
         tr(R("lt", 0, 128), R("lw", 0, 128))
         tr(R("lt", 128, 256), R("lw", 16, 144))
-        ts(LO, ind(R("lt"), R("offl", 0, 1)), 32.0, A.mult, 160.0, A.add)
+        ts(LO, ind(R("lt"), OL), C(SC), A.mult, 160.0, A.add)
         LO = R("lo%d" % rnd, 0, 8)
         send(mate, LI, LO, "rl%d" % rnd, "ol%d" % rnd, FAR)
         for b in range(4):
             act(R("he", 128 * b, 128 * b + 128), ind(R("zw", 448 * b + 128, 448 * b + 448), LO), F.Copy, scale=0.5)
-        ts(R("cq"), ind(R("cw"), R("offq", 0, 3)), 32.0, A.mult, 280.5, A.add)
-        ts(R("zq", 0, 48), R("kq"), 120.0, A.is_gt)
-        tt(R("cq"), R("cq"), R("kq"), A.subtract)
-        tt(R("zq", 48, 96), R("cq"), R("zq", 0, 48), A.mult)
-        tt(R("wz"), R("zq", 48, 96), R("kq"), A.add)
-        wrap("wz", "offz", 7.5, 1)
+        tr(R("rt", 0, 320), RC)
+        tr(R("rt", 320, 672), R("rc"))
+        ts(R("wz", 0, 32), ind(R("rt"), OK2), C(SC), A.mult, 288.0, A.add)
+        ts(R("wz", 32, 64), ind(R("kq"), OK1), 0.5, A.mult, -353.0, A.add)
+        ts(R("wz", 64, 96), R("wz", 32, 64), -127.5, A.add, 1024.0, A.mult)
+        tt(R("wz", 96, 128), R("wz", 32, 64), R("wz", 64, 96), A.max)
+        tt(R("wz", 128, 160), R("wz", 96, 128), R("wz", 0, 32), A.min)
+        cp(R("offz"), R("wz", 128, 160))
         if rnd == 2:
-            lin(R("rcf"), R("rc"), 32.0, 160.0)
+            lin(R("rcf"), RC, C(SC), 160.0)
             for k in range(8):
                 dma("sy", H(T.cl[k:k + 1, :]), R("rcf", p=(16 * k, 16 * k + 1)))
         for b in range(4):

@@ -15,7 +15,7 @@ _S = {
     "ss": (320, F32), "sb": (176, F32), "d0": (352, BF), "d1": (352, BF), "x0": (384, BF), "xj": (6 * 192, BF),
     "tw": (3 * 352, BF), "xu": (160, BF), "xc": (176, BF), "nb": (176, BF), "r0": (176, F32), "r1": (176, F32), "n0": (176, F32),
     "ap": (160, BF), "apt": (160, BF), "ar0": (160, BF), "arx": (160, BF), "ar": (160, BF), "thr": (160, F16), "pj": (176, BF),
-    "dm": (160, BF), "dc": (160, BF), "r32": (160, BF), "seg": (160, BF), "dn": (160, BF), "de": (160, BF),
+    "dm": (160, BF), "dr": (160, BF), "fl": (160, BF), "ao": (160, BF), "dc": (160, BF), "r32": (160, BF), "seg": (160, BF), "dn": (160, BF), "de": (160, BF),
     "cnt": (160, BF), "yy": (160, BF), "lf": (160, BF), "n0s": (320, BF), "n1s": (320, BF), "gg": (320, BF), "dd": (160, BF),
     "dy": (160, BF), "u0": (320, BF), "u1": (4 * 320, BF), "up": (4 * 384, BF), "sm": (64, BF),
     "z0": (480, BF), "rho": (480, BF), "y2": (640, BF), "y2t": (640, BF), "k3": (640, BF), "xs": (640, BF),
@@ -37,10 +37,11 @@ SCRATCH["pb"] = ("psum", [128, 2048], F32)
 SEMAPHORES = ["v", "a", "pe", "gp"] + ["m%d" % i for i in range(32)] + ["%s%d" % (n, t) for n in ("rq", "rs", "rl", "oq", "os", "ol") for t in range(3)]
 U = [2.0 ** -6, 2.0 ** -6, 2.0 ** -12, 2.0 ** -18, 2.0 ** -24]
 SLOT = (0, 0, 17, 26)
-CY, WAKE, FAR = 0.001, 0.1, 2.0
+TINY = 2.0 ** -60
+CY, WAKE, FAR = 0.00083, 0.2, 1.1
 PASSES = 6
 STEPS = (1, 3, 3)
-ZV, XV = (3, 6, 7), (1, 3, 5, 7)
+ZV, XV = (2, 3, 7), (1, 3, 5, 7)
 
 
 def rank_program(g, core, T, topo):
@@ -114,7 +115,7 @@ def rank_program(g, core, T, topo):
     def tr(o, i): op("v", V.transpose, 1, cc(o, i), o, i)
     def ms(o, c): op("v", V.memset, 1, cc(o, o), o, c)
     def sc(o, a, b, i, f0, f1): op("v", V.tensor_tensor_scan, 1, cc(o, a, b), o, a, b, i, f0, f1)
-    def qz(c, s, i): op("v", V.quantize_mx, 2, 0.015 + 0.00105 * c[2], c, s, i)
+    def qz(c, s, i): op("v", V.quantize_mx, 2, 0.012 + 0.00088 * c[2], c, s, i)
     def act(o, i, f, **kw): op("a", S.activation, 1, cc(o, i) if i[4] else CY * max(64, o[2]), o, i, f, **kw)
     def lin(o, i, m, c): act(o, i, F.Identity, scale=m, bias=c)
     def iota(o, pat, base, cm): op("gp", g.iota, 1, 0.15 + 2 * CY * o[2], o, pat, base, cm, allow_small_or_imprecise_dtypes=True)
@@ -196,7 +197,7 @@ def rank_program(g, core, T, topo):
     def C(k): return R("cf", k, k + 1)
     def quad(k): return (32 * k, 32 * k + 32)
     (J, R16, SB, EB, P1, P6, P14, E16, E33, NS, ROOT, NR, NRU, RHO, KC, IDX, OD, IB, VV, VB, PH, SC, ACC, T5,
-     T0, T1, T2, T3, T4, T6, T7, T8, T9, TA, TB, TC) = range(36)
+     T0, T1, T2, T3, T4, T6, T7, T8, T9, TA, TB, TC, FL, NB, LV) = range(39)
     OU, OL, OF, OK1, OK2 = [R("offk", a, b) for a, b in ((0, 8), (8, 9), (10, 11), (12, 14), (14, 16))]
 
     dma("sy", R("xt", 0, 640), H(T.x[:, 0:640]), 3.0)
@@ -207,15 +208,15 @@ def rank_program(g, core, T, topo):
     dma("sy", R("pt", 0, 20, p=(16, 32)), H(T.p0[:]))
     dma("a", R("pt", 25, 45, p=(0, 16)), H(T.p1[:]))
     dma("sy", R("pt", 24, 44, p=(16, 32)), H(T.p1[:]))
-    dma("sy", u8(R("qw")), H(T.wc[:]))
-    dma("sy", R("sw"), H(T.ws[:]))
-    dma("sy", R("vt"), H(T.v[:]))
+    dma("sy", u8(R("qw")), (T.wc[:], R("xt")[1]))
+    dma("sy", R("sw"), (T.ws[:], R("xt")[1]))
+    dma("sy", R("vt"), (T.v[:], R("xt")[1]))
     iota(R("ci", 7, 8), [[0, 1]], 0, 1)
     iota(R("ct"), [[1, 516]], -3, -4)
     iota(R("iw"), [[1, 320]], 0, 0)
     iota(R("tab", 0, 10), [[16, 10]], 0, 0)
     iota(R("r32"), [[0, 5], [1, 32]], 0, 0)
-    iota(R("tab", 16, 21), [[32, 5]], -161, 0)
+    iota(R("tab", 16, 21), [[32, 5]], 0, 0)
     for k, m in enumerate((31, 15, 32, 16, 1, 6, 14)):
         ts(R("ci", k, k + 1), R("ci", 7, 8), m, A.bitwise_and)
     ts(R("ct"), R("ct"), 0.0, A.is_equal, 32.0, A.mult)
@@ -238,8 +239,8 @@ def rank_program(g, core, T, topo):
     ts(R("ni"), R("ni"), 31, A.bitwise_and)
     ts(R("offa"), R("tab", 0, 10), C(R16), A.add, C(E16), A.add)
     ts(R("n0"), R("ni"), C(J), A.not_equal, C(NRU), A.mult)
-    lin(C(T5 + 20), C(ROOT), 255.0, 0.0)
-    lin(R("nb"), R("n0"), 1.0, C(T5 + 20))
+    lin(C(NB), C(ROOT), 255.0, 0.0)
+    lin(R("nb"), R("n0"), 1.0, C(NB))
     qz(R("qu"), R("su"), R("ut"))
     cp(u32(R("qu2")), ind(R("qu"), OU, dt.uint32))
     act(R("su2"), ind(R("su"), OU), F.Copy)
@@ -256,11 +257,19 @@ def rank_program(g, core, T, topo):
     tt(R("d1", 1, 352, 2), R("r1"), R("n0"), A.add)
     lin(C(OD), C(EB), 1.0 / 16, 0.0)
     lin(C(IB), C(SB), 1.0 / 32, 0.0)
-    lin(C(RHO), C(ROOT), 63.0 / 64, 0.0)
+    lin(C(RHO), C(ROOT), 63.5, 0.5)
+    lin(C(FL), C(ROOT), 1.0, TINY)
+    lin(C(LV + 3), C(NR), 1.0 / TINY, 1.0)
     lin(C(KC), C(NR), U[3], 0.0)
     lin(C(IDX), C(J), U[4], U[4])
     for l in (1, 2, 3):
-        lin(C(TC + l), C(ROOT), 2.0, U[l] / 2)
+        lin(C(LV + 5 * l), C(ROOT), 4.0, U[l])
+        lin(C(LV + 5 * l + 1), C(RHO), -U[l] / 64, U[l] / 2)
+        lin(C(LV + 5 * l + 2), C(RHO), U[l], 0.0)
+        lin(C(LV + 5 * l + 3), C(NR), (2.0 - 1.0 / 64) / U[l], 1.0 / 64 / U[l])
+        lin(C(LV + 5 * l + 4), C(ROOT), -63.5 * U[l], 0.0)
+    lin(C(LV), C(RHO), U[1], -33.0 * U[1])
+    ms(R("fl"), 0.0)
     ts(C(T0), C(R16), 1.0, A.add, C(OD), A.subtract)
     ts(C(T1), C(P1), C(OD), A.is_equal)
     lin(C(T0), C(T0), 16.0, 0.0)
@@ -317,8 +326,6 @@ def rank_program(g, core, T, topo):
     lin(C(TB), C(TA), 32.0, C(EB))
     cp(R("offk", 14, 15), C(TB))
     ts(R("offk", 15, 16), C(TB), 256.0, A.add, 671.0, A.min)
-    ts(R("tab", 24, 29), R("tab", 16, 21), C(NS), A.subtract, 1.0 / 32, A.mult)
-    ts(R("tab", 32, 37), R("tab", 16, 21), C(NS), A.subtract, U[4], A.mult)
     qz(R("qv"), R("sv"), R("vt"))
 
     def E(b): return R("qc", 128 * b, 128 * b + 128), R("sc", 128 * b, 128 * b + 128)
@@ -343,7 +350,8 @@ def rank_program(g, core, T, topo):
             mm(bank(0, b), *E(b), run("qx", 0), run("sx", 0), True, False)
         for b in range(4):
             act(R("tt", b, 1280, 4), bank(1, b, 320), F.Copy, scale=2.0 ** -5)
-        qz(QT, ST, R("tt"))
+        for k in range(2):
+            qz(run("qt%d" % rnd, k), run("st%d" % rnd, k), run("tt", k, 4))
         send(mate, QL, QT, "rq%d" % rnd, "oq%d" % rnd, FAR + 9.0, True)
         send(mate, SL, ST, "rs%d" % rnd, "os%d" % rnd, FAR + 9.0)
         for b in range(4):
@@ -381,32 +389,40 @@ def rank_program(g, core, T, topo):
         ts(R("ar0"), R("apt"), -64.0, A.mult, 17.5 * U[1], A.add)
         lin(R("arx"), R("apt"), -128.0, 4.0)
         sc(R("ar"), R("arx"), R("thr"), 0.0, A.max, A.subtract)
-        lin(R("pj", 16, 176), R("ap"), 64.0, 2.0)
+        ts(R("pj", 16, 176), R("ap"), 64.0, A.mult, 2.0, A.add)
         sc(R("dm"), R("pj", 16, 176), R("pj", 15, 175), 0.0, A.max, A.subtract)
         act(R("dc"), R("dm"), F.Copy, scale=U[3])
         ms(R("dc", 0, 160, 32), -4.0)
+        ts(R("dr"), R("dm"), -1.0 / TINY, A.mult, 1.0, A.add)
+        ts(R("dr"), R("dr"), TINY, A.max)
+        ms(R("dr", 0, 160, 32), 0.0)
         ms(R("dm", 0, 160, 32), -4.0)
-        lin(R("dm", 1, 160, 32), R("ap", 1, 160, 32), 64.0, 0.0)
+        ts(R("sm", 48, 53), R("ap", 1, 160, 32), 0.0, A.is_equal, TINY, A.max)
+        for t in range(5):
+            lin(R("ao", 32 * t, 32 * t + 32), R("ap", 32 * t, 32 * t + 32), -128.0, float(t))
         for l in range(4):
             U1 = 320 * l
             if l == 0:
-                NV = R("sm", 0, 5)
-                lin(NV, ends("cnt"), 1.0, -33.0 * U[1])
-                ts(R("sm", 8, 13), ends("cnt"), 17.5 * U[1], A.is_le, 33.0 * U[1], A.mult)
-                tt(last("u0"), R("sm", 8, 13), NV, A.add)
+                NV = ends("cnt")
+                lin(last("u1"), NV, 1.0, C(LV))
+                lin(R("sm", 0, 5), NV, 1.0, C(LV + 7))
+                ts(R("sm", 8, 13), NV, 17.5 * U[1], A.is_gt, -1.0, A.mult)
+                tt(last("u0"), R("sm", 8, 13), R("sm", 0, 5), A.add)
                 for t in range(5):
                     ts(R("dy", 32 * t, 32 * t + 32), R("ar0", 32 * t, 32 * t + 32), col("cnt", 32 * t + 31), A.is_gt, col("cnt", 32 * t + 31), A.mult)
             else:
                 o = 384 * (l - 1)
                 NV = last("up", o)
+                lin(R("dm", 1, 160, 32), R("ap", 1, 160, 32), 64.0, C(LV + 5 * l + 4))
+                act(R("dr", 1, 160, 32), R("sm", 48, 53), F.Copy, scale=C(LV + 5 * l + 3))
+                sc(R("lf"), R("dr"), R("up", o + 63, o + 383, 2), 0.0, A.mult, A.max)
                 sc(R("yy"), R("dm"), R("up", o + 63, o + 383, 2), 0.0, A.add, A.max)
-                lin(last("n0s"), NV, -2.0, C(TC + l))
+                lin(last("n0s"), NV, -2.0, C(LV + 5 * l))
                 if l < 3:
-                    lin(last("n1s"), NV, 1.0 / 64, U[l] / 2)
-                    lin(R("sm", 16, 21), NV, 1.0 / 64, 0.0)
+                    lin(last("n1s"), NV, 1.0 / 64, C(LV + 5 * l + 1))
+                    lin(last("u1", U1), NV, 1.0 / 64, 0.0)
                 else:
                     lin(last("n1s"), NV, 0.0, C(IDX))
-                ts(R("lf"), R("yy"), 0.0, A.is_equal, C(RHO), A.max)
                 tr(R("n0s", 0, 320, 2), R("lf"))
                 tr(R("n1s", 0, 320, 2), R("yy"))
                 sc(R("gg"), R("n0s"), R("n1s"), 0.0, A.add, A.min)
@@ -414,9 +430,13 @@ def rank_program(g, core, T, topo):
                 for t in range(5):
                     ts(R("dy", 32 * t, 32 * t + 32), R("ar", 32 * t, 32 * t + 32), col("dd", 32 * t + 31), A.is_gt, col("gg", 64 * t + 63), A.mult)
                 if l < 3:
-                    tt(last("u0"), last("gg"), R("sm", 16, 21), A.max)
+                    lin(last("u0"), last("gg"), 1.0, C(LV + 5 * l + 7))
                 else:
-                    lin(last("u0"), NV, 0.0, C(KC))
+                    act(R("dr", 1, 160, 32), R("sm", 48, 53), F.Copy, scale=C(LV + 3))
+                    ts(R("fl", 0, 160, 32), last("gg"), 0.0, A.is_gt, C(FL), A.mult)
+                    sc(R("lf"), R("dr"), R("fl"), 0.0, A.mult, A.max)
+                    tr(run("k3", l), R("lf"))
+                    lin(last("u0"), R("tab", 16, 21), -U[4], C(KC))
             DT = R("u1", U1, U1 + 320, 2)
             tr(DT, R("dy"))
             sc(R("up", 384 * l, 384 * l + 320), R("u0"), R("u1", U1, U1 + 320), 0.0, A.subtract, A.max)
@@ -424,33 +444,35 @@ def rank_program(g, core, T, topo):
                 d, b = 2 * (k // 2) + min(l, 1), 160 * (k % 2) + SLOT[l]
                 src = NV[1][0]
                 i, o = R(src[0], src[3], src[4], src[5], p=quad(k)), R("sl", b, b + 160 - SLOT[l], 32, p=quad(d))
+                c = R("cf", RHO, RHO + 1, p=quad(k)) if l else 33.0
                 if k % 2 and l == 3:
-                    ts(o, i, -1.0 / U[l], A.mult)
+                    ts(o, i, -1.0 / U[l], A.mult, c, A.add)
                 else:
-                    act(o, i, F.Copy, scale=-1.0 / U[l])
+                    lin(o, i, -1.0 / U[l], c)
             if l < 3:
                 act(run("z0", l), DT, F.Sign, bias=-U[4] / 4)
                 sc(run("rho", l), R("dn"), run("z0", l), -1.0, A.add, A.max)
                 for t in range(5):
                     o = 160 * l + 32 * t
-                    act(R("y2", o, o + 32), R("ap", 32 * t, 32 * t + 32), F.Identity, scale=-128.0, bias=col("rho", o + 31))
+                    act(R("y2", o, o + 32), R("ao", 32 * t, 32 * t + 32), F.Identity, bias=col("rho", o + 31))
                 tr(run("y2t", l), run("y2", l))
-                act(run("k3", l), run("y2t", l), F.Sign, scale=-1.0, bias=1.0 / 64)
+                for t in range(5):
+                    o = 160 * l + 32 * t
+                    act(R("k3", o, o + 32), R("y2t", o, o + 32), F.Sign, scale=-1.0, bias=t + 1.0 / 64)
                 sc(run("xs", l), run("k3", l), run("y2t", l), 0.0, A.mult, A.max)
             else:
                 sc(run("y2", l), R("dc"), R("up", 384 * l + 63, 384 * l + 383, 2), 0.0, A.add, A.max)
                 tr(run("y2t", l), run("y2", l))
-                ts(run("k3", l), run("y2t", l), 0.0, A.is_ge)
-                sc(run("xs", l), run("k3", l), run("y2t", l), 0.0, A.mult, A.min)
-            if l < 3:
-                tt(R("sm", 24 + 8 * l, 29 + 8 * l), ends("xs", 160 * l), R("tab", 24, 29), A.add)
+                sc(run("xs", l), run("k3", l), run("y2t", l), 0.0, A.add, A.min)
             for k in range(4):
                 d, b = 2 * (k // 2) + l // 2, 160 * (k % 2) + 16 * (l % 2)
                 o = R("m2", b, 160 * (k % 2) + 160, 32, p=quad(d))
                 if l < 3:
-                    act(o, R("sm", 24 + 8 * l, 29 + 8 * l, p=quad(k)), F.Copy)
+                    lin(o, ends("xs", 160 * l, p=quad(k)), 1.0, (160.0 * (k % 2) - 161.0) / 32)
+                elif k % 2:
+                    lin(o, ends("xs", 160 * l, p=quad(k)), -1.0, -U[4])
                 else:
-                    tt(o, R("tab", 32, 37, p=quad(k)), ends("xs", 160 * l, p=quad(k)), A.subtract)
+                    ts(o, ends("xs", 160 * l, p=quad(k)), -1.0, A.mult, -161.0 * U[4], A.add)
         sc(R("mm"), R("km", 0, 320), R("sl"), 0.0, A.mult, A.add)
         tr(R("rs"), R("mm"))
         act(R("sg"), R("rs"), F.Sign, bias=C(VB), accum_out=C(ACC))

@@ -6,17 +6,17 @@ BF, F32, F16, U16, I32, X4, U8 = "bfloat16", "float32", "float16", "uint16", "in
 PARTNER = [1, 2, 4]
 _S = {
     "xt": (1280, BF), "ut": (512, BF), "vt": (512, BF), "ct": (516, BF), "tt": (1280, BF), "zt": (1280, BF),
-    "qx": (320, X4), "sx": (320, U8), "qu": (128, X4), "su": (128, U8), "qu2": (128, X4), "su2": (128, U8),
+    "qx": (320, X4), "sx": (320, U8), "qu": (128, X4), "su": (128, U8),
     "qv": (128, X4), "sv": (128, U8), "qw": (512, X4), "sw": (512, U8), "qc": (512, X4), "sc": (512, U8),
     "qz": (320, X4), "sz": (320, U8),
     "zw": (1792, BF), "gw": (1280, BF), "he": (512, BF), "yo": (320, F32),
-    "pt": (48, I32), "ci": (8, I32), "cf": (64, F32), "tab": (48, F32), "iw": (320, F32), "ni": (176, I32),
-    "offk": (16, U16), "offp": (36, U16), "offd": (52, U16), "offa": (10, U16), "offs": (32, U16), "offz": (32, U16),
-    "ss": (320, F32), "sb": (176, F32), "d0": (352, BF), "d1": (352, BF), "x0": (384, BF), "xj": (6 * 192, BF),
-    "tw": (3 * 352, BF), "xu": (160, BF), "xc": (176, BF), "nb": (176, BF), "r0": (176, F32), "r1": (176, F32), "n0": (176, F32),
-    "ap": (160, BF), "apt": (160, BF), "ar0": (160, BF), "arx": (160, BF), "ar": (160, BF), "thr": (160, F16), "pj": (176, BF),
+    "pt": (40, I32), "ci": (8, I32), "cf": (64, F32), "tab": (16, F32), "iw": (320, F32),
+    "offk": (24, U16), "offp": (32, U16), "offd": (144, U16), "offs": (32, U16), "offz": (32, U16),
+    "ss": (320, F32), "sb": (160, F32), "d0": (320, BF), "d1": (320, BF), "x0": (448, BF), "xj": (6 * 224, BF),
+    "tw": (3 * 416, BF), "xc": (320, BF), "nb": (160, BF), "r0": (160, F32), "r1": (160, F32), "n0": (160, F32),
+    "ap": (176, BF), "apt": (160, BF), "w0": (320, BF), "b0": (160, BF), "arx": (160, BF), "ar": (160, BF), "thr": (160, F16), "pj": (160, BF),
     "dm": (160, BF), "dr": (160, BF), "fl": (160, BF), "ao": (160, BF), "dc": (160, BF), "r32": (160, BF), "seg": (160, BF), "dn": (160, BF), "de": (160, BF),
-    "cnt": (160, BF), "yy": (160, BF), "lf": (160, BF), "n0s": (320, BF), "n1s": (320, BF), "gg": (320, BF), "dd": (160, BF),
+    "cnt": (192, BF), "yy": (160, BF), "lf": (160, BF), "n0s": (320, BF), "n1s": (320, BF), "gg": (320, BF), "dd": (160, BF),
     "dy": (160, BF), "u0": (320, BF), "u1": (4 * 320, BF), "up": (4 * 384, BF), "sm": (64, BF),
     "z0": (480, BF), "rho": (480, BF), "y2": (640, BF), "y2t": (640, BF), "k3": (640, BF), "xs": (640, BF),
     "sl": (320, BF), "km": (672, BF), "mm": (320, BF), "rs": (320, BF), "sg": (320, BF),
@@ -39,7 +39,10 @@ U = [2.0 ** -6, 2.0 ** -6, 2.0 ** -12, 2.0 ** -18, 2.0 ** -24]
 SLOT = (0, 0, 17, 26)
 TINY = 2.0 ** -60
 CY, WAKE, FAR = 0.00083, 0.2, 1.1
-PASSES = 6
+NEAR, RATE = 1.0, 250.0
+PASSES = 8
+LANES = ((0, 3), (3, 5))
+LL = (((0, 2), (2, 5)),) * 3 + (((0, 5),),)
 STEPS = (1, 3, 3)
 ZV, XV = (2, 3, 7), (1, 3, 5, 7)
 
@@ -70,7 +73,7 @@ def rank_program(g, core, T, topo):
         return (x[3] - y[3]) % math.gcd(x[5], y[5]) == 0
 
     def node(q, reads, writes, emit, cost, lat=0.0, ev=None, free=False, after=()):
-        me, deps, soft = len(nodes), set(after), set()
+        me, deps, soft = len(nodes), set(), set(after)
         for regs, wr in ((reads, False), (writes, True)):
             for x in regs:
                 psum = x[0] in ("pa", "pb")
@@ -127,27 +130,29 @@ def rank_program(g, core, T, topo):
         else:
             op("v", V.tensor_scalar, 1, cc(o, i), o, i, s1, s2, f0, f1)
 
-    def dma(q, o, i, lat=2.0):
+    def dma(q, o, i, kb=4, after=()):
         ev = ("m%d" % pool[0], 16)
         pool[0] += 1
-        node(q, i[1], o[1], lambda: Q[q].dma_start(o[0], i[0]).then_inc(T.sem[ev[0]], 16), 0.1, lat, ev)
+        k = node(q, i[1], [], lambda: Q[q].dma_start(o[0], i[0]).then_inc(T.sem[ev[0]], 16), 0.05, 0.0, ev, after=[j for j in after if nodes[j]["q"] == q])
+        node("eng", [], o[1], None, 0.02 + kb / RATE, NEAR, ev, after=[k] + [j for j in after if nodes[j]["q"] == "eng"])
 
     def send(dst, o, i, rs, ls, lat, codes=False):
         rid, pid, _ = topo.addr(dst)
         a, b = (o[0].bitcast(dt.uint8), i[0].bitcast(dt.uint8)) if codes else (o[0], i[0])
-        k = node("gp", i[1], [], lambda: g.remote_dma(a, b, T.sem[rs], T.sem[ls], pid, rid, topo.mask(core, dst)), 0.5, lat, (ls, len(topo.engines(core, dst))))
-        node("far", [], o[1], None, 0.0, 0.0, (rs, len(topo.engines(dst, core))), after=(k,))
+        k = node("gp", i[1], [], lambda: g.remote_dma(a, b, T.sem[rs], T.sem[ls], pid, rid, topo.mask(core, dst)), 0.5, 0.0, (ls, len(topo.engines(core, dst))),
+                 after=[j for j, x in enumerate(nodes) if x["q"] == "gp"])
+        node("far", [], o[1], None, 0.0, lat, (rs, len(topo.engines(dst, core))), after=(k,))
 
     def lay_out():
         n = len(nodes)
-        ins = [[(d, nodes[d]["lat"] + (WAKE if d in x["deps"] else 0.001)) for d in x["all"]] for x in nodes]
+        ins = [[(d, nodes[d]["lat"] + WAKE if d in x["deps"] else 0.001) for d in x["all"]] for x in nodes]
         outs = [[] for _ in nodes]
         for k in range(n):
             for d, w in ins[k]:
                 outs[d].append((k, w))
 
         def place(order, before, back):
-            end, used = [0.0] * n, {q: [] for q in Q}
+            end, used = [0.0] * n, {q: [] for q in list(Q) + ["eng"]}
             for k in order:
                 x = nodes[k]
                 t = max([x["lat"] if back else 0.0] + [end[d] + w for d, w in before[k]])
@@ -174,7 +179,7 @@ def rank_program(g, core, T, topo):
         for k in sorted(range(n), key=lambda i: (best[1][i] - nodes[i]["cost"], i)):
             x = nodes[k]
             q = x["q"]
-            if q != "far":
+            if q in Q:
                 need = {}
                 for d in x["deps"]:
                     e = nodes[d]["ev"]
@@ -200,61 +205,52 @@ def rank_program(g, core, T, topo):
      T0, T1, T2, T3, T4, T6, T7, T8, T9, TA, TB, TC, FL, NB, LV) = range(39)
     OU, OL, OF, OK1, OK2 = [R("offk", a, b) for a, b in ((0, 8), (8, 9), (10, 11), (12, 14), (14, 16))]
 
-    dma("sy", R("xt", 0, 640), H(T.x[:, 0:640]), 3.0)
-    dma("a", R("xt", 640, 1280), H(T.x[:, 640:1280]), 3.0)
-    dma("sy", R("ut"), H(T.u[:]), 2.5)
-    ms(R("pt"), 0)
-    dma("a", R("pt", 1, 21, p=(0, 16)), H(T.p0[:]))
-    dma("sy", R("pt", 0, 20, p=(16, 32)), H(T.p0[:]))
-    dma("a", R("pt", 25, 45, p=(0, 16)), H(T.p1[:]))
-    dma("sy", R("pt", 24, 44, p=(16, 32)), H(T.p1[:]))
-    dma("sy", u8(R("qw")), (T.wc[:], R("xt")[1]))
-    dma("sy", R("sw"), (T.ws[:], R("xt")[1]))
-    dma("sy", R("vt"), (T.v[:], R("xt")[1]))
+    for k in range(2):
+        dma("sy", R("ut", 256 * k, 256 * k + 128), H(T.u[:, 256 * k:256 * k + 128]), 33)
+        dma("a", R("ut", 256 * k + 128, 256 * k + 256), H(T.u[:, 256 * k:256 * k + 128]), 33)
+    dma("a", R("xt", 0, 640), H(T.x[:, 0:640]), 164, range(len(nodes)))
+    dma("sy", R("xt", 640, 1280), H(T.x[:, 640:1280]), 164, range(len(nodes)))
+    for k in range(2):
+        dma("a", R("pt", 0, 20, p=(16 * k, 16 * k + 16)), H(T.p0[:]), 4, range(len(nodes)))
+        dma("a" if k == 0 else "sy", R("pt", 20, 40, p=(16 * k, 16 * k + 16)), H(T.p1[:]), 4, range(len(nodes)))
+    dma("sy", u8(R("qw")), (T.wc[:], R("xt")[1]), 262)
+    dma("sy", R("sw"), (T.ws[:], R("xt")[1]), 66)
+    dma("sy", R("vt"), (T.v[:], R("xt")[1]), 131)
     iota(R("ci", 7, 8), [[0, 1]], 0, 1)
     iota(R("ct"), [[1, 516]], -3, -4)
     iota(R("iw"), [[1, 320]], 0, 0)
-    iota(R("tab", 0, 10), [[16, 10]], 0, 0)
     iota(R("r32"), [[0, 5], [1, 32]], 0, 0)
-    iota(R("tab", 16, 21), [[32, 5]], 0, 0)
+    iota(R("tab", 0, 5), [[32, 5]], 0, 0)
+    iota(R("tab", 8, 13), [[1, 5]], 0, 0)
     for k, m in enumerate((31, 15, 32, 16, 1, 6, 14)):
         ts(R("ci", k, k + 1), R("ci", 7, 8), m, A.bitwise_and)
     ts(R("ct"), R("ct"), 0.0, A.is_equal, 32.0, A.mult)
     for b in range(4):
         qz(R("qc", 128 * b, 128 * b + 128), R("sc", 128 * b, 128 * b + 128), R("ct", 3 - b, 515 - b))
     cp(R("cf", 0, 7), R("ci", 0, 7))
-    ms(R("offk", 0, 4), 0)
-    ms(R("offk", 4, 8), 64)
-    ms(R("x0", 352, 384), 0.0)
+    ms(R("x0"), 0.0)
     for k in (0, 3):
-        ms(R("xj", 192 * k + 176, 192 * k + 192), 0.0)
-    ms(R("d0", 0, 352, 2), 0.0)
-    lin(C(E16), C(EB), -1.0, 16.0)
+        ms(R("xj", 224 * k, 224 * k + 224), 0.0)
+    ms(R("d0", 0, 320, 2), 0.0)
     lin(C(NS), C(SB), -5.0, 0.0)
     ts(C(ROOT), C(J), 0.0, A.is_equal)
     ts(C(NR), C(J), 0.0, A.not_equal)
     lin(C(NRU), C(NR), U[1], 0.0)
-    ts(R("ni"), R("iw", 0, 176), C(E16), A.add)
-    lin(C(E33), C(E16), 2.0, 1.0)
-    ts(R("ni"), R("ni"), 31, A.bitwise_and)
-    ts(R("offa"), R("tab", 0, 10), C(R16), A.add, C(E16), A.add)
-    ts(R("n0"), R("ni"), C(J), A.not_equal, C(NRU), A.mult)
+    ts(R("nb"), R("r32"), C(J), A.not_equal, 2.0, A.add)
+    act(R("n0"), R("nb"), F.Copy, scale=C(NRU))
     lin(C(NB), C(ROOT), 255.0, 0.0)
     lin(R("nb"), R("n0"), 1.0, C(NB))
     qz(R("qu"), R("su"), R("ut"))
-    cp(u32(R("qu2")), ind(R("qu"), OU, dt.uint32))
-    act(R("su2"), ind(R("su"), OU), F.Copy)
     for k in range(2):
         qz(R("qx", 160 * k, 160 * k + 160), R("sx", 160 * k, 160 * k + 160), R("xt", 640 * k, 640 * k + 640))
     for k in range(4):
-        cp(R("offp", 0, 35, p=quad(k)), R("pt", 10 * (k % 2), 10 * (k % 2) + 35, p=quad(0)))
-    O0, O1 = R("offp", 0, 11), R("offp", 24, 35)
-    ts(R("r0"), ind(R("iw"), O0), C(NS), A.add, 0.0, A.max)
-    act(R("r1"), ind(R("iw"), O1), F.Relu, bias=C(NS))
-    tt(R("r0"), R("r0"), R("r1"), A.subtract)
-    act(R("d0", 1, 352, 2), R("r0"), F.Copy, scale=C(ROOT))
-    act(R("r1"), R("r1"), F.Copy, scale=C(ROOT))
-    tt(R("d1", 1, 352, 2), R("r1"), R("n0"), A.add)
+        cp(R("offp", 0, 30, p=quad(k)), R("pt", 10 * (k % 2), 10 * (k % 2) + 30, p=quad(0)))
+    O0, O1 = R("offp", 0, 10), R("offp", 20, 30)
+    ts(C(E33), C(NS), 1.0, A.add, C(ROOT), A.mult)
+    lin(R("r1"), ind(R("iw"), O1), C(ROOT), C(E33))
+    lin(R("r0"), ind(R("iw"), O0), C(ROOT), C(E33))
+    tt(R("d1", 1, 320, 2), R("r1"), R("n0"), A.add)
+    tt(R("d0", 1, 320, 2), R("r0"), R("r1"), A.subtract)
     lin(C(OD), C(EB), 1.0 / 16, 0.0)
     lin(C(IB), C(SB), 1.0 / 32, 0.0)
     lin(C(RHO), C(ROOT), 63.5, 0.5)
@@ -267,18 +263,26 @@ def rank_program(g, core, T, topo):
         lin(C(LV + 5 * l + 1), C(RHO), -U[l] / 64, U[l] / 2)
         lin(C(LV + 5 * l + 2), C(RHO), U[l], 0.0)
         lin(C(LV + 5 * l + 3), C(NR), (2.0 - 1.0 / 64) / U[l], 1.0 / 64 / U[l])
-        lin(C(LV + 5 * l + 4), C(ROOT), -63.5 * U[l], 0.0)
-    lin(C(LV), C(RHO), U[1], -33.0 * U[1])
+        lin(C(LV + 5 * l + 4), C(ROOT), -63.5 * U[l], -2.0)
+    lin(C(LV), C(ROOT), 159.5 * U[1], -95.5 * U[1])
+    lin(C(LV + 1), C(ROOT), -96.0 * U[1], -112.5 * U[1])
+    lin(C(LV + 2), C(ROOT), 2.0 * U[1], 0.0)
     ms(R("fl"), 0.0)
-    ts(C(T0), C(R16), 1.0, A.add, C(OD), A.subtract)
-    ts(C(T1), C(P1), C(OD), A.is_equal)
-    lin(C(T0), C(T0), 16.0, 0.0)
-    ts(C(T1), C(T1), 176.0, A.mult, C(T0), A.add)
-    ts(OF, C(T1), 351.0, A.min)
+    ts(C(E16), C(P1), C(OD), A.not_equal)
+    lin(C(T1), C(P14), 16.0, 0.0)
+    for n, (a, b) in enumerate(LANES):
+        lin(C(T0), C(EB), -2.0, 32.0 * (b - a) + 32.0)
+        ts(C(T0), C(E16), C(T0), A.mult, C(T1), A.add)
+        ts(R("offk", 16 + 2 * n, 17 + 2 * n), C(T0), 64.0 * (b - a) + 31.0, A.min)
     lin(C(TC), C(P1), 128.0, C(EB))
     ts(OL, C(P6), 16.0, A.mult, C(TC), A.add)
-    ms(R("seg"), 1.0)
-    ms(R("seg", 0, 160, 32), U[1])
+    ms(R("seg"), -4.0)
+    ms(R("seg", 0, 160, 32), -128.0 * U[1])
+    ms(R("cnt", 160, 192), -4.0)
+    ms(R("b0"), 0.0)
+    ms(R("b0", 0, 160, 32), -4.0)
+    ms(R("b0", 1, 160, 32), 96.0 * U[1])
+    ms(R("w0", 1, 320, 2), 0.0)
     ms(R("dn"), -1.0 / 32)
     ms(R("de"), -1.0 / 64)
     ts(R("yy"), R("r32"), C(J), A.is_equal, -1.0, A.mult)
@@ -288,10 +292,10 @@ def rank_program(g, core, T, topo):
     iota(R("n1s"), [[0, 320]], 1, 0)
     ms(R("u0"), -0.25)
     ms(R("u0", 0, 320, 64), -4.0)
-    iota(R("u1"), [[0, 1280]], -1, 0)
+    iota(R("u1"), [[0, 1280]], -4, 0)
     for l in range(4):
         ms(R("up", 384 * l + 320, 384 * l + 384), -1.0)
-    ms(R("pj", 0, 16), 2.0)
+    ms(R("ap", 0, 16), 2.0 * U[1])
     iota(R("sl"), [[0, 320]], 0, 0)
     iota(R("km"), [[0, 672]], 1, 0)
     ms(R("km", 0, 672, 32), 0.0)
@@ -334,17 +338,27 @@ def rank_program(g, core, T, topo):
     def run(n, k, w=1): return R(n, 160 * w * k, 160 * w * (k + 1))
     def bank(k, b, n=160): return R("pa" if k else "pb", 512 * b, 512 * b + n)
     def col(n, k): return R(n, k, k + 1)
+    def lanes(x): return list(enumerate(x))[::-1]
+    def one(n, a, b, o=0): return R(n, o + 32 * a, o + 32 * b)
+    def two(n, a, b, o=0): return R(n, o + 64 * a, o + 64 * b - o % 2, 2)
+    AP = R("ap", 16, 176)
 
     for rnd in range(3):
         mate = T.cores[rank ^ PARTNER[rnd]]
         QT, ST, QL, SL, LO, LI = [R("%s%d" % (n, rnd)) for n in ("qt", "st", "ql", "sl", "lo", "li")]
         for k in range(2):
-            mm(bank(0, k), R("qu2"), R("su2"), run("qx", k), run("sx", k))
+            mm(bank(0, k), R("qu"), R("su"), run("qx", k), run("sx", k))
         cp(run("ss", 0), bank(0, 0))
         act(run("ss", 1), bank(0, 1), F.Copy)
-        act(R("sb"), ind(R("ss"), O1), F.Copy)
-        tt(R("d1", 0, 352, 2), ind(R("ss"), O0), R("sb"), A.is_ge)
-        sc(R("x0", 0, 352), R("d0"), R("d1"), 0.0, A.mult, A.add)
+        for n, (a, b) in lanes(LANES):
+            o, i = one("sb", a, b), ind(R("ss"), R("offp", 20 + 2 * a, 20 + 2 * b))
+            if n:
+                cp(o, i)
+            else:
+                act(o, i, F.Copy)
+        for n, (a, b) in lanes(LANES):
+            tt(two("d1", a, b), ind(R("ss"), R("offp", 2 * a, 2 * b)), one("sb", a, b), A.is_ge)
+            sc(R("x0", 32 * n + 32 + 64 * a, 32 * n + 32 + 64 * b), R("d0", 64 * a, 64 * b), R("d1", 64 * a, 64 * b), 0.0, A.mult, A.add)
         for b in range(4):
             mm(bank(1, b, 320), *E(b), R("qx"), R("sx"))
             mm(bank(0, b), *E(b), run("qx", 0), run("sx", 0), True, False)
@@ -360,96 +374,98 @@ def rank_program(g, core, T, topo):
             mm(bank(1, b, 320), *E(b), QL, SL)
             act(R("gw", 320 * b, 320 * b + 320), bank(1, b, 320), F.Copy, scale=2.0 ** -6)
             mm(bank(1, b), *E(b), run("qx", 1), run("sx", 1), True, False)
-        k = 0
-        for ph, steps in enumerate(STEPS):
-            o, f = 352 * ph, 12 * ph
-            if ph == 0:
-                tr(R("tw", 0, 192), R("x0", 1, 384, 2))
-                tr(R("tw", 192, 352), R("x0", 33, 353, 2))
-                base, win, m, e = R("nb"), R("x0", 0, 352), 2.0, C(E33)
-            else:
-                a = 192 * (k - 1)
-                tr(R("tw", o, o + 192), R("xj", a, a + 192))
-                tr(R("tw", o + 192, o + 352), R("xj", a + 16, a + 176))
-                base, win, m, e = R("xc"), R("xj", a, a + 176), 1.0, C(E16)
-                act(base, win, F.Copy)
-            ts(R("offd", f, f + 12, 2), R("tw", o, o + 192, 32), m, A.mult, e, A.add)
-            ts(R("offd", f + 1, f + 11, 2), R("tw", o + 192, o + 352, 32), m, A.mult, e, A.add)
-            if ph == len(STEPS) - 1:
-                steps -= 1
-                ts(R("offd", 36, 52), ind(R("tw", o, o + 352), OF), e, A.add)
-                act(R("xu"), ind(win, R("offa")), F.Copy, scale=C(NR))
-            for _ in range(steps):
-                tt(R("xj", 192 * k, 192 * k + 176), ind(win, R("offd", f, f + 11)), base, A.min)
-                win = R("xj", 192 * k, 192 * k + 176)
-                k += 1
-        tt(R("ap"), ind(win, R("offd", 36, 46)), R("xu"), A.min)
-        sc(R("cnt"), R("seg"), R("ap"), U[1], A.min, A.add)
-        tr(R("apt"), R("ap"))
-        ts(R("ar0"), R("apt"), -64.0, A.mult, 17.5 * U[1], A.add)
-        lin(R("arx"), R("apt"), -128.0, 4.0)
+        for n, (a, b) in lanes(LANES):
+            k, w, s = 0, 32 * (b - a), 16 * n + 16 + 32 * a
+            for ph, steps in enumerate(STEPS):
+                o, f = 416 * ph + 64 * a + 32 * n, 48 * ph + 16 * n
+                if ph == 0:
+                    tr(R("tw", o + w, o + 2 * w + 32), R("x0", 2 * s - 31, 2 * (s + w) + 32, 2))
+                    tr(R("tw", o, o + w), R("x0", 2 * s + 1, 2 * (s + w), 2))
+                    base, win, m = one("nb", a, b), R("x0", 2 * s, 2 * (s + w)), 2.0
+                else:
+                    tr(R("tw", o + w, o + 2 * w + 32), R("xj", 224 * (k - 1) + s - 16, 224 * (k - 1) + s + w + 16))
+                    tr(R("tw", o, o + w), win)
+                    base, m = one("xc", a, b, 160 * (ph - 1)), 1.0
+                    if ph == len(STEPS) - 1:
+                        lin(base, win, C(NR), C(LV + 2))
+                    else:
+                        act(base, win, F.Copy)
+                ts(R("offd", f, f + 16), ind(R("tw", o, o + 2 * w + 32), R("offk", 16 + 2 * n, 17 + 2 * n)), m, A.mult, -1.0 - 32.0 * a * m, A.add)
+                for _ in range(steps):
+                    out = R("xj", 224 * k + s, 224 * k + s + w) if k < sum(STEPS) - 1 else one("ap", a, b, 16)
+                    tt(out, ind(win, R("offd", f, f + w // 16)), base, A.min)
+                    win = out
+                    k += 1
+        for n, (a, b) in lanes(LL[0]):
+            sc(one("cnt", a, b), one("seg", a, b), one("ap", a, b, 16), -4.0, A.max, A.subtract)
+        tr(R("apt"), AP)
+        lin(R("arx"), R("apt"), -128.0, 8.0)
         sc(R("ar"), R("arx"), R("thr"), 0.0, A.max, A.subtract)
-        ts(R("pj", 16, 176), R("ap"), 64.0, A.mult, 2.0, A.add)
-        sc(R("dm"), R("pj", 16, 176), R("pj", 15, 175), 0.0, A.max, A.subtract)
-        act(R("dc"), R("dm"), F.Copy, scale=U[3])
-        ms(R("dc", 0, 160, 32), -4.0)
-        ts(R("dr"), R("dm"), -1.0 / TINY, A.mult, 1.0, A.add)
+        sc(R("pj"), AP, R("ap", 15, 175), 0.0, A.max, A.subtract)
+        act(R("dm"), R("pj"), F.Copy, scale=64.0)
+        act(R("dc"), R("pj"), F.Copy, scale=64.0 * U[3])
+        lin(R("dc", 0, 160, 32), R("tab", 0, 5), 0.0, -4.0)
+        ts(R("dr"), R("pj"), -64.0 / TINY, A.mult, 1.0, A.add)
         ts(R("dr"), R("dr"), TINY, A.max)
-        ms(R("dr", 0, 160, 32), 0.0)
-        ms(R("dm", 0, 160, 32), -4.0)
-        ts(R("sm", 48, 53), R("ap", 1, 160, 32), 0.0, A.is_equal, TINY, A.max)
+        lin(R("dr", 0, 160, 32), R("tab", 0, 5), 0.0, 0.0)
+        lin(R("dm", 0, 160, 32), R("tab", 0, 5), 0.0, -4.0)
+        ts(R("sm", 48, 53), R("ap", 17, 176, 32), 2.0 * U[1], A.is_equal, TINY, A.max)
         for t in range(5):
-            lin(R("ao", 32 * t, 32 * t + 32), R("ap", 32 * t, 32 * t + 32), -128.0, float(t))
+            lin(R("ao", 32 * t, 32 * t + 32), R("ap", 32 * t + 16, 32 * t + 48), -128.0, t + 4.0)
         for l in range(4):
             U1 = 320 * l
             if l == 0:
                 NV = ends("cnt")
-                lin(last("u1"), NV, 1.0, C(LV))
-                lin(R("sm", 0, 5), NV, 1.0, C(LV + 7))
-                ts(R("sm", 8, 13), NV, 17.5 * U[1], A.is_gt, -1.0, A.mult)
-                tt(last("u0"), R("sm", 8, 13), R("sm", 0, 5), A.add)
-                for t in range(5):
-                    ts(R("dy", 32 * t, 32 * t + 32), R("ar0", 32 * t, 32 * t + 32), col("cnt", 32 * t + 31), A.is_gt, col("cnt", 32 * t + 31), A.mult)
+                lin(last("w0"), NV, -1.0, C(LV))
+                ts(R("u1", 62, 320, 64), NV, -208.5 * U[1], A.is_lt, 128.0 * U[1], A.mult)
+                for n, (a, b) in lanes(LL[0]):
+                    sc(one("yy", a, b), one("b0", a, b), one("cnt", a, b, 31), 0.0, A.add, A.max)
+                    tr(two("u1", a, b, 1), one("yy", a, b))
+                    ts(two("w0", a, b), two("u1", a, b, 1), C(LV + 1), A.is_gt, 4.0, A.mult)
+                    sc(R("up", 64 * a, 64 * b), R("w0", 64 * a, 64 * b), R("u1", 64 * a, 64 * b), 0.0, A.subtract, A.max)
             else:
                 o = 384 * (l - 1)
                 NV = last("up", o)
-                lin(R("dm", 1, 160, 32), R("ap", 1, 160, 32), 64.0, C(LV + 5 * l + 4))
+                lin(R("dm", 1, 160, 32), R("ap", 17, 176, 32), 64.0, C(LV + 5 * l + 4))
                 act(R("dr", 1, 160, 32), R("sm", 48, 53), F.Copy, scale=C(LV + 5 * l + 3))
-                sc(R("lf"), R("dr"), R("up", o + 63, o + 383, 2), 0.0, A.mult, A.max)
-                sc(R("yy"), R("dm"), R("up", o + 63, o + 383, 2), 0.0, A.add, A.max)
                 lin(last("n0s"), NV, -2.0, C(LV + 5 * l))
                 if l < 3:
                     lin(last("n1s"), NV, 1.0 / 64, C(LV + 5 * l + 1))
                     lin(last("u1", U1), NV, 1.0 / 64, 0.0)
                 else:
                     lin(last("n1s"), NV, 0.0, C(IDX))
-                tr(R("n0s", 0, 320, 2), R("lf"))
-                tr(R("n1s", 0, 320, 2), R("yy"))
-                sc(R("gg"), R("n0s"), R("n1s"), 0.0, A.add, A.min)
-                sc(R("dd"), R("de"), R("n0s", 0, 320, 2), 0.0, A.add, A.max)
+                for n, (a, b) in lanes(LL[l]):
+                    sc(one("lf", a, b), one("dr", a, b), two("up", a, b, o + 63), 0.0, A.mult, A.max)
+                    sc(one("yy", a, b), one("dm", a, b), two("up", a, b, o + 63), 0.0, A.add, A.max)
+                    tr(two("n0s", a, b), one("lf", a, b))
+                    tr(two("n1s", a, b), one("yy", a, b))
+                    sc(R("gg", 64 * a, 64 * b), R("n0s", 64 * a, 64 * b), R("n1s", 64 * a, 64 * b), 0.0, A.add, A.min)
+                    sc(one("dd", a, b), one("de", a, b), two("n0s", a, b), 0.0, A.add, A.max)
                 for t in range(5):
                     ts(R("dy", 32 * t, 32 * t + 32), R("ar", 32 * t, 32 * t + 32), col("dd", 32 * t + 31), A.is_gt, col("gg", 64 * t + 63), A.mult)
                 if l < 3:
-                    lin(last("u0"), last("gg"), 1.0, C(LV + 5 * l + 7))
+                    for n, (a, b) in lanes(LL[l]):
+                        lin(R("u0", 64 * a + 63, 64 * b, 64), R("gg", 64 * a + 63, 64 * b, 64), 1.0, C(LV + 5 * l + 7))
                 else:
                     act(R("dr", 1, 160, 32), R("sm", 48, 53), F.Copy, scale=C(LV + 3))
                     ts(R("fl", 0, 160, 32), last("gg"), 0.0, A.is_gt, C(FL), A.mult)
                     sc(R("lf"), R("dr"), R("fl"), 0.0, A.mult, A.max)
                     tr(run("k3", l), R("lf"))
-                    lin(last("u0"), R("tab", 16, 21), -U[4], C(KC))
+                    lin(last("u0"), R("tab", 0, 5), -U[4], C(KC))
             DT = R("u1", U1, U1 + 320, 2)
-            tr(DT, R("dy"))
-            sc(R("up", 384 * l, 384 * l + 320), R("u0"), R("u1", U1, U1 + 320), 0.0, A.subtract, A.max)
+            for n, (a, b) in lanes(LL[l] if l else ()):
+                tr(two("u1", a, b, U1), one("dy", a, b))
+                sc(R("up", 384 * l + 64 * a, 384 * l + 64 * b), R("u0", 64 * a, 64 * b), R("u1", U1 + 64 * a, U1 + 64 * b), 0.0, A.subtract, A.max)
             for k in range(4):
                 d, b = 2 * (k // 2) + min(l, 1), 160 * (k % 2) + SLOT[l]
                 src = NV[1][0]
                 i, o = R(src[0], src[3], src[4], src[5], p=quad(k)), R("sl", b, b + 160 - SLOT[l], 32, p=quad(d))
-                c = R("cf", RHO, RHO + 1, p=quad(k)) if l else 33.0
-                if k % 2 and l == 3:
-                    ts(o, i, -1.0 / U[l], A.mult, c, A.add)
-                else:
-                    lin(o, i, -1.0 / U[l], c)
-            if l < 3:
+                lin(o, i, (-1.0 if l else 1.0) / U[l], R("cf", RHO, RHO + 1, p=quad(k)) if l else 224.0)
+            if l == 0:
+                act(run("z0", 0), R("w0", 0, 320, 2), F.Copy, scale=0.25)
+                sc(run("rho", 0), R("dn"), run("z0", 0), -1.0, A.add, A.max)
+                tt(ends("xs"), ends("rho"), R("tab", 8, 13), A.add)
+            elif l < 3:
                 act(run("z0", l), DT, F.Sign, bias=-U[4] / 4)
                 sc(run("rho", l), R("dn"), run("z0", l), -1.0, A.add, A.max)
                 for t in range(5):
@@ -530,11 +546,11 @@ def rank_program(g, core, T, topo):
 
     for k in range(2):
         mm(bank(0, k), R("qv"), R("sv"), run("qx", k), run("sx", k))
-        dma("sy", H(T.oc[:, 640 * k:640 * k + 640]), u8(run("qx", k)))
+        dma("sy", H(T.oc[:, 640 * k:640 * k + 640]), u8(run("qx", k)), 82)
     for k in range(4):
-        dma("gp" if k == 3 else "sy", H(T.osc[4 * k:4 * k + 4, :]), R("sx", p=(32 * k, 32 * k + 4)))
+        dma("sy", H(T.osc[4 * k:4 * k + 4, :]), R("sx", p=(32 * k, 32 * k + 4)))
     act(run("yo", 0), bank(0, 0), F.Copy)
     cp(run("yo", 1), bank(0, 1))
-    dma("a", H(T.y[:, 0:160]), run("yo", 0))
-    dma("sy", H(T.y[:, 160:320]), run("yo", 1))
+    dma("a", H(T.y[:, 0:160]), run("yo", 0), 82)
+    dma("a", H(T.y[:, 160:320]), run("yo", 1), 82)
     lay_out()

@@ -1,4 +1,5 @@
 import math
+import numpy
 from concourse.mybir import dt, AluOpType, ActivationFunctionType
 A = AluOpType
 F = ActivationFunctionType
@@ -9,19 +10,21 @@ _S = {
     "qx": (320, X4), "sx": (320, U8), "qu": (128, X4), "su": (128, U8),
     "qv": (128, X4), "sv": (128, U8), "qw": (512, X4), "sw": (512, U8), "qc": (512, X4), "sc": (512, U8),
     "qz": (320, X4), "sz": (320, U8),
-    "zw": (1792, BF), "gw": (1280, BF), "he": (512, BF), "yo": (320, F32),
-    "pt": (40, I32), "ci": (8, I32), "cf": (64, F32), "tab": (16, F32), "iw": (320, F32),
-    "offk": (24, U16), "offp": (32, U16), "offd": (144, U16), "offs": (32, U16), "offz": (32, U16),
+    "zw": (1792, BF), "gw": (1280, BF), "he": (512, BF), "fh": (1280, BF), "yo": (320, F32), "zz": (336, BF),
+    "pt": (40, I32), "ci": (8, I32), "cf": (72, F32), "sm": (48, F32), "tab": (48, F32), "iw": (320, F32),
+    "offk": (24, U16), "offp": (32, U16), "offd": (144, U16), "offs": (32, U16), "offz": (32, U16), "offc": (32, U16),
     "ss": (320, F32), "sb": (160, F32), "d0": (320, BF), "d1": (320, BF), "x0": (448, BF), "xj": (6 * 224, BF),
     "tw": (3 * 416, BF), "xc": (320, BF), "nb": (160, BF), "r0": (160, F32), "r1": (160, F32), "n0": (160, F32),
-    "ap": (176, BF), "apt": (160, BF), "w0": (320, BF), "b0": (160, BF), "arx": (160, BF), "ar": (160, BF), "thr": (160, F16), "pj": (160, BF),
-    "dm": (160, BF), "dr": (160, BF), "fl": (160, BF), "ao": (160, BF), "dc": (160, BF), "r32": (160, BF), "seg": (160, BF), "dn": (160, BF), "de": (160, BF),
-    "cnt": (192, BF), "yy": (160, BF), "lf": (160, BF), "n0s": (320, BF), "n1s": (320, BF), "gg": (320, BF), "dd": (160, BF),
-    "dy": (160, BF), "u0": (320, BF), "u1": (4 * 320, BF), "up": (4 * 384, BF), "sm": (64, BF),
-    "z0": (480, BF), "rho": (480, BF), "y2": (640, BF), "y2t": (640, BF), "k3": (640, BF), "xs": (640, BF),
+    "ap": (176, BF), "apt": (160, BF), "sgn": (160, BF), "rr": (160, BF), "g1": (320, BF), "vv": (320, BF), "n1": (320, BF),
+    "e3": (960, BF), "o3": (960, BF), "xa": (160, BF), "dp1": (160, BF), "va": (160, BF), "arx": (160, BF), "ar": (160, BF), "thr": (160, F16), "pj": (160, BF),
+    "dm": (160, BF), "dr": (160, BF), "ao": (160, BF), "r32": (160, BF), "seg": (160, BF), "dn": (160, BF), "dp": (160, BF), "de": (160, BF),
+    "cnt": (160, BF), "ly": (320, BF), "ns": (1280, BF), "gg": (320, BF), "dd": (160, BF),
+    "dy": (160, BF), "u0": (320, BF), "u1": (3 * 320, BF), "up": (3 * 384, BF),
+    "pv": (320, F32), "ab": (320, BF), "a0": (320, BF), "xe": (320, BF),
+    "z0": (480, BF), "rho": (480, BF), "y2": (480, BF), "y2t": (480, BF), "k3": (480, BF), "xs": (480, BF),
     "sl": (320, BF), "km": (672, BF), "mm": (320, BF), "rs": (320, BF), "sg": (320, BF),
     "e1": (320, F16), "e2": (336, F16), "pp": (352, F16), "pq": (672, F16), "ps": (672, F16), "kq": (72, F32),
-    "m2": (320, BF), "rc": (352, BF), "rt": (672, BF), "rcf": (320, F32), "wz": (160, F32),
+    "rc": (352, BF), "rt": (672, BF), "rcf": (320, F32), "wz": (192, F32),
     "lw": (336, BF), "lt": (256, BF),
 }
 for _t in range(3):
@@ -35,16 +38,143 @@ SCRATCH = {k: ("sbuf", [128, n], d) for k, (n, d) in _S.items()}
 SCRATCH["pa"] = ("psum", [128, 2048], F32)
 SCRATCH["pb"] = ("psum", [128, 2048], F32)
 SEMAPHORES = ["v", "a", "pe", "gp"] + ["m%d" % i for i in range(32)] + ["%s%d" % (n, t) for n in ("rq", "rs", "rl", "oq", "os", "ol") for t in range(3)]
-U = [2.0 ** -6, 2.0 ** -6, 2.0 ** -12, 2.0 ** -18, 2.0 ** -24]
+U = [2.0 ** -6, 2.0 ** -6, 2.0 ** -6, 2.0 ** -12, 2.0 ** -18]
+MARK = 32.0
+MU = 2.0 ** -28
 SLOT = (0, 0, 17, 26)
 TINY = 2.0 ** -60
-CY, WAKE, FAR = 0.00083, 0.2, 1.1
-NEAR, RATE = 1.0, 250.0
-PASSES = 8
 LANES = ((0, 3), (3, 5))
 LL = (((0, 2), (2, 5)),) * 3 + (((0, 5),),)
+CUT = (0, 192, 320)
 STEPS = (1, 3, 3)
-ZV, XV = (2, 3, 7), (1, 3, 5, 7)
+NB1 = 2
+XV, M2V, KQV, SLV, FHV = (1, 3, 5, 7), (0, 2), (0,), (0, 2), (2,)
+CY, FAR, BULK, NEAR, RATE = 0.00083, 0.5, 8.0, 1.5, 250.0
+CASES = ((1.2, 0.22, 1.6, 4.0), (1.45, 0.24, 2.0, 5.5))
+MOVES, HEAT = (60000, 10000), (0.12, 0.03)
+ORDER = []
+
+
+def arrange(nodes, keep, first, focus, moves, heat):
+    n, at = len(keep), {k: i for i, k in enumerate(keep)}
+    X = [nodes[k] for k in keep]
+    qs, lat = [x["q"] for x in X], [x["lat"] for x in X]
+    needs = [set(at[d] for d in x["all"] if d in at) for x in X]
+    users = [set() for _ in X]
+    for k in range(n):
+        for d in needs[k]:
+            users[d].add(k)
+    cases = [([x["cost"][0] + c[0] * (x["cost"][1] + c[2] * x["cost"][2] + c[3] * x["cost"][3]) for x in X],
+              [[(d, lat[d] + c[1] if keep[d] in X[k]["deps"] else 0.001) for d in sorted(needs[k])] for k in range(n)]) for c in CASES]
+    tails, many = [k for k in range(n) if not users[k]], len(set(qs))
+
+    def walk(order, cost, ins, old=None, same=0):
+        end, why = (old[3][:], old[2][:]) if old else ([0.0] * n, [None] * n)
+        last = {}
+        for k in order[:same][::-1]:
+            if qs[k] not in last:
+                last[qs[k]] = k
+                if len(last) == many:
+                    break
+        last["far"] = None
+        for k in order[same:]:
+            q = qs[k]
+            y = last.get(q)
+            t = 0.0 if y is None else end[y]
+            for d, w in ins[k]:
+                e = end[d] + w
+                if e > t:
+                    t, y = e, -1 - d
+            end[k] = t + cost[k]
+            why[k] = y
+            if q != "far":
+                last[q] = k
+        k = max(tails, key=lambda i: end[i] + lat[i])
+        return end[k] + lat[k], k, why, end
+
+    def place(order, cost, before, back):
+        end, used = [0.0] * n, {q: [] for q in qs}
+        for k in order:
+            t = max([lat[k] if back else 0.0] + [end[d] + w for d, w in before[k]])
+            if qs[k] != "far":
+                u, i = used[qs[k]], 0
+                while i < len(u) and u[i][0] < t + cost[k]:
+                    t = max(t, u[i][1])
+                    i += 1
+                u.insert(i, (t, t + cost[k]))
+            end[k] = t + cost[k]
+        return end
+
+    def ahead(order, a, b, of):
+        pa, pb = order.index(a), order.index(b)
+        need, queues, moved, rest = set(of[b]), set(), [b], []
+        for x in order[pb - 1:pa:-1]:
+            if x in need or qs[x] in queues:
+                moved.append(x)
+                need |= of[x]
+                if qs[x] != "far":
+                    queues.add(qs[x])
+            else:
+                rest.append(x)
+        if a in need or qs[a] in queues:
+            return None
+        return order[:pa] + moved[::-1] + [a] + rest[::-1] + order[pb + 1:]
+
+    cost, ins = cases[0]
+    if first is None:
+        late = [0.0] * n
+        for k in range(n - 1, -1, -1):
+            late[k] = cost[k] + max([lat[k]] + [late[i] + w for i in users[k] for d, w in ins[i] if d == k])
+        first = sorted(range(n), key=lambda i: (-late[i], i))
+    end, rank = place(first, cost, ins, False), {k: i for i, k in enumerate(first)}
+    order = sorted(first, key=lambda i: (end[i] - cost[i], rank[i]))
+    runs = [walk(order, *c) for c in cases]
+    now = sum(r[0] for r in runs)
+    best, rng = (now, order), numpy.random.default_rng(1)
+    for step in range(moves):
+        _, k, why, _ = runs[step % len(cases)]
+        pairs = []
+        while why[k] is not None:
+            if why[k] >= 0 and k in focus:
+                pairs.append((why[k], k))
+            k = why[k] if why[k] >= 0 else -1 - why[k]
+        if not pairs:
+            break
+        a, b = pairs[int(rng.integers(len(pairs)))]
+        mine = [x for x in order if qs[x] == qs[a]]
+        i, j = mine.index(a), int(rng.geometric(0.5)) - 1
+        if rng.random() < 0.5:
+            new = ahead(order, mine[max(i - j, 0)], b, needs)
+        else:
+            new = ahead(order[::-1], mine[min(i + 1 + j, len(mine) - 1)], a, users)
+            new = new and new[::-1]
+        if new:
+            same = 0
+            while new[same] == order[same]:
+                same += 1
+            trial = [walk(new, c[0], c[1], r, same) for c, r in zip(cases, runs)]
+            total = sum(r[0] for r in trial)
+            if total <= now or rng.random() < math.exp((now - total) / (heat * len(cases) * (1.0 - step / moves) + 1e-6)):
+                order, runs, now = new, trial, total
+                if now < best[0]:
+                    best = (now, order)
+    end = walk(best[1], cost, ins)[3]
+    return [keep[k] for k in best[1]], {keep[k]: end[k] - cost[k] for k in range(n)}, best[0] / len(cases)
+
+
+def order_of(nodes, rounds, meets):
+    n, size = len(nodes), rounds[1] - rounds[0]
+    order, start, _ = arrange(nodes, list(range(meets[1], meets[2])), None, range(size), MOVES[0], HEAT[0])
+    rank, key = {k: i for i, k in enumerate(order)}, {}
+    for k in range(rounds[0], rounds[3]):
+        s = (k - meets[1]) // size
+        key[k] = (100.0 * s + start[k - s * size], rank[k - s * size])
+    for k in range(rounds[0] - 1, -1, -1):
+        key[k] = (min([key[i][0] for i in range(k + 1, rounds[3]) if k in nodes[i]["all"]] + [200.0]) - 0.3, k)
+    for k in range(rounds[3], n):
+        key[k] = (max([key[d][0] for d in nodes[k]["all"]]) + 0.3, k)
+    ends = set(range(meets[0])) | set(range(meets[2], n))
+    return arrange(nodes, list(range(n)), sorted(range(n), key=lambda k: key[k]), ends, MOVES[1], HEAT[1])[0]
 
 
 def rank_program(g, core, T, topo):
@@ -52,7 +182,7 @@ def rank_program(g, core, T, topo):
     if rank is None:
         return
     Q = {"v": g.vector, "a": g.scalar, "pe": g.tensor, "gp": g, "sy": g.sync}
-    nodes, hist, pool = [], {}, [0]
+    nodes, hist, pool, rounds, meets = [], {}, [0], [], []
 
     def R(name, a=None, b=None, s=1, p=(0, 128)):
         if a is None:
@@ -63,9 +193,8 @@ def rank_program(g, core, T, topo):
             return (ap, [(name, 0, 128, a // 512 * 512, a // 512 * 512 + 512, 1)], n, False, False)
         return (ap, [(name, p[0], p[1], a, b, s)], n, _S[name][1] in (BF, F16, U16), False)
 
-    def ind(w, o, cast=None):
-        ap = w[0] if cast is None else w[0].bitcast(cast)
-        return (ap.indirect(o[0]), w[1] + o[1], 16 * o[2], False, True)
+    def ind(w, o):
+        return (w[0].indirect(o[0]), w[1] + o[1], 16 * o[2], False, True)
 
     def meet(x, y):
         if x[2] <= y[1] or y[2] <= x[1] or x[4] <= y[3] or y[4] <= x[3]:
@@ -106,23 +235,27 @@ def rank_program(g, core, T, topo):
 
     V, S = g.vector, g.scalar
 
+    def fixed(t): return (t, 0.0, 0.0, 0.0)
+    def cyc(n): return (0.0, CY * max(64, n), 0.0, 0.0)
+
     def cc(o, *ins):
         if ins[0][4]:
-            return 0.055 + 0.0013 * ins[0][2]
+            return (0.055, 0.0, CY * ins[0][2], 0.0)
         if o[4]:
-            return 0.05 + 0.0032 * o[2]
-        return CY * max(64, o[2] * (0.5 if o[3] and all(i[3] for i in ins) else 1))
+            return (0.05, 0.0, 0.0, CY * o[2])
+        return cyc(o[2] * (0.5 if o[3] and all(i[3] for i in ins) else 1))
 
     def cp(o, i): op("v", V.tensor_copy, 1, cc(o, i), o, i)
-    def tt(o, a, b, f): op("v", V.tensor_tensor, 1, cc(o, a) if a[4] else CY * max(64, 2 * o[2]), o, a, b, f)
+    def tt(o, a, b, f): op("v", V.tensor_tensor, 1, cc(o, a) if a[4] else cyc(2 * o[2]), o, a, b, f)
     def tr(o, i): op("v", V.transpose, 1, cc(o, i), o, i)
     def ms(o, c): op("v", V.memset, 1, cc(o, o), o, c)
     def sc(o, a, b, i, f0, f1): op("v", V.tensor_tensor_scan, 1, cc(o, a, b), o, a, b, i, f0, f1)
-    def qz(c, s, i): op("v", V.quantize_mx, 2, 0.012 + 0.00088 * c[2], c, s, i)
-    def act(o, i, f, **kw): op("a", S.activation, 1, cc(o, i) if i[4] else CY * max(64, o[2]), o, i, f, **kw)
+    def qz(c, s, i): op("v", V.quantize_mx, 2, (0.0, 0.012 + 0.00088 * c[2], 0.0, 0.0), c, s, i)
+    def act(o, i, f, **kw): op("a", S.activation, 1, cc(o, i) if i[4] else cyc(o[2]), o, i, f, **kw)
     def lin(o, i, m, c): act(o, i, F.Identity, scale=m, bias=c)
-    def iota(o, pat, base, cm): op("gp", g.iota, 1, 0.15 + 2 * CY * o[2], o, pat, base, cm, allow_small_or_imprecise_dtypes=True)
-    def mm(o, w, ws, x, xs, start=True, stop=True): op("pe", g.tensor.matmul_mx, 1, 0.0006 * (o[2] + 16), o, w, ws, x, xs, start, stop, free=not start)
+    def fill(o, c): lin(o, R("zz", 0, o[2], p=o[1][0][1:3]), 0.0, c)
+    def iota(o, pat, base, cm): op("gp", g.iota, 1, (0.0, 0.13 + 2 * CY * o[2], 0.0, 0.0), o, pat, base, cm, allow_small_or_imprecise_dtypes=True)
+    def mm(o, w, ws, x, xs, start=True, stop=True): op("pe", g.tensor.matmul_mx, 1, (0.0, 0.0006 * (o[2] + 16), 0.0, 0.0), o, w, ws, x, xs, start, stop, free=not start)
 
     def ts(o, i, s1, f0, s2=None, f1=None):
         if f1 is None:
@@ -130,53 +263,30 @@ def rank_program(g, core, T, topo):
         else:
             op("v", V.tensor_scalar, 1, cc(o, i), o, i, s1, s2, f0, f1)
 
+    def copy(vector, o, i, m=1.0, c=0.0):
+        if vector:
+            ts(o, i, m, A.mult, c, A.add)
+        else:
+            lin(o, i, m, c)
+
     def dma(q, o, i, kb=4, after=()):
         ev = ("m%d" % pool[0], 16)
         pool[0] += 1
-        k = node(q, i[1], [], lambda: Q[q].dma_start(o[0], i[0]).then_inc(T.sem[ev[0]], 16), 0.05, 0.0, ev, after=[j for j in after if nodes[j]["q"] == q])
-        node("eng", [], o[1], None, 0.02 + kb / RATE, NEAR, ev, after=[k] + [j for j in after if nodes[j]["q"] == "eng"])
+        k = node(q, i[1], [], lambda: Q[q].dma_start(o[0], i[0]).then_inc(T.sem[ev[0]], 16), fixed(0.05), 0.0, ev, after=[j for j in after if nodes[j]["q"] == q])
+        node("eng", [], o[1], None, fixed(0.02 + kb / RATE), NEAR, ev, after=[k] + [j for j in after if nodes[j]["q"] == "eng"])
 
     def send(dst, o, i, rs, ls, lat, codes=False):
         rid, pid, _ = topo.addr(dst)
         a, b = (o[0].bitcast(dt.uint8), i[0].bitcast(dt.uint8)) if codes else (o[0], i[0])
-        k = node("gp", i[1], [], lambda: g.remote_dma(a, b, T.sem[rs], T.sem[ls], pid, rid, topo.mask(core, dst)), 0.5, 0.0, (ls, len(topo.engines(core, dst))),
+        k = node("gp", i[1], [], lambda: g.remote_dma(a, b, T.sem[rs], T.sem[ls], pid, rid, topo.mask(core, dst)), fixed(0.4), 0.0, (ls, len(topo.engines(core, dst))),
                  after=[j for j, x in enumerate(nodes) if x["q"] == "gp"])
-        node("far", [], o[1], None, 0.0, lat, (rs, len(topo.engines(dst, core))), after=(k,))
+        node("far", [], o[1], None, fixed(0.0), lat, (rs, len(topo.engines(dst, core))), after=(k,))
 
     def lay_out():
-        n = len(nodes)
-        ins = [[(d, nodes[d]["lat"] + WAKE if d in x["deps"] else 0.001) for d in x["all"]] for x in nodes]
-        outs = [[] for _ in nodes]
-        for k in range(n):
-            for d, w in ins[k]:
-                outs[d].append((k, w))
-
-        def place(order, before, back):
-            end, used = [0.0] * n, {q: [] for q in list(Q) + ["eng"]}
-            for k in order:
-                x = nodes[k]
-                t = max([x["lat"] if back else 0.0] + [end[d] + w for d, w in before[k]])
-                if x["q"] != "far":
-                    u, i = used[x["q"]], 0
-                    while i < len(u) and u[i][0] < t + x["cost"]:
-                        t = max(t, u[i][1])
-                        i += 1
-                    u.insert(i, (t, t + x["cost"]))
-                end[k] = t + x["cost"]
-            return end
-
-        late = [0.0] * n
-        for k in range(n - 1, -1, -1):
-            late[k] = nodes[k]["cost"] + max([nodes[k]["lat"]] + [late[i] + w for i, w in outs[k]])
-        best = None
-        for _ in range(PASSES):
-            end = place(sorted(range(n), key=lambda i: (-late[i], i)), ins, False)
-            span = max(end[k] + nodes[k]["lat"] for k in range(n))
-            if best is None or span < best[0]:
-                best = (span, end)
-            late = place(sorted(range(n), key=lambda i: (-end[i], -i)), outs, True)
+        if not ORDER:
+            ORDER.extend(order_of(nodes, rounds, meets))
         count, known, final = {}, {q: {} for q in Q}, {}
-        for k in sorted(range(n), key=lambda i: (best[1][i] - nodes[i]["cost"], i)):
+        for k in ORDER:
             x = nodes[k]
             q = x["q"]
             if q in Q:
@@ -198,182 +308,209 @@ def rank_program(g, core, T, topo):
 
     def H(t): return (t, [])
     def u8(x): return (x[0].bitcast(dt.uint8),) + x[1:]
-    def u32(x): return (x[0].bitcast(dt.uint32),) + x[1:]
     def C(k): return R("cf", k, k + 1)
     def quad(k): return (32 * k, 32 * k + 32)
-    (J, R16, SB, EB, P1, P6, P14, E16, E33, NS, ROOT, NR, NRU, RHO, KC, IDX, OD, IB, VV, VB, PH, SC, ACC, T5,
-     T0, T1, T2, T3, T4, T6, T7, T8, T9, TA, TB, TC, FL, NB, LV) = range(39)
-    OU, OL, OF, OK1, OK2 = [R("offk", a, b) for a, b in ((0, 8), (8, 9), (10, 11), (12, 14), (14, 16))]
+    def cut(n, k, w=1): return R(n, w * CUT[k], w * CUT[k + 1])
+    def wid(k): return CUT[k + 1] - CUT[k]
+    (J, SB, EB, P1, P6, P14, E16, ROOT, NR, NRU, RHO, KC, IDX, OD, IB, VV, VB, PH, SC, ACC, HV, NJ,
+     T0, T1, T2, T3, T4, T5, T6, T7, T8, T9, TA, TB, TC, TD, FL, NB, LV) = range(39)
+    L31, SG, FM, BT, BP, BW, PS, RT, DP = range(60, 69)
+    OL, OK1, OK2 = [R("offk", a, b) for a, b in ((8, 9), (12, 14), (14, 16))]
 
     for k in range(2):
-        dma("sy", R("ut", 256 * k, 256 * k + 128), H(T.u[:, 256 * k:256 * k + 128]), 33)
-        dma("a", R("ut", 256 * k + 128, 256 * k + 256), H(T.u[:, 256 * k:256 * k + 128]), 33)
-    dma("a", R("xt", 0, 640), H(T.x[:, 0:640]), 164, range(len(nodes)))
-    dma("sy", R("xt", 640, 1280), H(T.x[:, 640:1280]), 164, range(len(nodes)))
+        dma("a", R("pt", 0, 20, p=(16 * k, 16 * k + 16)), H(T.p0[:]), 2, range(len(nodes)))
+        dma("sy", R("pt", 20, 40, p=(16 * k, 16 * k + 16)), H(T.p1[:]), 2, range(len(nodes)))
     for k in range(2):
-        dma("a", R("pt", 0, 20, p=(16 * k, 16 * k + 16)), H(T.p0[:]), 4, range(len(nodes)))
-        dma("a" if k == 0 else "sy", R("pt", 20, 40, p=(16 * k, 16 * k + 16)), H(T.p1[:]), 4, range(len(nodes)))
+        dma("sy", R("ut", 256 * k, 256 * k + 128), H(T.u[:, 256 * k:256 * k + 128]), 33, range(len(nodes)))
+        dma("a", R("ut", 256 * k + 128, 256 * k + 256), H(T.u[:, 256 * k:256 * k + 128]), 33, range(len(nodes)))
+    dma("a", cut("xt", 0, 4), H(T.x[:, 0:4 * CUT[1]]), 197, range(len(nodes)))
+    dma("sy", cut("xt", 1, 4), H(T.x[:, 4 * CUT[1]:1280]), 131, range(len(nodes)))
     dma("sy", u8(R("qw")), (T.wc[:], R("xt")[1]), 262)
     dma("sy", R("sw"), (T.ws[:], R("xt")[1]), 66)
     dma("sy", R("vt"), (T.v[:], R("xt")[1]), 131)
+    ms(R("zz"), 0.0)
     iota(R("ci", 7, 8), [[0, 1]], 0, 1)
     iota(R("ct"), [[1, 516]], -3, -4)
-    iota(R("iw"), [[1, 320]], 0, 0)
+    iota(R("iw"), [[32, 5], [0, 2], [1, 32]], 1, 0)
     iota(R("r32"), [[0, 5], [1, 32]], 0, 0)
-    iota(R("tab", 0, 5), [[32, 5]], 0, 0)
-    iota(R("tab", 8, 13), [[1, 5]], 0, 0)
-    for k, m in enumerate((31, 15, 32, 16, 1, 6, 14)):
+    iota(R("tab", 0, 5), [[64, 5]], -128, 0)
+    iota(R("tab", 8, 13), [[2, 5]], -4, 0)
+    for k, m in enumerate((31, 32, 16, 1, 6, 14)):
         ts(R("ci", k, k + 1), R("ci", 7, 8), m, A.bitwise_and)
     ts(R("ct"), R("ct"), 0.0, A.is_equal, 32.0, A.mult)
     for b in range(4):
         qz(R("qc", 128 * b, 128 * b + 128), R("sc", 128 * b, 128 * b + 128), R("ct", 3 - b, 515 - b))
-    cp(R("cf", 0, 7), R("ci", 0, 7))
+    cp(R("cf", 0, 6), R("ci", 0, 6))
     ms(R("x0"), 0.0)
     for k in (0, 3):
         ms(R("xj", 224 * k, 224 * k + 224), 0.0)
-    ms(R("d0", 0, 320, 2), 0.0)
-    lin(C(NS), C(SB), -5.0, 0.0)
-    ts(C(ROOT), C(J), 0.0, A.is_equal)
-    ts(C(NR), C(J), 0.0, A.not_equal)
-    lin(C(NRU), C(NR), U[1], 0.0)
+    fill(R("d0", 0, 320, 2), 0.0)
+    act(C(ROOT), C(J), F.Relu, scale=-1.0, bias=1.0)
+    lin(C(NR), C(ROOT), -1.0, 1.0)
+    lin(C(NRU), C(NR), -U[1], 0.0)
     ts(R("nb"), R("r32"), C(J), A.not_equal, 2.0, A.add)
-    act(R("n0"), R("nb"), F.Copy, scale=C(NRU))
-    lin(C(NB), C(ROOT), 255.0, 0.0)
-    lin(R("nb"), R("n0"), 1.0, C(NB))
+    lin(R("n0"), R("nb"), C(NRU), 256.0)
+    lin(C(NB), C(ROOT), 255.0, 256.0)
+    lin(R("nb"), R("n0"), -1.0, C(NB))
     qz(R("qu"), R("su"), R("ut"))
     for k in range(2):
-        qz(R("qx", 160 * k, 160 * k + 160), R("sx", 160 * k, 160 * k + 160), R("xt", 640 * k, 640 * k + 640))
+        qz(cut("qx", k), cut("sx", k), cut("xt", k, 4))
     for k in range(4):
-        cp(R("offp", 0, 30, p=quad(k)), R("pt", 10 * (k % 2), 10 * (k % 2) + 30, p=quad(0)))
-    O0, O1 = R("offp", 0, 10), R("offp", 20, 30)
-    ts(C(E33), C(NS), 1.0, A.add, C(ROOT), A.mult)
-    lin(R("r1"), ind(R("iw"), O1), C(ROOT), C(E33))
-    lin(R("r0"), ind(R("iw"), O0), C(ROOT), C(E33))
-    tt(R("d1", 1, 320, 2), R("r1"), R("n0"), A.add)
-    tt(R("d0", 1, 320, 2), R("r0"), R("r1"), A.subtract)
+        for e in range(2):
+            cp(R("offp", e, 20, 2, p=quad(k)), R("pt", 2 * (k % 2) + e, 40, 4, p=quad(0)))
+    lin(R("r1"), ind(R("iw"), R("offp", 10, 20)), C(ROOT), 256.0)
+    lin(R("r0"), ind(R("iw"), R("offp", 0, 10)), C(ROOT), 256.0)
+    sc(R("d1", 1, 320, 2), R("r1"), R("n0"), 0.0, A.max, A.subtract)
+    sc(R("d0", 1, 320, 2), R("r0"), R("r1"), 0.0, A.max, A.subtract)
     lin(C(OD), C(EB), 1.0 / 16, 0.0)
     lin(C(IB), C(SB), 1.0 / 32, 0.0)
     lin(C(RHO), C(ROOT), 63.5, 0.5)
-    lin(C(FL), C(ROOT), 1.0, TINY)
-    lin(C(LV + 3), C(NR), 1.0 / TINY, 1.0)
-    lin(C(KC), C(NR), U[3], 0.0)
-    lin(C(IDX), C(J), U[4], U[4])
-    for l in (1, 2, 3):
-        lin(C(LV + 5 * l), C(ROOT), 4.0, U[l])
+    act(C(T0), C(J), F.Sign, bias=-1.5)
+    lin(C(KC), C(T0), 0.5, 0.5)
+    act(C(FL), C(KC), F.Exp, scale=math.log(TINY))
+    lin(C(IDX), C(J), -U[4] / 2, 16.0 * U[4])
+    lin(C(T2), C(J), U[4], -30.0 * U[4])
+    lin(C(LV + 3), C(ROOT), -63.5 * U[3], C(T2))
+    for l in (2, 3):
+        lin(C(LV + 5 * l), C(ROOT), 4.0, U[l] + 16.0 * U[4] * (l == 3))
         lin(C(LV + 5 * l + 1), C(RHO), -U[l] / 64, U[l] / 2)
         lin(C(LV + 5 * l + 2), C(RHO), U[l], 0.0)
-        lin(C(LV + 5 * l + 3), C(NR), (2.0 - 1.0 / 64) / U[l], 1.0 / 64 / U[l])
-        lin(C(LV + 5 * l + 4), C(ROOT), -63.5 * U[l], -2.0)
-    lin(C(LV), C(ROOT), 159.5 * U[1], -95.5 * U[1])
-    lin(C(LV + 1), C(ROOT), -96.0 * U[1], -112.5 * U[1])
+        lin(C(T3), C(NR), (2.0 - 1.0 / 64) / U[l], 1.0 / 64 / U[l])
+        act(C(LV + 5 * l + 3), C(T3), F.Copy, scale=C(FL))
+        lin(C(LV + 5 * l + 4), C(ROOT), -63.5 * U[l], C(KC))
+    act(C(L31), C(J), F.Relu, bias=-30.0)
+    lin(C(SG), C(L31), -U[1], 96.0 * U[1])
+    lin(C(FM), C(ROOT), -2.0 * MARK * U[1], (32.0 + MARK) * U[1])
+    lin(C(BT), C(L31), 2.0 * U[1], (64.0 + MARK) * U[1])
+    lin(C(HV), C(ROOT), 2.0 * MARK * U[1], 0.0)
+    lin(C(T1), C(L31), -U[1], 2.0 * U[1])
+    lin(C(BP), C(HV), 1.0, C(T1))
+    lin(C(LV), C(L31), U[1], 0.0)
+    lin(C(BW), C(HV), -1.0, C(LV))
+    lin(C(PS), C(RHO), U[1], -1.0)
+    lin(C(RT), C(ROOT), -63.5 * U[1], 0.0)
+    lin(C(DP), C(J), 1.0 / 32, 1.0 + 2.0 / 32)
     lin(C(LV + 2), C(ROOT), 2.0 * U[1], 0.0)
-    ms(R("fl"), 0.0)
-    ts(C(E16), C(P1), C(OD), A.not_equal)
-    lin(C(T1), C(P14), 16.0, 0.0)
+    act(C(E16), C(OD), F.Abs, scale=-1.0, bias=C(P1))
+    lin(C(T4), C(P14), 16.0, 0.0)
     for n, (a, b) in enumerate(LANES):
-        lin(C(T0), C(EB), -2.0, 32.0 * (b - a) + 32.0)
-        ts(C(T0), C(E16), C(T0), A.mult, C(T1), A.add)
-        ts(R("offk", 16 + 2 * n, 17 + 2 * n), C(T0), 64.0 * (b - a) + 31.0, A.min)
+        lin(C(T5), C(EB), -2.0, 32.0 * (b - a) + 32.0)
+        lin(C(T5), C(T5), C(E16), C(T4))
+        ts(R("offk", 16 + 2 * n, 17 + 2 * n), C(T5), 64.0 * (b - a) + 31.0, A.min)
     lin(C(TC), C(P1), 128.0, C(EB))
     ts(OL, C(P6), 16.0, A.mult, C(TC), A.add)
-    ms(R("seg"), -4.0)
-    ms(R("seg", 0, 160, 32), -128.0 * U[1])
-    ms(R("cnt", 160, 192), -4.0)
-    ms(R("b0"), 0.0)
-    ms(R("b0", 0, 160, 32), -4.0)
-    ms(R("b0", 1, 160, 32), 96.0 * U[1])
-    ms(R("w0", 1, 320, 2), 0.0)
-    ms(R("dn"), -1.0 / 32)
-    ms(R("de"), -1.0 / 64)
-    ts(R("yy"), R("r32"), C(J), A.is_equal, -1.0, A.mult)
+    fill(R("seg"), -4.0)
+    fill(R("seg", 0, 160, 32), C(SG))
+    fill(R("rr", 0, 160, 32), 0.0)
+    ms(R("g1"), 0.0)
+    ms(R("e3", 0, 320), (64.0 + MARK) * U[1])
+    ms(R("e3", 320, 960), 0.0)
+    fill(R("e3", 0, 960, 64), -4.0)
+    fill(R("dp1"), 1.0 / 32)
+    fill(R("dp1", 0, 160, 32), 2.0)
+    fill(R("dn"), -1.0 / 32)
+    fill(R("dp"), 1.0 / 32)
+    fill(R("de"), -1.0 / 64)
+    ts(R("va"), R("r32"), C(J), A.is_equal, -1.0, A.mult)
     lin(R("yo", 0, 160), R("r32"), -1.0 / 64, 3.0 + 31.5 / 64)
-    tt(R("thr"), R("yy"), R("yo", 0, 160), A.add)
-    iota(R("n0s"), [[0, 320]], 0, 0)
-    iota(R("n1s"), [[0, 320]], 1, 0)
+    tt(R("thr"), R("va"), R("yo", 0, 160), A.add)
+    for l in (2, 3):
+        for a, b in LL[l]:
+            n0, w = 640 * (l // 3) + 128 * a, 64 * (b - a)
+            fill(R("ns", n0 + 1, n0 + w, 2), -U[4] * (l // 3))
+            fill(R("ns", n0 + w + 1, n0 + 2 * w, 2), 1.0)
+            if l == 3:
+                fill(R("ns", n0 + w + 63, n0 + 2 * w, 64), C(IDX))
+    fill(R("tab", 16, 48), 1.0 / 512)
+    fill(R("dr", 0, 160, 32), 0.0)
+    fill(R("dm", 0, 160, 32), -4.0)
+    fill(R("ab", 1, 320, 2), 1.0)
+    iota(R("a0"), [[0, 320]], 0, 0)
+    fill(R("a0", 0, 320, 64), 1.0)
+    lin(R("a0", 63, 320, 64), R("tab", 0, 5), -MU, 0.0)
     ms(R("u0"), -0.25)
-    ms(R("u0", 0, 320, 64), -4.0)
-    iota(R("u1"), [[0, 1280]], -4, 0)
-    for l in range(4):
-        ms(R("up", 384 * l + 320, 384 * l + 384), -1.0)
-    ms(R("ap", 0, 16), 2.0 * U[1])
+    fill(R("u0", 0, 320, 64), -4.0)
+    for l in (1, 2):
+        fill(R("u1", 320 * l + 1, 320 * l + 320, 2), -4.0)
+        fill(R("up", 384 * l + 320, 384 * l + 384), -1.0)
+    fill(R("ap", 0, 16), 2.0 * U[1])
     iota(R("sl"), [[0, 320]], 0, 0)
     iota(R("km"), [[0, 672]], 1, 0)
-    ms(R("km", 0, 672, 32), 0.0)
+    fill(R("km", 0, 672, 32), 0.0)
     for k in (1, 3):
         for x in SLOT[2:]:
-            ms(R("km", x, 672, 32, p=quad(k)), 0.0)
-    ts(C(T2), C(J), SLOT[2], A.is_ge, SLOT[2], A.mult)
-    ts(C(T3), C(J), SLOT[3], A.is_ge, SLOT[3] - SLOT[2], A.mult)
-    ts(C(T4), C(T2), C(T3), A.add, 1.0, A.add)
-    ts(C(T5), C(T4), C(IB), A.mult, C(J), A.subtract)
-    lin(C(VV), C(T5), -1.0, 1.0)
-    lin(C(VB), C(T5), 1.0, -1.5)
+            fill(R("km", x, 672, 32, p=quad(k)), 0.0)
+    act(C(T6), C(J), F.Sign, bias=0.5 - SLOT[2])
+    act(C(T7), C(J), F.Sign, bias=0.5 - SLOT[3])
+    lin(C(T6), C(T6), SLOT[2] / 2, SLOT[3] / 2 + 1.0)
+    lin(C(T6), C(T7), (SLOT[3] - SLOT[2]) / 2, C(T6))
+    lin(C(NJ), C(J), -1.0, 0.0)
+    lin(C(T7), C(T6), C(IB), C(NJ))
+    lin(C(VV), C(T7), -1.0, 1.0)
+    lin(C(VB), C(T7), 1.0, -1.5)
     ms(R("e2", 0, 16), 0.0)
     ms(R("pp", 0, 16), 0.0)
     ms(R("pp", 336, 352), 0.0)
-    ms(R("rc", 0, 16), 0.0)
-    ms(R("rc", 336, 352), 0.0)
-    iota(R("m2"), [[0, 320]], 0, 0)
-    ms(R("kq"), 0.0)
-    ms(R("lw", 0, 144), 0.0)
+    fill(R("rc", 0, 16), 0.0)
+    fill(R("rc", 336, 352), 0.0)
+    iota(R("rt", 0, 320), [[0, 320]], 0, 0)
+    fill(R("wz", 64, 128, 2), 4096.0)
+    fill(R("kq"), 0.0)
+    fill(R("lw", 0, 144), 0.0)
+    for b in range(NB1, 4):
+        fill(R("zw", 448 * b, 448 * b + 128), 0.0)
     lin(C(PH), C(EB), 1.0, -353.0)
-    ts(C(T6), C(OD), C(IB), A.mult)
-    lin(C(SC), C(T6), 1.0 / U[4] - 32.0, 32.0)
-    ts(C(T7), C(P1), C(OD), A.not_equal)
+    act(C(TD), C(OD), F.Copy, scale=C(IB))
+    lin(C(SC), C(TD), 1.0 / MU - 32.0, 32.0)
     lin(C(T8), C(OD), -1.0, 11.0)
     lin(C(T9), C(P14), 0.5, 0.0)
-    ts(C(TA), C(T7), C(T8), A.mult, C(T9), A.add)
-    lin(C(T7), C(OD), 42.0, C(TA))
-    lin(C(T8), C(T6), -63.0, C(T7))
-    for k in range(2):
-        ts(R("offk", 12 + k, 13 + k), C(IB), 21.0, A.mult, C(T8), A.add) if k == 0 else ts(R("offk", 13, 14), R("offk", 12, 13), 8.0, A.add)
+    lin(C(TA), C(T8), C(E16), C(T9))
+    lin(C(T8), C(OD), 42.0, C(TA))
+    lin(C(T9), C(TD), -63.0, C(T8))
+    ts(R("offk", 12, 13), C(IB), 21.0, A.mult, C(T9), A.add)
+    ts(R("offk", 13, 14), R("offk", 12, 13), 8.0, A.add)
     lin(C(TB), C(TA), 32.0, C(EB))
     cp(R("offk", 14, 15), C(TB))
     ts(R("offk", 15, 16), C(TB), 256.0, A.add, 671.0, A.min)
     qz(R("qv"), R("sv"), R("vt"))
 
     def E(b): return R("qc", 128 * b, 128 * b + 128), R("sc", 128 * b, 128 * b + 128)
-    def ends(n, a=0, k=5, p=(0, 128)): return R(n, a + 31, a + 32 * k, 32, p=p)
+    def ends(n, a=0, p=(0, 128)): return R(n, a + 31, a + 160, 32, p=p)
     def last(n, a=0, p=(0, 128)): return R(n, a + 63, a + 320, 64, p=p)
     def run(n, k, w=1): return R(n, 160 * w * k, 160 * w * (k + 1))
-    def bank(k, b, n=160): return R("pa" if k else "pb", 512 * b, 512 * b + n)
+    def bank(k, b, n): return R("pa" if k else "pb", 512 * b, 512 * b + n)
     def col(n, k): return R(n, k, k + 1)
     def lanes(x): return list(enumerate(x))[::-1]
     def one(n, a, b, o=0): return R(n, o + 32 * a, o + 32 * b)
     def two(n, a, b, o=0): return R(n, o + 64 * a, o + 64 * b - o % 2, 2)
-    AP = R("ap", 16, 176)
+    AP, RC = R("ap", 16, 176), R("rc", 16, 336)
 
     for rnd in range(3):
+        rounds.append(len(nodes))
         mate = T.cores[rank ^ PARTNER[rnd]]
         QT, ST, QL, SL, LO, LI = [R("%s%d" % (n, rnd)) for n in ("qt", "st", "ql", "sl", "lo", "li")]
         for k in range(2):
-            mm(bank(0, k), R("qu"), R("su"), run("qx", k), run("sx", k))
-        cp(run("ss", 0), bank(0, 0))
-        act(run("ss", 1), bank(0, 1), F.Copy)
+            mm(bank(0, k, wid(k)), R("qu"), R("su"), cut("qx", k), cut("sx", k))
+            copy(k == 0, cut("ss", k), bank(0, k, wid(k)))
         for n, (a, b) in lanes(LANES):
-            o, i = one("sb", a, b), ind(R("ss"), R("offp", 20 + 2 * a, 20 + 2 * b))
-            if n:
-                cp(o, i)
-            else:
-                act(o, i, F.Copy)
-        for n, (a, b) in lanes(LANES):
-            tt(two("d1", a, b), ind(R("ss"), R("offp", 2 * a, 2 * b)), one("sb", a, b), A.is_ge)
+            copy(n == 1, one("sb", a, b), ind(R("ss", 0, 64 * b), R("offp", 10 + 2 * a, 10 + 2 * b)))
+            tt(two("d1", a, b), ind(R("ss", 0, 64 * b), R("offp", 2 * a, 2 * b)), one("sb", a, b), A.is_ge)
             sc(R("x0", 32 * n + 32 + 64 * a, 32 * n + 32 + 64 * b), R("d0", 64 * a, 64 * b), R("d1", 64 * a, 64 * b), 0.0, A.mult, A.add)
         for b in range(4):
             mm(bank(1, b, 320), *E(b), R("qx"), R("sx"))
-            mm(bank(0, b), *E(b), run("qx", 0), run("sx", 0), True, False)
+            mm(bank(0, b, wid(0)), *E(b), cut("qx", 0), cut("sx", 0), True, False)
         for b in range(4):
             act(R("tt", b, 1280, 4), bank(1, b, 320), F.Copy, scale=2.0 ** -5)
         for k in range(2):
             qz(run("qt%d" % rnd, k), run("st%d" % rnd, k), run("tt", k, 4))
-        send(mate, QL, QT, "rq%d" % rnd, "oq%d" % rnd, FAR + 9.0, True)
-        send(mate, SL, ST, "rs%d" % rnd, "os%d" % rnd, FAR + 9.0)
+        send(mate, QL, QT, "rq%d" % rnd, "oq%d" % rnd, FAR + BULK, True)
+        send(mate, SL, ST, "rs%d" % rnd, "os%d" % rnd, FAR + BULK)
         for b in range(4):
-            act(R("zw", 448 * b + 128, 448 * b + 448), bank(1, b, 320), F.Copy, scale=2.0 ** -5)
+            act(R("zw", 448 * b + 128, 448 * b + 448), bank(1, b, 320), F.Copy, scale=2.0 ** -5 if b < NB1 else 2.0 ** -6)
         for b in range(4):
             mm(bank(1, b, 320), *E(b), QL, SL)
             act(R("gw", 320 * b, 320 * b + 320), bank(1, b, 320), F.Copy, scale=2.0 ** -6)
-            mm(bank(1, b), *E(b), run("qx", 1), run("sx", 1), True, False)
+            mm(bank(1, b, wid(1)), *E(b), cut("qx", 1), cut("sx", 1), True, False)
         for n, (a, b) in lanes(LANES):
             k, w, s = 0, 32 * (b - a), 16 * n + 16 + 32 * a
             for ph, steps in enumerate(STEPS):
@@ -402,93 +539,114 @@ def rank_program(g, core, T, topo):
         lin(R("arx"), R("apt"), -128.0, 8.0)
         sc(R("ar"), R("arx"), R("thr"), 0.0, A.max, A.subtract)
         sc(R("pj"), AP, R("ap", 15, 175), 0.0, A.max, A.subtract)
-        act(R("dm"), R("pj"), F.Copy, scale=64.0)
-        act(R("dc"), R("pj"), F.Copy, scale=64.0 * U[3])
-        lin(R("dc", 0, 160, 32), R("tab", 0, 5), 0.0, -4.0)
-        ts(R("dr"), R("pj"), -64.0 / TINY, A.mult, 1.0, A.add)
-        ts(R("dr"), R("dr"), TINY, A.max)
-        lin(R("dr", 0, 160, 32), R("tab", 0, 5), 0.0, 0.0)
-        lin(R("dm", 0, 160, 32), R("tab", 0, 5), 0.0, -4.0)
-        ts(R("sm", 48, 53), R("ap", 17, 176, 32), 2.0 * U[1], A.is_equal, TINY, A.max)
+        for n, (a, b) in lanes(LANES):
+            lin(one("sgn", a, b), one("ap", a, b, 16), -128.0, 5.0)
+        lin(R("xa"), R("apt"), 128.0, (63.5 + MARK - 256.0) * U[1])
         for t in range(5):
-            lin(R("ao", 32 * t, 32 * t + 32), R("ap", 32 * t + 16, 32 * t + 48), -128.0, t + 4.0)
+            tt(R("rr", 32 * t + 1, 32 * t + 32), R("sgn", 32 * t + 1, 32 * t + 32), R("sgn", 32 * t, 32 * t + 31), A.mult)
+            act(R("dm", 32 * t + 2, 32 * t + 32), R("pj", 32 * t + 2, 32 * t + 32), F.Copy, scale=64.0)
+            act(R("dr", 32 * t + 2, 32 * t + 32), R("pj", 32 * t + 2, 32 * t + 32), F.Exp, scale=64.0 * math.log(TINY))
+            lin(one("ao", t, t + 1), one("ap", t, t + 1, 16), 128.0, -2.0 * t)
         for l in range(4):
             U1 = 320 * l
             if l == 0:
-                NV = ends("cnt")
-                lin(last("w0"), NV, -1.0, C(LV))
-                ts(R("u1", 62, 320, 64), NV, -208.5 * U[1], A.is_lt, 128.0 * U[1], A.mult)
+                NV = ("cnt", 31, 160, 32)
+                H0, H1, G1 = R("sm", 0, 5), R("sm", 8, 13), R("g1", 160, 320, 32)
+                ts(H0, R(*NV), 15.5 * U[1], A.is_gt, 32.0 * U[1], A.mult)
+                ts(H1, R(*NV), 15.5 * U[1], A.is_gt, C(FM), A.mult)
+                tt(R("g1", 0, 160, 32), H0, R(*NV), A.subtract)
+                tt(G1, H1, R(*NV), A.subtract)
+                lin(R("e3", 1, 320, 64), H0, -(64.0 + MARK) / 32, (64.0 + MARK) * U[1])
+                lin(last("e3"), R(*NV), 2.0, C(BT))
+                lin(R("e3", 320 + 62, 640, 64), H0, -8.0, 0.0)
+                lin(last("e3", 320), G1, 1.0, C(BP))
+                lin(R("e3", 640 + 62, 960, 64), H0, 8.0, -4.0)
+                lin(last("e3", 640), G1, -1.0, C(BW))
                 for n, (a, b) in lanes(LL[0]):
-                    sc(one("yy", a, b), one("b0", a, b), one("cnt", a, b, 31), 0.0, A.add, A.max)
-                    tr(two("u1", a, b, 1), one("yy", a, b))
-                    ts(two("w0", a, b), two("u1", a, b, 1), C(LV + 1), A.is_gt, 4.0, A.mult)
-                    sc(R("up", 64 * a, 64 * b), R("w0", 64 * a, 64 * b), R("u1", 64 * a, 64 * b), 0.0, A.subtract, A.max)
+                    for e in range(2):
+                        sc(one("vv", a, b, 160 * e), one("rr", a, b), one("g1", a, b, 160 * e), 0.0, A.mult, A.add)
+                        tr(two("n1", a, b, e), one("vv", a, b, 160 * e))
+                    for e in range(3):
+                        sc(R("o3", 320 * e + 64 * a, 320 * e + 64 * b), R("e3", 320 * e + 64 * a, 320 * e + 64 * b), R("n1", 64 * a, 64 * b), 0.0, A.add if e else A.subtract, A.max)
+            elif l == 1:
+                NV = ("o3", 640 + 63, 960, 64)
+                ts(R("sm", 16, 21), last("o3"), (63.5 + MARK) * U[1], A.is_gt, C(PS), A.add)
+                tt(last("u0"), last("o3", 320), R("sm", 16, 21), A.add)
+                lin(last("u1", U1), R(*NV), -1.0, C(LV + 12))
+                lin(R("sm", 24, 29), R("sm", 16, 21), 1.0, C(RT))
+                for n, (a, b) in lanes(LL[l]):
+                    for t in range(a, b):
+                        ts(one("dy", t, t + 1), one("xa", t, t + 1), col("o3", 64 * t + 63), A.is_lt, col("o3", 320 + 64 * t + 63), A.mult)
+                    tr(two("u1", a, b, U1), one("dy", a, b))
+                    sc(R("up", 384 * l + 64 * a, 384 * l + 64 * b), R("u0", 64 * a, 64 * b), R("u1", U1 + 64 * a, U1 + 64 * b), 0.0, A.subtract, A.max)
             else:
                 o = 384 * (l - 1)
-                NV = last("up", o)
-                lin(R("dm", 1, 160, 32), R("ap", 17, 176, 32), 64.0, C(LV + 5 * l + 4))
-                act(R("dr", 1, 160, 32), R("sm", 48, 53), F.Copy, scale=C(LV + 5 * l + 3))
-                lin(last("n0s"), NV, -2.0, C(LV + 5 * l))
+                NV = ("up", o + 63, o + 320, 64)
+                fill(R("dm", 1, 160, 32), C(LV + 5 * l + 4))
+                fill(R("dr", 1, 160, 32), C(LV + 5 * l + 3))
                 if l < 3:
-                    lin(last("n1s"), NV, 1.0 / 64, C(LV + 5 * l + 1))
-                    lin(last("u1", U1), NV, 1.0 / 64, 0.0)
-                else:
-                    lin(last("n1s"), NV, 0.0, C(IDX))
+                    lin(last("u1", U1), R(*NV), 1.0 / 64, 0.0)
                 for n, (a, b) in lanes(LL[l]):
-                    sc(one("lf", a, b), one("dr", a, b), two("up", a, b, o + 63), 0.0, A.mult, A.max)
-                    sc(one("yy", a, b), one("dm", a, b), two("up", a, b, o + 63), 0.0, A.add, A.max)
-                    tr(two("n0s", a, b), one("lf", a, b))
-                    tr(two("n1s", a, b), one("yy", a, b))
-                    sc(R("gg", 64 * a, 64 * b), R("n0s", 64 * a, 64 * b), R("n1s", 64 * a, 64 * b), 0.0, A.add, A.min)
-                    sc(one("dd", a, b), one("de", a, b), two("n0s", a, b), 0.0, A.add, A.max)
-                for t in range(5):
-                    ts(R("dy", 32 * t, 32 * t + 32), R("ar", 32 * t, 32 * t + 32), col("dd", 32 * t + 31), A.is_gt, col("gg", 64 * t + 63), A.mult)
-                if l < 3:
-                    for n, (a, b) in lanes(LL[l]):
+                    w, n0, nv = 32 * (b - a), 640 * (l // 3) + 128 * a, R("up", o + 64 * a + 63, o + 64 * b, 64)
+                    n1 = n0 + 2 * w
+                    lin(R("ns", n0 + 63, n1, 64), nv, -2.0, C(LV + 5 * l))
+                    if l < 3:
+                        lin(R("ns", n1 + 63, n1 + 2 * w, 64), nv, 1.0 / 64, C(LV + 5 * l + 1))
+                    else:
+                        act(R("ns", n0 + 61, n1, 64), nv, F.Relu, scale=4.0 / U[3])
+                        lin(R("ns", n1 + 61, n1 + 2 * w, 64), nv, 1.0, C(LV + 3))
+                    sc(R("ly", 64 * a, 64 * a + w), one("dr", a, b), two("up", a, b, o + 63), 0.0, A.mult, A.max)
+                    sc(R("ly", 64 * a + w, 64 * b), one("dm", a, b), two("up", a, b, o + 63), 0.0, A.add, A.max)
+                    tr(R("ns", n0, n0 + 4 * w, 2), R("ly", 64 * a, 64 * b))
+                    sc(R("gg", 64 * a, 64 * b), R("ns", n0, n1), R("ns", n1, n1 + 2 * w), 0.0, A.add, A.min)
+                    if l < 3:
+                        sc(one("dd", a, b), one("de", a, b), R("ns", n0, n1, 2), 0.0, A.add, A.max)
                         lin(R("u0", 64 * a + 63, 64 * b, 64), R("gg", 64 * a + 63, 64 * b, 64), 1.0, C(LV + 5 * l + 7))
-                else:
-                    act(R("dr", 1, 160, 32), R("sm", 48, 53), F.Copy, scale=C(LV + 3))
-                    ts(R("fl", 0, 160, 32), last("gg"), 0.0, A.is_gt, C(FL), A.mult)
-                    sc(R("lf"), R("dr"), R("fl"), 0.0, A.mult, A.max)
-                    tr(run("k3", l), R("lf"))
-                    lin(last("u0"), R("tab", 0, 5), -U[4], C(KC))
-            DT = R("u1", U1, U1 + 320, 2)
-            for n, (a, b) in lanes(LL[l] if l else ()):
-                tr(two("u1", a, b, U1), one("dy", a, b))
-                sc(R("up", 384 * l + 64 * a, 384 * l + 64 * b), R("u0", 64 * a, 64 * b), R("u1", U1 + 64 * a, U1 + 64 * b), 0.0, A.subtract, A.max)
+                    for t in range(a, b):
+                        if l < 3:
+                            ts(one("dy", t, t + 1), one("ar", t, t + 1), col("dd", 32 * t + 31), A.is_gt, col("gg", 64 * t + 63), A.mult)
+                        else:
+                            ts(one("pv", t, t + 1), R("tab", 16, 48), col("gg", 64 * t + 63), A.mult, col("gg", 64 * t + 61), A.add)
+                    if l < 3:
+                        tr(two("u1", a, b, U1), one("dy", a, b))
+                        sc(R("up", 384 * l + 64 * a, 384 * l + 64 * b), R("u0", 64 * a, 64 * b), R("u1", U1 + 64 * a, U1 + 64 * b), 0.0, A.subtract, A.max)
             for k in range(4):
-                d, b = 2 * (k // 2) + min(l, 1), 160 * (k % 2) + SLOT[l]
-                src = NV[1][0]
-                i, o = R(src[0], src[3], src[4], src[5], p=quad(k)), R("sl", b, b + 160 - SLOT[l], 32, p=quad(d))
-                lin(o, i, (-1.0 if l else 1.0) / U[l], R("cf", RHO, RHO + 1, p=quad(k)) if l else 224.0)
+                d, b, c = 2 * (k // 2) + min(l, 1), 32 * (k % 2) + SLOT[l], RHO if l else L31
+                copy(l == 3 and k in SLV, R("sl", b, 320, 64, p=quad(d)), R(*NV, p=quad(k)), (-1.0 if l > 1 else 1.0) / U[l], 0.0 if l == 1 else R("cf", c, c + 1, p=quad(k)))
             if l == 0:
-                act(run("z0", 0), R("w0", 0, 320, 2), F.Copy, scale=0.25)
+                act(R("va"), R("n1", 1, 320, 2), F.Abs)
+                act(run("z0", 0), R("va"), F.Sign, bias=-20.0 * U[1])
                 sc(run("rho", 0), R("dn"), run("z0", 0), -1.0, A.add, A.max)
                 tt(ends("xs"), ends("rho"), R("tab", 8, 13), A.add)
             elif l < 3:
-                act(run("z0", l), DT, F.Sign, bias=-U[4] / 4)
-                sc(run("rho", l), R("dn"), run("z0", l), -1.0, A.add, A.max)
-                for t in range(5):
-                    o = 160 * l + 32 * t
-                    act(R("y2", o, o + 32), R("ao", 32 * t, 32 * t + 32), F.Identity, bias=col("rho", o + 31))
-                tr(run("y2t", l), run("y2", l))
-                for t in range(5):
-                    o = 160 * l + 32 * t
-                    act(R("k3", o, o + 32), R("y2t", o, o + 32), F.Sign, scale=-1.0, bias=t + 1.0 / 64)
-                sc(run("xs", l), run("k3", l), run("y2t", l), 0.0, A.mult, A.max)
-            else:
-                sc(run("y2", l), R("dc"), R("up", 384 * l + 63, 384 * l + 383, 2), 0.0, A.add, A.max)
-                tr(run("y2t", l), run("y2", l))
-                sc(run("xs", l), run("k3", l), run("y2t", l), 0.0, A.add, A.min)
-            for k in range(4):
-                d, b = 2 * (k // 2) + l // 2, 160 * (k % 2) + 16 * (l % 2)
-                o = R("m2", b, 160 * (k % 2) + 160, 32, p=quad(d))
-                if l < 3:
-                    lin(o, ends("xs", 160 * l, p=quad(k)), 1.0, (160.0 * (k % 2) - 161.0) / 32)
-                elif k % 2:
-                    lin(o, ends("xs", 160 * l, p=quad(k)), -1.0, -U[4])
+                if l == 1:
+                    tt(R("sm", 32, 37), R("up", 384 + 62, 384 + 320, 64), R("sm", 24, 29), A.subtract)
+                    for t in range(5):
+                        act(one("z0", t, t + 1, 160), two("u1", t, t + 1, U1), F.Sign, scale=-1.0, bias=col("sm", 32 + t))
+                    act(R("sm", 40, 45), R(*NV), F.Relu, scale=-4.0 / U[1], bias=C(DP))
+                    lin(ends("dp1"), R("sm", 40, 45), -1.0, 1.0 / 32)
                 else:
-                    ts(o, ends("xs", 160 * l, p=quad(k)), -1.0, A.mult, -161.0 * U[4], A.add)
+                    act(run("z0", l), R("u1", U1, U1 + 320, 2), F.Sign, scale=-1.0, bias=U[4] / 4)
+                sc(run("rho", l), R("dp1" if l == 1 else "dp"), run("z0", l), 1.0, A.add, A.min)
+                for t in range(5):
+                    act(one("y2", t, t + 1, 160 * l), one("ao", t, t + 1), F.Identity, bias=col("rho", 160 * l + 32 * t + 31))
+                tr(run("y2t", l), run("y2", l))
+                for t in range(5):
+                    act(one("k3", t, t + 1, 160 * l), one("y2t", t, t + 1, 160 * l), F.Relu, scale=-1024.0, bias=1024.0 * (4.0 - 2.0 * t) - 16.0)
+                sc(run("xs", l), run("k3", l), run("y2t", l), 0.0, A.add, A.min)
+            else:
+                for n, (a, b) in lanes(LL[l]):
+                    tr(one("pv", a, b, 160), one("pv", a, b))
+                    for t in range(a, b):
+                        act(two("ab", t, t + 1), one("pv", t, t + 1, 160), F.Abs, scale=-1.0, bias=col("gg", 64 * t + 61))
+                    sc(R("xe", 64 * a, 64 * b), R("a0", 64 * a, 64 * b), R("ab", 64 * a, 64 * b), 0.0, A.add, A.min)
+            for k in range(4):
+                d, b = 2 * (k // 2) + l // 2, 32 * (k % 2) + 16 * (l % 2)
+                o = R("rt", b, 320, 64, p=quad(d))
+                if l < 3:
+                    lin(o, ends("xs", 160 * l, p=quad(k)), -1.0 if l else 1.0, k % 2 - 33.0 / 32)
+                else:
+                    copy(k in M2V, o, last("xe", p=quad(k)), -1.0, 32.0 * (k % 2) * MU)
         sc(R("mm"), R("km", 0, 320), R("sl"), 0.0, A.mult, A.add)
         tr(R("rs"), R("mm"))
         act(R("sg"), R("rs"), F.Sign, bias=C(VB), accum_out=C(ACC))
@@ -499,58 +657,62 @@ def rank_program(g, core, T, topo):
         tr(R("pq", 320, 672), R("pp"))
         sc(R("ps", 0, 320), R("km", 0, 320), R("pq", 0, 320), 0.0, A.mult, A.max)
         sc(R("ps", 320, 672), R("km", 320, 672), R("pq", 320, 672), 0.0, A.mult, A.max)
-        cp(R("kq", 0, 21), R("ps", 31, 672, 32))
-        act(R("kq", 21, 42), R("ps", SLOT[3] - 1, 672, 32), F.Copy)
-        cp(R("kq", 42, 63, p=quad(0)), R("ps", SLOT[2] - 1, 672, 32, p=quad(1)))
-        act(R("kq", 42, 63, p=quad(2)), R("ps", SLOT[2] - 1, 672, 32, p=quad(3)), F.Copy)
+        for n, (a, x, d, k) in enumerate(((0, 32, None, None), (21, SLOT[3], None, None), (42, SLOT[2], 0, 1), (42, SLOT[2], 2, 3))):
+            copy(n in KQV, R("kq", a, a + 21, p=(0, 128) if d is None else quad(d)), R("ps", x - 1, 672, 32, p=(0, 128) if d is None else quad(k)))
         ts(R("offs"), ind(R("kq"), OK1), 0.5, A.mult, C(PH), A.add)
-        RC = R("rc", 16, 336)
-        tr(RC, R("m2"))
+        tr(RC, R("rt", 0, 320))
         cp(ind(R("lw"), R("offs", 0, 20)), RC)
         tr(R("lt", 0, 128), R("lw", 0, 128))
         tr(R("lt", 128, 256), R("lw", 16, 144))
         ts(LO, ind(R("lt"), OL), C(SC), A.mult, 160.0, A.add)
         LO = R("lo%d" % rnd, 0, 8)
         send(mate, LI, LO, "rl%d" % rnd, "ol%d" % rnd, FAR)
-        for b in range(4):
+        for b in range(NB1):
             act(R("he", 128 * b, 128 * b + 128), ind(R("zw", 448 * b + 128, 448 * b + 448), LO), F.Copy, scale=0.5)
-        tr(R("rt", 0, 320), RC)
         tr(R("rt", 320, 672), R("rc"))
-        ts(R("wz", 0, 32), ind(R("rt"), OK2), C(SC), A.mult, 288.0, A.add)
-        ts(R("wz", 32, 64), ind(R("kq"), OK1), 0.5, A.mult, -353.0, A.add)
-        ts(R("wz", 64, 96), R("wz", 32, 64), -127.5, A.add, 1024.0, A.mult)
-        tt(R("wz", 96, 128), R("wz", 32, 64), R("wz", 64, 96), A.max)
-        tt(R("wz", 128, 160), R("wz", 96, 128), R("wz", 0, 32), A.min)
-        cp(R("offz"), R("wz", 128, 160))
-        if rnd == 2:
-            lin(R("rcf"), RC, C(SC), 160.0)
-            for k in range(8):
-                dma("sy", H(T.cl[k:k + 1, :]), R("rcf", p=(16 * k, 16 * k + 1)))
+        ts(R("offc"), ind(R("rt"), OK2), C(SC), A.mult, 288.0, A.add)
+        lin(R("wz", 1, 64, 2), ind(R("rt"), OK2), C(SC), 288.0)
+        lin(R("wz", 0, 64, 2), ind(R("kq"), OK1), 0.5, -353.0)
+        act(R("wz", 65, 128, 2), ind(R("kq"), OK1), F.Relu, scale=512.0, bias=-1024.0 * (353.0 + 127.5))
+        sc(R("wz", 128, 192), R("wz", 64, 128), R("wz", 0, 64), 0.0, A.add, A.min)
+        cp(R("offz"), R("wz", 129, 192, 2))
+        for b in range(NB1, 4):
+            copy(b in FHV, R("fh", 320 * b, 320 * b + 320), ind(R("zw", 448 * b, 448 * b + 448), R("offc", 0, 20)))
+        meets.append(len(nodes))
         for b in range(4):
-            tt(R("zw", 448 * b, 448 * b + 128), ind(R("gw", 320 * b, 320 * b + 320), LI), R("he", 128 * b, 128 * b + 128), A.add)
+            o, i = R("zw", 448 * b, 448 * b + 128), ind(R("gw", 320 * b, 320 * b + 320), LI)
+            if b < NB1:
+                tt(o, i, R("he", 128 * b, 128 * b + 128), A.add)
+            else:
+                act(o, i, F.Copy)
         for k in range(2):
             for b in range(4):
-                o, i = R("zt", 640 * k + b, 640 * k + 640, 4), ind(R("zw", 448 * b, 448 * b + 448), R("offz", 10 * k, 10 * k + 10))
-                if 4 * k + b in ZV:
-                    cp(o, i)
-                else:
+                o, i = R("zt", 4 * CUT[k] + b, 4 * CUT[k + 1], 4), ind(R("zw", 448 * b, 448 * b + 448), R("offz", CUT[k] // 16, CUT[k + 1] // 16))
+                if b < NB1:
                     act(o, i, F.Copy)
-            qz(run("qz", k), run("sz", k), run("zt", k, 4))
-            for b in range(4):
-                mm(bank(k, b), R("qw", 128 * b, 128 * b + 128), R("sw", 128 * b, 128 * b + 128), run("qz", k), run("sz", k), False, True)
-                if 4 * k + b in XV:
-                    ts(R("xt", 640 * k + b, 640 * k + 640, 4), bank(k, b), 2.0 ** -5, A.mult)
                 else:
-                    act(R("xt", 640 * k + b, 640 * k + 640, 4), bank(k, b), F.Copy, scale=2.0 ** -5)
-            qz(run("qx", k), run("sx", k), run("xt", k, 4))
+                    tt(o, i, R("fh", 320 * b + CUT[k], 320 * b + CUT[k + 1]), A.add)
+            qz(cut("qz", k), cut("sz", k), cut("zt", k, 4))
+            for b in range(4):
+                o, i = R("xt", 4 * CUT[k] + b, 4 * CUT[k + 1], 4), bank(k, b, wid(k))
+                mm(i, R("qw", 128 * b, 128 * b + 128), R("sw", 128 * b, 128 * b + 128), cut("qz", k), cut("sz", k), False, True)
+                if 4 * k + b in XV:
+                    ts(o, i, 2.0 ** -5, A.mult)
+                else:
+                    act(o, i, F.Copy, scale=2.0 ** -5)
+            qz(cut("qx", k), cut("sx", k), cut("xt", k, 4))
 
+    rounds.append(len(nodes))
+    lin(R("rcf"), RC, C(SC), 160.0)
+    for k in range(8):
+        dma("sy", H(T.cl[k:k + 1, :]), R("rcf", p=(16 * k, 16 * k + 1)))
     for k in range(2):
-        mm(bank(0, k), R("qv"), R("sv"), run("qx", k), run("sx", k))
-        dma("sy", H(T.oc[:, 640 * k:640 * k + 640]), u8(run("qx", k)), 82)
+        mm(bank(0, k, wid(k)), R("qv"), R("sv"), cut("qx", k), cut("sx", k))
+        dma("sy", H(T.oc[:, 4 * CUT[k]:4 * CUT[k + 1]]), u8(cut("qx", k)), wid(k) // 2)
     for k in range(4):
         dma("sy", H(T.osc[4 * k:4 * k + 4, :]), R("sx", p=(32 * k, 32 * k + 4)))
-    act(run("yo", 0), bank(0, 0), F.Copy)
-    cp(run("yo", 1), bank(0, 1))
-    dma("a", H(T.y[:, 0:160]), run("yo", 0), 82)
-    dma("a", H(T.y[:, 160:320]), run("yo", 1), 82)
+    act(cut("yo", 0), bank(0, 0, wid(0)), F.Copy)
+    cp(cut("yo", 1), bank(0, 1, wid(1)))
+    for k in range(2):
+        dma("a", H(T.y[:, CUT[k]:CUT[k + 1]]), cut("yo", k), wid(k) // 2)
     lay_out()

import math
import numpy
from concourse.mybir import dt, AluOpType, ActivationFunctionType
A = AluOpType
F = ActivationFunctionType
BF, F32, F16, U16, I32, X4, U8 = "bfloat16", "float32", "float16", "uint16", "int32", "float8_e4m3fn_x4", "uint8"
PARTNER = [1, 2, 4]
_S = {
    "xt": (1280, BF), "ut": (512, BF), "vt": (512, BF), "ct": (516, BF), "tt": (1280, BF), "zt": (1280, BF),
    "qx": (320, X4), "sx": (320, U8), "qu": (128, X4), "su": (128, U8),
    "qv": (128, X4), "sv": (128, U8), "qw": (512, X4), "sw": (512, U8), "qc": (512, X4), "sc": (512, U8),
    "qz": (320, X4), "sz": (320, U8),
    "zw": (1792, BF), "gw": (1280, BF), "he": (512, BF), "fh": (1280, BF), "yo": (320, F32), "zz": (336, BF),
    "pt": (40, I32), "ci": (8, I32), "cf": (72, F32), "sm": (48, F32), "tab": (48, F32), "iw": (320, F32),
    "offk": (24, U16), "offp": (32, U16), "offd": (144, U16), "offs": (32, U16), "offz": (32, U16), "offc": (32, U16),
    "ss": (320, F32), "sb": (160, F32), "d0": (320, BF), "d1": (320, BF), "x0": (448, BF), "xj": (6 * 224, BF),
    "tw": (3 * 416, BF), "xc": (320, BF), "nb": (160, BF), "r0": (160, F32), "r1": (160, F32), "n0": (160, F32),
    "ap": (176, BF), "apt": (160, BF), "sgn": (160, BF), "rr": (160, BF), "g1": (320, BF), "vv": (320, BF), "n1": (320, BF),
    "e3": (960, BF), "o3": (960, BF), "xa": (160, BF), "dp1": (160, BF), "va": (160, BF), "arx": (160, BF), "ar": (160, BF), "thr": (160, F16), "pj": (160, BF),
    "dm": (160, BF), "dr": (160, BF), "ao": (160, BF), "r32": (160, BF), "seg": (160, BF), "dn": (160, BF), "dp": (160, BF), "de": (160, BF),
    "cnt": (160, BF), "ly": (320, BF), "ns": (1280, BF), "gg": (320, BF), "dd": (160, BF),
    "dy": (160, BF), "u0": (320, BF), "u1": (3 * 320, BF), "up": (3 * 384, BF),
    "pv": (320, F32), "ab": (320, BF), "a0": (320, BF), "xe": (320, BF),
    "z0": (480, BF), "rho": (480, BF), "y2": (480, BF), "y2t": (480, BF), "k3": (480, BF), "xs": (480, BF),
    "sl": (320, BF), "km": (672, BF), "mm": (320, BF), "rs": (320, BF), "sg": (320, BF),
    "e1": (320, F16), "e2": (336, F16), "pp": (352, F16), "pq": (672, F16), "ps": (672, F16), "kq": (72, F32),
    "rc": (352, BF), "rt": (672, BF), "rcf": (320, F32), "wz": (192, F32),
    "lw": (336, BF), "lt": (256, BF),
}
for _t in range(3):
    _S["qt%d" % _t] = (320, X4)
    _S["st%d" % _t] = (320, U8)
    _S["ql%d" % _t] = (320, X4)
    _S["sl%d" % _t] = (320, U8)
    _S["lo%d" % _t] = (16, U16)
    _S["li%d" % _t] = (8, U16)
SCRATCH = {k: ("sbuf", [128, n], d) for k, (n, d) in _S.items()}
SCRATCH["pa"] = ("psum", [128, 2048], F32)
SCRATCH["pb"] = ("psum", [128, 2048], F32)
SEMAPHORES = ["v", "a", "pe", "gp"] + ["m%d" % i for i in range(32)] + ["%s%d" % (n, t) for n in ("rq", "rs", "rl", "oq", "os", "ol") for t in range(3)]
U = [2.0 ** -6, 2.0 ** -6, 2.0 ** -6, 2.0 ** -12, 2.0 ** -18]
MARK = 32.0
MU = 2.0 ** -28
SLOT = (0, 0, 17, 26)
TINY = 2.0 ** -60
LANES = ((0, 3), (3, 5))
LL = (((0, 2), (2, 5)),) * 3 + (((0, 5),),)
CUT = (0, 192, 320)
STEPS = (1, 3, 3)
NB1 = 2
XV, M2V, KQV, SLV, FHV = (1, 3, 5, 7), (0, 2), (0,), (0, 2), (2,)
CY, FAR, BULK, NEAR, RATE = 0.00083, 0.5, 8.0, 1.5, 250.0
CASES = ((1.2, 0.22, 1.6, 4.0), (1.45, 0.24, 2.0, 5.5))
MOVES, HEAT = (60000, 10000), (0.12, 0.03)
ORDER = []


def arrange(nodes, keep, first, focus, moves, heat):
    n, at = len(keep), {k: i for i, k in enumerate(keep)}
    X = [nodes[k] for k in keep]
    qs, lat = [x["q"] for x in X], [x["lat"] for x in X]
    needs = [set(at[d] for d in x["all"] if d in at) for x in X]
    users = [set() for _ in X]
    for k in range(n):
        for d in needs[k]:
            users[d].add(k)
    cases = [([x["cost"][0] + c[0] * (x["cost"][1] + c[2] * x["cost"][2] + c[3] * x["cost"][3]) for x in X],
              [[(d, lat[d] + c[1] if keep[d] in X[k]["deps"] else 0.001) for d in sorted(needs[k])] for k in range(n)]) for c in CASES]
    tails, many = [k for k in range(n) if not users[k]], len(set(qs))

    def walk(order, cost, ins, old=None, same=0):
        end, why = (old[3][:], old[2][:]) if old else ([0.0] * n, [None] * n)
        last = {}
        for k in order[:same][::-1]:
            if qs[k] not in last:
                last[qs[k]] = k
                if len(last) == many:
                    break
        last["far"] = None
        for k in order[same:]:
            q = qs[k]
            y = last.get(q)
            t = 0.0 if y is None else end[y]
            for d, w in ins[k]:
                e = end[d] + w
                if e > t:
                    t, y = e, -1 - d
            end[k] = t + cost[k]
            why[k] = y
            if q != "far":
                last[q] = k
        k = max(tails, key=lambda i: end[i] + lat[i])
        return end[k] + lat[k], k, why, end

    def place(order, cost, before, back):
        end, used = [0.0] * n, {q: [] for q in qs}
        for k in order:
            t = max([lat[k] if back else 0.0] + [end[d] + w for d, w in before[k]])
            if qs[k] != "far":
                u, i = used[qs[k]], 0
                while i < len(u) and u[i][0] < t + cost[k]:
                    t = max(t, u[i][1])
                    i += 1
                u.insert(i, (t, t + cost[k]))
            end[k] = t + cost[k]
        return end

    def ahead(order, a, b, of):
        pa, pb = order.index(a), order.index(b)
        need, queues, moved, rest = set(of[b]), set(), [b], []
        for x in order[pb - 1:pa:-1]:
            if x in need or qs[x] in queues:
                moved.append(x)
                need |= of[x]
                if qs[x] != "far":
                    queues.add(qs[x])
            else:
                rest.append(x)
        if a in need or qs[a] in queues:
            return None
        return order[:pa] + moved[::-1] + [a] + rest[::-1] + order[pb + 1:]

    cost, ins = cases[0]
    if first is None:
        late = [0.0] * n
        for k in range(n - 1, -1, -1):
            late[k] = cost[k] + max([lat[k]] + [late[i] + w for i in users[k] for d, w in ins[i] if d == k])
        first = sorted(range(n), key=lambda i: (-late[i], i))
    end, rank = place(first, cost, ins, False), {k: i for i, k in enumerate(first)}
    order = sorted(first, key=lambda i: (end[i] - cost[i], rank[i]))
    runs = [walk(order, *c) for c in cases]
    now = sum(r[0] for r in runs)
    best, rng = (now, order), numpy.random.default_rng(1)
    for step in range(moves):
        _, k, why, _ = runs[step % len(cases)]
        pairs = []
        while why[k] is not None:
            if why[k] >= 0 and k in focus:
                pairs.append((why[k], k))
            k = why[k] if why[k] >= 0 else -1 - why[k]
        if not pairs:
            break
        a, b = pairs[int(rng.integers(len(pairs)))]
        mine = [x for x in order if qs[x] == qs[a]]
        i, j = mine.index(a), int(rng.geometric(0.5)) - 1
        if rng.random() < 0.5:
            new = ahead(order, mine[max(i - j, 0)], b, needs)
        else:
            new = ahead(order[::-1], mine[min(i + 1 + j, len(mine) - 1)], a, users)
            new = new and new[::-1]
        if new:
            same = 0
            while new[same] == order[same]:
                same += 1
            trial = [walk(new, c[0], c[1], r, same) for c, r in zip(cases, runs)]
            total = sum(r[0] for r in trial)
            if total <= now or rng.random() < math.exp((now - total) / (heat * len(cases) * (1.0 - step / moves) + 1e-6)):
                order, runs, now = new, trial, total
                if now < best[0]:
                    best = (now, order)
    end = walk(best[1], cost, ins)[3]
    return [keep[k] for k in best[1]], {keep[k]: end[k] - cost[k] for k in range(n)}, best[0] / len(cases)


def order_of(nodes, rounds, meets):
    n, size = len(nodes), rounds[1] - rounds[0]
    order, start, _ = arrange(nodes, list(range(meets[1], meets[2])), None, range(size), MOVES[0], HEAT[0])
    rank, key = {k: i for i, k in enumerate(order)}, {}
    for k in range(rounds[0], rounds[3]):
        s = (k - meets[1]) // size
        key[k] = (100.0 * s + start[k - s * size], rank[k - s * size])
    for k in range(rounds[0] - 1, -1, -1):
        key[k] = (min([key[i][0] for i in range(k + 1, rounds[3]) if k in nodes[i]["all"]] + [200.0]) - 0.3, k)
    for k in range(rounds[3], n):
        key[k] = (max([key[d][0] for d in nodes[k]["all"]]) + 0.3, k)
    ends = set(range(meets[0])) | set(range(meets[2], n))
    return arrange(nodes, list(range(n)), sorted(range(n), key=lambda k: key[k]), ends, MOVES[1], HEAT[1])[0]


def rank_program(g, core, T, topo):
    rank = T.rank_of(core)
    if rank is None:
        return
    Q = {"v": g.vector, "a": g.scalar, "pe": g.tensor, "gp": g, "sy": g.sync}
    nodes, hist, pool, rounds, meets = [], {}, [0], [], []

    def R(name, a=None, b=None, s=1, p=(0, 128)):
        if a is None:
            a, b = 0, T[name].shape[1]
        ap = T[name][p[0]:p[1], a:b:s] if s > 1 else T[name][p[0]:p[1], a:b]
        n = (b - a + s - 1) // s
        if name in ("pa", "pb"):
            return (ap, [(name, 0, 128, a // 512 * 512, a // 512 * 512 + 512, 1)], n, False, False)
        return (ap, [(name, p[0], p[1], a, b, s)], n, _S[name][1] in (BF, F16, U16), False)

    def ind(w, o):
        return (w[0].indirect(o[0]), w[1] + o[1], 16 * o[2], False, True)

    def meet(x, y):
        if x[2] <= y[1] or y[2] <= x[1] or x[4] <= y[3] or y[4] <= x[3]:
            return False
        return (x[3] - y[3]) % math.gcd(x[5], y[5]) == 0

    def node(q, reads, writes, emit, cost, lat=0.0, ev=None, free=False, after=()):
        me, deps, soft = len(nodes), set(), set(after)
        for regs, wr in ((reads, False), (writes, True)):
            for x in regs:
                psum = x[0] in ("pa", "pb")
                for (y, w2, k) in hist.get(x[0], []):
                    if meet(x, y) and (wr or w2 or (psum and nodes[k]["q"] != q)):
                        (soft if free and psum and nodes[k]["q"] == q else deps).add(k)
        for x in writes:
            hist[x[0]] = [z for z in hist.get(x[0], []) if not ((x[5] == 1 or x[3:] == z[0][3:]) and x[1] <= z[0][1] and z[0][2] <= x[2] and x[3] <= z[0][3] and z[0][4] <= x[4])]
            hist[x[0]].append((x, True, me))
        for x in reads:
            hist.setdefault(x[0], []).append((x, False, me))
        nodes.append({"q": q, "deps": deps, "all": deps | soft, "emit": emit, "cost": cost, "lat": lat, "ev": ev})
        return me

    def op(q, fn, outs, cost, *args, free=False, **kw):
        reads, writes = [], []
        for i, x in enumerate(args):
            if isinstance(x, tuple):
                if i < outs:
                    writes.extend(x[1][:1])
                    reads.extend(x[1][1:])
                else:
                    reads.extend(x[1])
        for k in kw:
            if isinstance(kw[k], tuple):
                (writes if k == "accum_out" else reads).extend(kw[k][1])
        a2 = [x[0] if isinstance(x, tuple) else x for x in args]
        k2 = {k: (x[0] if isinstance(x, tuple) else x) for k, x in kw.items()}
        node(q, reads, writes, lambda: fn(*a2, **k2).then_inc(T.sem[q], 1), cost, free=free)

    V, S = g.vector, g.scalar

    def fixed(t): return (t, 0.0, 0.0, 0.0)
    def cyc(n): return (0.0, CY * max(64, n), 0.0, 0.0)

    def cc(o, *ins):
        if ins[0][4]:
            return (0.055, 0.0, CY * ins[0][2], 0.0)
        if o[4]:
            return (0.05, 0.0, 0.0, CY * o[2])
        return cyc(o[2] * (0.5 if o[3] and all(i[3] for i in ins) else 1))

    def cp(o, i): op("v", V.tensor_copy, 1, cc(o, i), o, i)
    def tt(o, a, b, f): op("v", V.tensor_tensor, 1, cc(o, a) if a[4] else cyc(2 * o[2]), o, a, b, f)
    def tr(o, i): op("v", V.transpose, 1, cc(o, i), o, i)
    def ms(o, c): op("v", V.memset, 1, cc(o, o), o, c)
    def sc(o, a, b, i, f0, f1): op("v", V.tensor_tensor_scan, 1, cc(o, a, b), o, a, b, i, f0, f1)
    def qz(c, s, i): op("v", V.quantize_mx, 2, (0.0, 0.012 + 0.00088 * c[2], 0.0, 0.0), c, s, i)
    def act(o, i, f, **kw): op("a", S.activation, 1, cc(o, i) if i[4] else cyc(o[2]), o, i, f, **kw)
    def lin(o, i, m, c): act(o, i, F.Identity, scale=m, bias=c)
    def fill(o, c): lin(o, R("zz", 0, o[2], p=o[1][0][1:3]), 0.0, c)
    def iota(o, pat, base, cm): op("gp", g.iota, 1, (0.0, 0.13 + 2 * CY * o[2], 0.0, 0.0), o, pat, base, cm, allow_small_or_imprecise_dtypes=True)
    def mm(o, w, ws, x, xs, start=True, stop=True): op("pe", g.tensor.matmul_mx, 1, (0.0, 0.0006 * (o[2] + 16), 0.0, 0.0), o, w, ws, x, xs, start, stop, free=not start)

    def ts(o, i, s1, f0, s2=None, f1=None):
        if f1 is None:
            op("v", V.tensor_scalar, 1, cc(o, i), o, i, s1, None, f0)
        else:
            op("v", V.tensor_scalar, 1, cc(o, i), o, i, s1, s2, f0, f1)

    def copy(vector, o, i, m=1.0, c=0.0):
        if vector:
            ts(o, i, m, A.mult, c, A.add)
        else:
            lin(o, i, m, c)

    def dma(q, o, i, kb=4, after=()):
        ev = ("m%d" % pool[0], 16)
        pool[0] += 1
        k = node(q, i[1], [], lambda: Q[q].dma_start(o[0], i[0]).then_inc(T.sem[ev[0]], 16), fixed(0.05), 0.0, ev, after=[j for j in after if nodes[j]["q"] == q])
        node("eng", [], o[1], None, fixed(0.02 + kb / RATE), NEAR, ev, after=[k] + [j for j in after if nodes[j]["q"] == "eng"])

    def send(dst, o, i, rs, ls, lat, codes=False):
        rid, pid, _ = topo.addr(dst)
        a, b = (o[0].bitcast(dt.uint8), i[0].bitcast(dt.uint8)) if codes else (o[0], i[0])
        k = node("gp", i[1], [], lambda: g.remote_dma(a, b, T.sem[rs], T.sem[ls], pid, rid, topo.mask(core, dst)), fixed(0.4), 0.0, (ls, len(topo.engines(core, dst))),
                 after=[j for j, x in enumerate(nodes) if x["q"] == "gp"])
        node("far", [], o[1], None, fixed(0.0), lat, (rs, len(topo.engines(dst, core))), after=(k,))

    def lay_out():
        if not ORDER:
            ORDER.extend(order_of(nodes, rounds, meets))
        count, known, final = {}, {q: {} for q in Q}, {}
        for k in ORDER:
            x = nodes[k]
            q = x["q"]
            if q in Q:
                need = {}
                for d in x["deps"]:
                    e = nodes[d]["ev"]
                    need[e[0]] = max(need.get(e[0], 0), e[1])
                for s in sorted(need):
                    if known[q].get(s, 0) < need[s]:
                        Q[q].wait_ge(T.sem[s], need[s])
                        known[q][s] = need[s]
                if x["ev"] is None:
                    count[q] = count.get(q, 0) + 1
                    x["ev"] = (q, count[q])
                x["emit"]()
            final[x["ev"][0]] = max(final.get(x["ev"][0], 0), x["ev"][1])
        for s in sorted(final):
            g.sync.wait_ge(T.sem[s], final[s])

    def H(t): return (t, [])
    def u8(x): return (x[0].bitcast(dt.uint8),) + x[1:]
    def C(k): return R("cf", k, k + 1)
    def quad(k): return (32 * k, 32 * k + 32)
    def cut(n, k, w=1): return R(n, w * CUT[k], w * CUT[k + 1])
    def wid(k): return CUT[k + 1] - CUT[k]
    (J, SB, EB, P1, P6, P14, E16, ROOT, NR, NRU, RHO, KC, IDX, OD, IB, VV, VB, PH, SC, ACC, HV, NJ,
     T0, T1, T2, T3, T4, T5, T6, T7, T8, T9, TA, TB, TC, TD, FL, NB, LV) = range(39)
    L31, SG, FM, BT, BP, BW, PS, RT, DP = range(60, 69)
    OL, OK1, OK2 = [R("offk", a, b) for a, b in ((8, 9), (12, 14), (14, 16))]

    for k in range(2):
        dma("a", R("pt", 0, 20, p=(16 * k, 16 * k + 16)), H(T.p0[:]), 2, range(len(nodes)))
        dma("sy", R("pt", 20, 40, p=(16 * k, 16 * k + 16)), H(T.p1[:]), 2, range(len(nodes)))
    for k in range(2):
        dma("sy", R("ut", 256 * k, 256 * k + 128), H(T.u[:, 256 * k:256 * k + 128]), 33, range(len(nodes)))
        dma("a", R("ut", 256 * k + 128, 256 * k + 256), H(T.u[:, 256 * k:256 * k + 128]), 33, range(len(nodes)))
    dma("a", cut("xt", 0, 4), H(T.x[:, 0:4 * CUT[1]]), 197, range(len(nodes)))
    dma("sy", cut("xt", 1, 4), H(T.x[:, 4 * CUT[1]:1280]), 131, range(len(nodes)))
    dma("sy", u8(R("qw")), (T.wc[:], R("xt")[1]), 262)
    dma("sy", R("sw"), (T.ws[:], R("xt")[1]), 66)
    dma("sy", R("vt"), (T.v[:], R("xt")[1]), 131)
    ms(R("zz"), 0.0)
    iota(R("ci", 7, 8), [[0, 1]], 0, 1)
    iota(R("ct"), [[1, 516]], -3, -4)
    iota(R("iw"), [[32, 5], [0, 2], [1, 32]], 1, 0)
    iota(R("r32"), [[0, 5], [1, 32]], 0, 0)
    iota(R("tab", 0, 5), [[64, 5]], -128, 0)
    iota(R("tab", 8, 13), [[2, 5]], -4, 0)
    for k, m in enumerate((31, 32, 16, 1, 6, 14)):
        ts(R("ci", k, k + 1), R("ci", 7, 8), m, A.bitwise_and)
    ts(R("ct"), R("ct"), 0.0, A.is_equal, 32.0, A.mult)
    for b in range(4):
        qz(R("qc", 128 * b, 128 * b + 128), R("sc", 128 * b, 128 * b + 128), R("ct", 3 - b, 515 - b))
    cp(R("cf", 0, 6), R("ci", 0, 6))
    ms(R("x0"), 0.0)
    for k in (0, 3):
        ms(R("xj", 224 * k, 224 * k + 224), 0.0)
    fill(R("d0", 0, 320, 2), 0.0)
    act(C(ROOT), C(J), F.Relu, scale=-1.0, bias=1.0)
    lin(C(NR), C(ROOT), -1.0, 1.0)
    lin(C(NRU), C(NR), -U[1], 0.0)
    ts(R("nb"), R("r32"), C(J), A.not_equal, 2.0, A.add)
    lin(R("n0"), R("nb"), C(NRU), 256.0)
    lin(C(NB), C(ROOT), 255.0, 256.0)
    lin(R("nb"), R("n0"), -1.0, C(NB))
    qz(R("qu"), R("su"), R("ut"))
    for k in range(2):
        qz(cut("qx", k), cut("sx", k), cut("xt", k, 4))
    for k in range(4):
        for e in range(2):
            cp(R("offp", e, 20, 2, p=quad(k)), R("pt", 2 * (k % 2) + e, 40, 4, p=quad(0)))
    lin(R("r1"), ind(R("iw"), R("offp", 10, 20)), C(ROOT), 256.0)
    lin(R("r0"), ind(R("iw"), R("offp", 0, 10)), C(ROOT), 256.0)
    sc(R("d1", 1, 320, 2), R("r1"), R("n0"), 0.0, A.max, A.subtract)
    sc(R("d0", 1, 320, 2), R("r0"), R("r1"), 0.0, A.max, A.subtract)
    lin(C(OD), C(EB), 1.0 / 16, 0.0)
    lin(C(IB), C(SB), 1.0 / 32, 0.0)
    lin(C(RHO), C(ROOT), 63.5, 0.5)
    act(C(T0), C(J), F.Sign, bias=-1.5)
    lin(C(KC), C(T0), 0.5, 0.5)
    act(C(FL), C(KC), F.Exp, scale=math.log(TINY))
    lin(C(IDX), C(J), -U[4] / 2, 16.0 * U[4])
    lin(C(T2), C(J), U[4], -30.0 * U[4])
    lin(C(LV + 3), C(ROOT), -63.5 * U[3], C(T2))
    for l in (2, 3):
        lin(C(LV + 5 * l), C(ROOT), 4.0, U[l] + 16.0 * U[4] * (l == 3))
        lin(C(LV + 5 * l + 1), C(RHO), -U[l] / 64, U[l] / 2)
        lin(C(LV + 5 * l + 2), C(RHO), U[l], 0.0)
        lin(C(T3), C(NR), (2.0 - 1.0 / 64) / U[l], 1.0 / 64 / U[l])
        act(C(LV + 5 * l + 3), C(T3), F.Copy, scale=C(FL))
        lin(C(LV + 5 * l + 4), C(ROOT), -63.5 * U[l], C(KC))
    act(C(L31), C(J), F.Relu, bias=-30.0)
    lin(C(SG), C(L31), -U[1], 96.0 * U[1])
    lin(C(FM), C(ROOT), -2.0 * MARK * U[1], (32.0 + MARK) * U[1])
    lin(C(BT), C(L31), 2.0 * U[1], (64.0 + MARK) * U[1])
    lin(C(HV), C(ROOT), 2.0 * MARK * U[1], 0.0)
    lin(C(T1), C(L31), -U[1], 2.0 * U[1])
    lin(C(BP), C(HV), 1.0, C(T1))
    lin(C(LV), C(L31), U[1], 0.0)
    lin(C(BW), C(HV), -1.0, C(LV))
    lin(C(PS), C(RHO), U[1], -1.0)
    lin(C(RT), C(ROOT), -63.5 * U[1], 0.0)
    lin(C(DP), C(J), 1.0 / 32, 1.0 + 2.0 / 32)
    lin(C(LV + 2), C(ROOT), 2.0 * U[1], 0.0)
    act(C(E16), C(OD), F.Abs, scale=-1.0, bias=C(P1))
    lin(C(T4), C(P14), 16.0, 0.0)
    for n, (a, b) in enumerate(LANES):
        lin(C(T5), C(EB), -2.0, 32.0 * (b - a) + 32.0)
        lin(C(T5), C(T5), C(E16), C(T4))
        ts(R("offk", 16 + 2 * n, 17 + 2 * n), C(T5), 64.0 * (b - a) + 31.0, A.min)
    lin(C(TC), C(P1), 128.0, C(EB))
    ts(OL, C(P6), 16.0, A.mult, C(TC), A.add)
    fill(R("seg"), -4.0)
    fill(R("seg", 0, 160, 32), C(SG))
    fill(R("rr", 0, 160, 32), 0.0)
    ms(R("g1"), 0.0)
    ms(R("e3", 0, 320), (64.0 + MARK) * U[1])
    ms(R("e3", 320, 960), 0.0)
    fill(R("e3", 0, 960, 64), -4.0)
    fill(R("dp1"), 1.0 / 32)
    fill(R("dp1", 0, 160, 32), 2.0)
    fill(R("dn"), -1.0 / 32)
    fill(R("dp"), 1.0 / 32)
    fill(R("de"), -1.0 / 64)
    ts(R("va"), R("r32"), C(J), A.is_equal, -1.0, A.mult)
    lin(R("yo", 0, 160), R("r32"), -1.0 / 64, 3.0 + 31.5 / 64)
    tt(R("thr"), R("va"), R("yo", 0, 160), A.add)
    for l in (2, 3):
        for a, b in LL[l]:
            n0, w = 640 * (l // 3) + 128 * a, 64 * (b - a)
            fill(R("ns", n0 + 1, n0 + w, 2), -U[4] * (l // 3))
            fill(R("ns", n0 + w + 1, n0 + 2 * w, 2), 1.0)
            if l == 3:
                fill(R("ns", n0 + w + 63, n0 + 2 * w, 64), C(IDX))
    fill(R("tab", 16, 48), 1.0 / 512)
    fill(R("dr", 0, 160, 32), 0.0)
    fill(R("dm", 0, 160, 32), -4.0)
    fill(R("ab", 1, 320, 2), 1.0)
    iota(R("a0"), [[0, 320]], 0, 0)
    fill(R("a0", 0, 320, 64), 1.0)
    lin(R("a0", 63, 320, 64), R("tab", 0, 5), -MU, 0.0)
    ms(R("u0"), -0.25)
    fill(R("u0", 0, 320, 64), -4.0)
    for l in (1, 2):
        fill(R("u1", 320 * l + 1, 320 * l + 320, 2), -4.0)
        fill(R("up", 384 * l + 320, 384 * l + 384), -1.0)
    fill(R("ap", 0, 16), 2.0 * U[1])
    iota(R("sl"), [[0, 320]], 0, 0)
    iota(R("km"), [[0, 672]], 1, 0)
    fill(R("km", 0, 672, 32), 0.0)
    for k in (1, 3):
        for x in SLOT[2:]:
            fill(R("km", x, 672, 32, p=quad(k)), 0.0)
    act(C(T6), C(J), F.Sign, bias=0.5 - SLOT[2])
    act(C(T7), C(J), F.Sign, bias=0.5 - SLOT[3])
    lin(C(T6), C(T6), SLOT[2] / 2, SLOT[3] / 2 + 1.0)
    lin(C(T6), C(T7), (SLOT[3] - SLOT[2]) / 2, C(T6))
    lin(C(NJ), C(J), -1.0, 0.0)
    lin(C(T7), C(T6), C(IB), C(NJ))
    lin(C(VV), C(T7), -1.0, 1.0)
    lin(C(VB), C(T7), 1.0, -1.5)
    ms(R("e2", 0, 16), 0.0)
    ms(R("pp", 0, 16), 0.0)
    ms(R("pp", 336, 352), 0.0)
    fill(R("rc", 0, 16), 0.0)
    fill(R("rc", 336, 352), 0.0)
    iota(R("rt", 0, 320), [[0, 320]], 0, 0)
    fill(R("wz", 64, 128, 2), 4096.0)
    fill(R("kq"), 0.0)
    fill(R("lw", 0, 144), 0.0)
    for b in range(NB1, 4):
        fill(R("zw", 448 * b, 448 * b + 128), 0.0)
    lin(C(PH), C(EB), 1.0, -353.0)
    act(C(TD), C(OD), F.Copy, scale=C(IB))
    lin(C(SC), C(TD), 1.0 / MU - 32.0, 32.0)
    lin(C(T8), C(OD), -1.0, 11.0)
    lin(C(T9), C(P14), 0.5, 0.0)
    lin(C(TA), C(T8), C(E16), C(T9))
    lin(C(T8), C(OD), 42.0, C(TA))
    lin(C(T9), C(TD), -63.0, C(T8))
    ts(R("offk", 12, 13), C(IB), 21.0, A.mult, C(T9), A.add)
    ts(R("offk", 13, 14), R("offk", 12, 13), 8.0, A.add)
    lin(C(TB), C(TA), 32.0, C(EB))
    cp(R("offk", 14, 15), C(TB))
    ts(R("offk", 15, 16), C(TB), 256.0, A.add, 671.0, A.min)
    qz(R("qv"), R("sv"), R("vt"))

    def E(b): return R("qc", 128 * b, 128 * b + 128), R("sc", 128 * b, 128 * b + 128)
    def ends(n, a=0, p=(0, 128)): return R(n, a + 31, a + 160, 32, p=p)
    def last(n, a=0, p=(0, 128)): return R(n, a + 63, a + 320, 64, p=p)
    def run(n, k, w=1): return R(n, 160 * w * k, 160 * w * (k + 1))
    def bank(k, b, n): return R("pa" if k else "pb", 512 * b, 512 * b + n)
    def col(n, k): return R(n, k, k + 1)
    def lanes(x): return list(enumerate(x))[::-1]
    def one(n, a, b, o=0): return R(n, o + 32 * a, o + 32 * b)
    def two(n, a, b, o=0): return R(n, o + 64 * a, o + 64 * b - o % 2, 2)
    AP, RC = R("ap", 16, 176), R("rc", 16, 336)

    for rnd in range(3):
        rounds.append(len(nodes))
        mate = T.cores[rank ^ PARTNER[rnd]]
        QT, ST, QL, SL, LO, LI = [R("%s%d" % (n, rnd)) for n in ("qt", "st", "ql", "sl", "lo", "li")]
        for k in range(2):
            mm(bank(0, k, wid(k)), R("qu"), R("su"), cut("qx", k), cut("sx", k))
            copy(k == 0, cut("ss", k), bank(0, k, wid(k)))
        for n, (a, b) in lanes(LANES):
            copy(n == 1, one("sb", a, b), ind(R("ss", 0, 64 * b), R("offp", 10 + 2 * a, 10 + 2 * b)))
            tt(two("d1", a, b), ind(R("ss", 0, 64 * b), R("offp", 2 * a, 2 * b)), one("sb", a, b), A.is_ge)
            sc(R("x0", 32 * n + 32 + 64 * a, 32 * n + 32 + 64 * b), R("d0", 64 * a, 64 * b), R("d1", 64 * a, 64 * b), 0.0, A.mult, A.add)
        for b in range(4):
            mm(bank(1, b, 320), *E(b), R("qx"), R("sx"))
            mm(bank(0, b, wid(0)), *E(b), cut("qx", 0), cut("sx", 0), True, False)
        for b in range(4):
            act(R("tt", b, 1280, 4), bank(1, b, 320), F.Copy, scale=2.0 ** -5)
        for k in range(2):
            qz(run("qt%d" % rnd, k), run("st%d" % rnd, k), run("tt", k, 4))
        send(mate, QL, QT, "rq%d" % rnd, "oq%d" % rnd, FAR + BULK, True)
        send(mate, SL, ST, "rs%d" % rnd, "os%d" % rnd, FAR + BULK)
        for b in range(4):
            act(R("zw", 448 * b + 128, 448 * b + 448), bank(1, b, 320), F.Copy, scale=2.0 ** -5 if b < NB1 else 2.0 ** -6)
        for b in range(4):
            mm(bank(1, b, 320), *E(b), QL, SL)
            act(R("gw", 320 * b, 320 * b + 320), bank(1, b, 320), F.Copy, scale=2.0 ** -6)
            mm(bank(1, b, wid(1)), *E(b), cut("qx", 1), cut("sx", 1), True, False)
        for n, (a, b) in lanes(LANES):
            k, w, s = 0, 32 * (b - a), 16 * n + 16 + 32 * a
            for ph, steps in enumerate(STEPS):
                o, f = 416 * ph + 64 * a + 32 * n, 48 * ph + 16 * n
                if ph == 0:
                    tr(R("tw", o + w, o + 2 * w + 32), R("x0", 2 * s - 31, 2 * (s + w) + 32, 2))
                    tr(R("tw", o, o + w), R("x0", 2 * s + 1, 2 * (s + w), 2))
                    base, win, m = one("nb", a, b), R("x0", 2 * s, 2 * (s + w)), 2.0
                else:
                    tr(R("tw", o + w, o + 2 * w + 32), R("xj", 224 * (k - 1) + s - 16, 224 * (k - 1) + s + w + 16))
                    tr(R("tw", o, o + w), win)
                    base, m = one("xc", a, b, 160 * (ph - 1)), 1.0
                    if ph == len(STEPS) - 1:
                        lin(base, win, C(NR), C(LV + 2))
                    else:
                        act(base, win, F.Copy)
                ts(R("offd", f, f + 16), ind(R("tw", o, o + 2 * w + 32), R("offk", 16 + 2 * n, 17 + 2 * n)), m, A.mult, -1.0 - 32.0 * a * m, A.add)
                for _ in range(steps):
                    out = R("xj", 224 * k + s, 224 * k + s + w) if k < sum(STEPS) - 1 else one("ap", a, b, 16)
                    tt(out, ind(win, R("offd", f, f + w // 16)), base, A.min)
                    win = out
                    k += 1
        for n, (a, b) in lanes(LL[0]):
            sc(one("cnt", a, b), one("seg", a, b), one("ap", a, b, 16), -4.0, A.max, A.subtract)
        tr(R("apt"), AP)
        lin(R("arx"), R("apt"), -128.0, 8.0)
        sc(R("ar"), R("arx"), R("thr"), 0.0, A.max, A.subtract)
        sc(R("pj"), AP, R("ap", 15, 175), 0.0, A.max, A.subtract)
        for n, (a, b) in lanes(LANES):
            lin(one("sgn", a, b), one("ap", a, b, 16), -128.0, 5.0)
        lin(R("xa"), R("apt"), 128.0, (63.5 + MARK - 256.0) * U[1])
        for t in range(5):
            tt(R("rr", 32 * t + 1, 32 * t + 32), R("sgn", 32 * t + 1, 32 * t + 32), R("sgn", 32 * t, 32 * t + 31), A.mult)
            act(R("dm", 32 * t + 2, 32 * t + 32), R("pj", 32 * t + 2, 32 * t + 32), F.Copy, scale=64.0)
            act(R("dr", 32 * t + 2, 32 * t + 32), R("pj", 32 * t + 2, 32 * t + 32), F.Exp, scale=64.0 * math.log(TINY))
            lin(one("ao", t, t + 1), one("ap", t, t + 1, 16), 128.0, -2.0 * t)
        for l in range(4):
            U1 = 320 * l
            if l == 0:
                NV = ("cnt", 31, 160, 32)
                H0, H1, G1 = R("sm", 0, 5), R("sm", 8, 13), R("g1", 160, 320, 32)
                ts(H0, R(*NV), 15.5 * U[1], A.is_gt, 32.0 * U[1], A.mult)
                ts(H1, R(*NV), 15.5 * U[1], A.is_gt, C(FM), A.mult)
                tt(R("g1", 0, 160, 32), H0, R(*NV), A.subtract)
                tt(G1, H1, R(*NV), A.subtract)
                lin(R("e3", 1, 320, 64), H0, -(64.0 + MARK) / 32, (64.0 + MARK) * U[1])
                lin(last("e3"), R(*NV), 2.0, C(BT))
                lin(R("e3", 320 + 62, 640, 64), H0, -8.0, 0.0)
                lin(last("e3", 320), G1, 1.0, C(BP))
                lin(R("e3", 640 + 62, 960, 64), H0, 8.0, -4.0)
                lin(last("e3", 640), G1, -1.0, C(BW))
                for n, (a, b) in lanes(LL[0]):
                    for e in range(2):
                        sc(one("vv", a, b, 160 * e), one("rr", a, b), one("g1", a, b, 160 * e), 0.0, A.mult, A.add)
                        tr(two("n1", a, b, e), one("vv", a, b, 160 * e))
                    for e in range(3):
                        sc(R("o3", 320 * e + 64 * a, 320 * e + 64 * b), R("e3", 320 * e + 64 * a, 320 * e + 64 * b), R("n1", 64 * a, 64 * b), 0.0, A.add if e else A.subtract, A.max)
            elif l == 1:
                NV = ("o3", 640 + 63, 960, 64)
                ts(R("sm", 16, 21), last("o3"), (63.5 + MARK) * U[1], A.is_gt, C(PS), A.add)
                tt(last("u0"), last("o3", 320), R("sm", 16, 21), A.add)
                lin(last("u1", U1), R(*NV), -1.0, C(LV + 12))
                lin(R("sm", 24, 29), R("sm", 16, 21), 1.0, C(RT))
                for n, (a, b) in lanes(LL[l]):
                    for t in range(a, b):
                        ts(one("dy", t, t + 1), one("xa", t, t + 1), col("o3", 64 * t + 63), A.is_lt, col("o3", 320 + 64 * t + 63), A.mult)
                    tr(two("u1", a, b, U1), one("dy", a, b))
                    sc(R("up", 384 * l + 64 * a, 384 * l + 64 * b), R("u0", 64 * a, 64 * b), R("u1", U1 + 64 * a, U1 + 64 * b), 0.0, A.subtract, A.max)
            else:
                o = 384 * (l - 1)
                NV = ("up", o + 63, o + 320, 64)
                fill(R("dm", 1, 160, 32), C(LV + 5 * l + 4))
                fill(R("dr", 1, 160, 32), C(LV + 5 * l + 3))
                if l < 3:
                    lin(last("u1", U1), R(*NV), 1.0 / 64, 0.0)
                for n, (a, b) in lanes(LL[l]):
                    w, n0, nv = 32 * (b - a), 640 * (l // 3) + 128 * a, R("up", o + 64 * a + 63, o + 64 * b, 64)
                    n1 = n0 + 2 * w
                    lin(R("ns", n0 + 63, n1, 64), nv, -2.0, C(LV + 5 * l))
                    if l < 3:
                        lin(R("ns", n1 + 63, n1 + 2 * w, 64), nv, 1.0 / 64, C(LV + 5 * l + 1))
                    else:
                        act(R("ns", n0 + 61, n1, 64), nv, F.Relu, scale=4.0 / U[3])
                        lin(R("ns", n1 + 61, n1 + 2 * w, 64), nv, 1.0, C(LV + 3))
                    sc(R("ly", 64 * a, 64 * a + w), one("dr", a, b), two("up", a, b, o + 63), 0.0, A.mult, A.max)
                    sc(R("ly", 64 * a + w, 64 * b), one("dm", a, b), two("up", a, b, o + 63), 0.0, A.add, A.max)
                    tr(R("ns", n0, n0 + 4 * w, 2), R("ly", 64 * a, 64 * b))
                    sc(R("gg", 64 * a, 64 * b), R("ns", n0, n1), R("ns", n1, n1 + 2 * w), 0.0, A.add, A.min)
                    if l < 3:
                        sc(one("dd", a, b), one("de", a, b), R("ns", n0, n1, 2), 0.0, A.add, A.max)
                        lin(R("u0", 64 * a + 63, 64 * b, 64), R("gg", 64 * a + 63, 64 * b, 64), 1.0, C(LV + 5 * l + 7))
                    for t in range(a, b):
                        if l < 3:
                            ts(one("dy", t, t + 1), one("ar", t, t + 1), col("dd", 32 * t + 31), A.is_gt, col("gg", 64 * t + 63), A.mult)
                        else:
                            ts(one("pv", t, t + 1), R("tab", 16, 48), col("gg", 64 * t + 63), A.mult, col("gg", 64 * t + 61), A.add)
                    if l < 3:
                        tr(two("u1", a, b, U1), one("dy", a, b))
                        sc(R("up", 384 * l + 64 * a, 384 * l + 64 * b), R("u0", 64 * a, 64 * b), R("u1", U1 + 64 * a, U1 + 64 * b), 0.0, A.subtract, A.max)
            for k in range(4):
                d, b, c = 2 * (k // 2) + min(l, 1), 32 * (k % 2) + SLOT[l], RHO if l else L31
                copy(l == 3 and k in SLV, R("sl", b, 320, 64, p=quad(d)), R(*NV, p=quad(k)), (-1.0 if l > 1 else 1.0) / U[l], 0.0 if l == 1 else R("cf", c, c + 1, p=quad(k)))
            if l == 0:
                act(R("va"), R("n1", 1, 320, 2), F.Abs)
                act(run("z0", 0), R("va"), F.Sign, bias=-20.0 * U[1])
                sc(run("rho", 0), R("dn"), run("z0", 0), -1.0, A.add, A.max)
                tt(ends("xs"), ends("rho"), R("tab", 8, 13), A.add)
            elif l < 3:
                if l == 1:
                    tt(R("sm", 32, 37), R("up", 384 + 62, 384 + 320, 64), R("sm", 24, 29), A.subtract)
                    for t in range(5):
                        act(one("z0", t, t + 1, 160), two("u1", t, t + 1, U1), F.Sign, scale=-1.0, bias=col("sm", 32 + t))
                    act(R("sm", 40, 45), R(*NV), F.Relu, scale=-4.0 / U[1], bias=C(DP))
                    lin(ends("dp1"), R("sm", 40, 45), -1.0, 1.0 / 32)
                else:
                    act(run("z0", l), R("u1", U1, U1 + 320, 2), F.Sign, scale=-1.0, bias=U[4] / 4)
                sc(run("rho", l), R("dp1" if l == 1 else "dp"), run("z0", l), 1.0, A.add, A.min)
                for t in range(5):
                    act(one("y2", t, t + 1, 160 * l), one("ao", t, t + 1), F.Identity, bias=col("rho", 160 * l + 32 * t + 31))
                tr(run("y2t", l), run("y2", l))
                for t in range(5):
                    act(one("k3", t, t + 1, 160 * l), one("y2t", t, t + 1, 160 * l), F.Relu, scale=-1024.0, bias=1024.0 * (4.0 - 2.0 * t) - 16.0)
                sc(run("xs", l), run("k3", l), run("y2t", l), 0.0, A.add, A.min)
            else:
                for n, (a, b) in lanes(LL[l]):
                    tr(one("pv", a, b, 160), one("pv", a, b))
                    for t in range(a, b):
                        act(two("ab", t, t + 1), one("pv", t, t + 1, 160), F.Abs, scale=-1.0, bias=col("gg", 64 * t + 61))
                    sc(R("xe", 64 * a, 64 * b), R("a0", 64 * a, 64 * b), R("ab", 64 * a, 64 * b), 0.0, A.add, A.min)
            for k in range(4):
                d, b = 2 * (k // 2) + l // 2, 32 * (k % 2) + 16 * (l % 2)
                o = R("rt", b, 320, 64, p=quad(d))
                if l < 3:
                    lin(o, ends("xs", 160 * l, p=quad(k)), -1.0 if l else 1.0, k % 2 - 33.0 / 32)
                else:
                    copy(k in M2V, o, last("xe", p=quad(k)), -1.0, 32.0 * (k % 2) * MU)
        sc(R("mm"), R("km", 0, 320), R("sl"), 0.0, A.mult, A.add)
        tr(R("rs"), R("mm"))
        act(R("sg"), R("rs"), F.Sign, bias=C(VB), accum_out=C(ACC))
        ts(R("e1"), R("rs"), C(VV), A.is_equal, 1026.0, A.mult)
        ts(R("e2", 16, 336), R("rs"), C(VV), A.is_equal, 1024.0, A.mult)
        sc(R("pp", 16, 336), R("e1"), R("e2", 15, 335), C(ACC), A.add, A.subtract)
        tr(R("pq", 0, 320), R("pp", 16, 336))
        tr(R("pq", 320, 672), R("pp"))
        sc(R("ps", 0, 320), R("km", 0, 320), R("pq", 0, 320), 0.0, A.mult, A.max)
        sc(R("ps", 320, 672), R("km", 320, 672), R("pq", 320, 672), 0.0, A.mult, A.max)
        for n, (a, x, d, k) in enumerate(((0, 32, None, None), (21, SLOT[3], None, None), (42, SLOT[2], 0, 1), (42, SLOT[2], 2, 3))):
            copy(n in KQV, R("kq", a, a + 21, p=(0, 128) if d is None else quad(d)), R("ps", x - 1, 672, 32, p=(0, 128) if d is None else quad(k)))
        ts(R("offs"), ind(R("kq"), OK1), 0.5, A.mult, C(PH), A.add)
        tr(RC, R("rt", 0, 320))
        cp(ind(R("lw"), R("offs", 0, 20)), RC)
        tr(R("lt", 0, 128), R("lw", 0, 128))
        tr(R("lt", 128, 256), R("lw", 16, 144))
        ts(LO, ind(R("lt"), OL), C(SC), A.mult, 160.0, A.add)
        LO = R("lo%d" % rnd, 0, 8)
        send(mate, LI, LO, "rl%d" % rnd, "ol%d" % rnd, FAR)
        for b in range(NB1):
            act(R("he", 128 * b, 128 * b + 128), ind(R("zw", 448 * b + 128, 448 * b + 448), LO), F.Copy, scale=0.5)
        tr(R("rt", 320, 672), R("rc"))
        ts(R("offc"), ind(R("rt"), OK2), C(SC), A.mult, 288.0, A.add)
        lin(R("wz", 1, 64, 2), ind(R("rt"), OK2), C(SC), 288.0)
        lin(R("wz", 0, 64, 2), ind(R("kq"), OK1), 0.5, -353.0)
        act(R("wz", 65, 128, 2), ind(R("kq"), OK1), F.Relu, scale=512.0, bias=-1024.0 * (353.0 + 127.5))
        sc(R("wz", 128, 192), R("wz", 64, 128), R("wz", 0, 64), 0.0, A.add, A.min)
        cp(R("offz"), R("wz", 129, 192, 2))
        for b in range(NB1, 4):
            copy(b in FHV, R("fh", 320 * b, 320 * b + 320), ind(R("zw", 448 * b, 448 * b + 448), R("offc", 0, 20)))
        meets.append(len(nodes))
        for b in range(4):
            o, i = R("zw", 448 * b, 448 * b + 128), ind(R("gw", 320 * b, 320 * b + 320), LI)
            if b < NB1:
                tt(o, i, R("he", 128 * b, 128 * b + 128), A.add)
            else:
                act(o, i, F.Copy)
        for k in range(2):
            for b in range(4):
                o, i = R("zt", 4 * CUT[k] + b, 4 * CUT[k + 1], 4), ind(R("zw", 448 * b, 448 * b + 448), R("offz", CUT[k] // 16, CUT[k + 1] // 16))
                if b < NB1:
                    act(o, i, F.Copy)
                else:
                    tt(o, i, R("fh", 320 * b + CUT[k], 320 * b + CUT[k + 1]), A.add)
            qz(cut("qz", k), cut("sz", k), cut("zt", k, 4))
            for b in range(4):
                o, i = R("xt", 4 * CUT[k] + b, 4 * CUT[k + 1], 4), bank(k, b, wid(k))
                mm(i, R("qw", 128 * b, 128 * b + 128), R("sw", 128 * b, 128 * b + 128), cut("qz", k), cut("sz", k), False, True)
                if 4 * k + b in XV:
                    ts(o, i, 2.0 ** -5, A.mult)
                else:
                    act(o, i, F.Copy, scale=2.0 ** -5)
            qz(cut("qx", k), cut("sx", k), cut("xt", k, 4))

    rounds.append(len(nodes))
    lin(R("rcf"), RC, C(SC), 160.0)
    for k in range(8):
        dma("sy", H(T.cl[k:k + 1, :]), R("rcf", p=(16 * k, 16 * k + 1)))
    for k in range(2):
        mm(bank(0, k, wid(k)), R("qv"), R("sv"), cut("qx", k), cut("sx", k))
        dma("sy", H(T.oc[:, 4 * CUT[k]:4 * CUT[k + 1]]), u8(cut("qx", k)), wid(k) // 2)
    for k in range(4):
        dma("sy", H(T.osc[4 * k:4 * k + 4, :]), R("sx", p=(32 * k, 32 * k + 4)))
    act(cut("yo", 0), bank(0, 0, wid(0)), F.Copy)
    cp(cut("yo", 1), bank(0, 1, wid(1)))
    for k in range(2):
        dma("a", H(T.y[:, CUT[k]:CUT[k + 1]]), cut("yo", k), wid(k) // 2)
    lay_out()
